import numpy as np, ml_dtypes
CORES = [78,86,94,102,110,118]
N = 6
BF = ml_dtypes.bfloat16
def gentries(a):
    return np.ascontiguousarray(a.reshape(8, 16, -1).transpose(0, 2, 1)).reshape(8, -1)
def gtable(e):
    e = np.asarray(e); return np.ascontiguousarray(e.reshape(8, -1, 16).transpose(0, 2, 1)).reshape(128, -1).astype(np.int32)
W, H, L, CAP, RO = 2560, 1024, 128, 192, 4
def pick(t, e):
    return np.take_along_axis(t, e[:, None, :], 2)
def at(x, c):
    return pick(x, c.reshape(8, -1)).reshape(8, 16, 16, -1)
def moved(v, dl):
    return np.clip(v + dl[:, :, None, :], 0, 63)
def spot(u):
    return (((u * u) >> 5) + 37 * u) & (H - 1)
def parts(rng):
    x = rng.integers(0, 64, (N, 8, 16, W)); su = rng.integers(0, W, (N, 8, 16, W)); co = np.argsort(rng.random((N, 8, 16, W)), axis=-1)
    dl = rng.integers(-20, 21, (N, 8, 16, L)); la = rng.integers(0, W, (N, 8, L)); lb = rng.integers(0, W, (N, 8, L))
    wt = rng.integers(0, 256, (N, 8, 16)); th = 110 + 20 * np.argsort(rng.random((N, 8)), axis=-1) + rng.integers(0, 20, (N, 8))
    return x, su, co, dl, la, lb, wt, th
def pack(x, su, co, dl, la, lb, wt, th):
    fl = lambda a, n: np.ascontiguousarray(np.asarray(a).reshape(N, 128, n)).astype(np.float32).astype(BF)
    it = lambda a: np.ascontiguousarray(np.asarray(a).reshape(N, 128, W)).astype(np.int32)
    return {"x0": fl(x, W), "su": it(su), "co": it(co), "dl": fl(dl, L), "la": np.stack([gtable(a) for a in la]), "lb": np.stack([gtable(a) for a in lb]),
            "wt": fl(wt, 1), "th": np.asarray(th).reshape(N, 8, 1).astype(np.int32)}
def put(p, c, v):
    w = np.argmax(p == v[..., None], axis=-1); old = p[..., c].copy()
    np.put_along_axis(p, w[..., None], old[..., None], -1); p[..., c] = v
def two(rng, n):
    c = rng.integers(0, 3, (N, 8, 1, n)); return np.where(c < 2, c, rng.integers(0, 2, (N, 8, 16, n)))
def spots(dl, wt):
    return spot(np.sum(63 * wt[:, :, None] * (dl > 0), axis=1) & 4095)
def setup_inputs(rng):
    return pack(*parts(rng))
def setup_inputs_spread(rng):
    x, su, co, dl, la, lb, wt, th = parts(rng)
    p = np.exp2(rng.integers(-2, 3, (N, 8, 1, W))); x = np.minimum((64 * rng.random((N, 8, 16, W)) ** p).astype(np.int64), 63)
    p = np.exp2(rng.integers(-2, 3, (N, 8, 1, W))); su = np.minimum((W * rng.random((N, 8, 16, W)) ** p).astype(np.int64), W - 1)
    dl = np.rint((2 * rng.random((N, 8, 16, L)) - 1) * rng.choice(np.array([0, 1, 3, 9, 27, 63]), (N, 8, 1, L))).astype(np.int64)
    la = np.minimum((W * rng.random((N, 8, L)) ** 2).astype(np.int64), W - 1); lb = W - 1 - np.minimum((W * rng.random((N, 8, L)) ** 2).astype(np.int64), W - 1)
    wt = np.minimum(np.exp2(8 * rng.random((N, 8, 16))).astype(np.int64), 256) - 1
    th = np.where(rng.random((N, 8)) < 0.5, np.minimum(np.exp2(10 * rng.random((N, 8))).astype(np.int64), 1024) - 1, rng.integers(100, 300, (N, 8)))
    return pack(x, su, co, dl, la, lb, wt, th)
def setup_inputs_ends(rng):
    x, su, co, dl, la, lb, wt, th = parts(rng)
    x = 63 * two(rng, W); su = (W - 1) * two(rng, W); dl = 126 * two(rng, L) - 63
    la = (W - 1) * rng.integers(0, 2, (N, 8, L)); lb = (W - 1) * rng.integers(0, 2, (N, 8, L)); la[:, :, L - 1] = W - 1; lb[:, :, 0] = 0
    wt = 255 * rng.integers(0, 2, (N, 8, 16)); wt[:, 0] = 255 * (np.arange(16) & 1); wt[:, 7] = 255
    th = 1023 * rng.integers(0, 2, (N, 8)); th[:, 0] = 1023; th[:, 1] = 0; th[:, 7] = 0; th[0, 6] = 1023
    z = rng.integers(0, 2, (N, 8, 16)); z[:, :, 0] = 1; z[:, :, 15] = 0
    put(co, 0, (W - 1) * z); put(co, W - 1, (W - 1) * (1 - z))
    dl[:, 7] = np.where(rng.random((N, 1, L)) < 0.5, 63, -63); dl[:, 7, :, 0] = 63; dl[:, 7, :, 1] = -63; dl[:, 7, :, L - 1] = 63
    x[:, 7, :, 0] = 0; x[:, 7, :, W - 1] = 0; x[:, 7, :, spot((16 * 63 * 255) & 4095)] = 0
    x[:, 6, :, 0] = 63; x[:, 6, :, W - 1] = 63; dl[:, 6, :, 0] = -63; dl[:, 6, :, L - 1] = -63
    return pack(x, su, co, dl, la, lb, wt, th)
def setup_inputs_corners(rng):
    x, su, co, dl, la, lb, wt, th = parts(rng); th[:] = 0; dl = 126 * rng.integers(0, 2, (N, 8, 16, L)) - 63
    for r in range(N):
        own = spots(dl[r], wt[r]); come = spots(dl[r - 1], wt[r])
        for i in range(8):
            p = np.unique(own[i]); z = p[:0]
            if i % 2: z = p; p = np.setdiff1d(come[i], z)
            n = int(rng.choice(np.array([0, 1, CAP - 1, CAP, CAP + 1, W - H])))
            if r in (0, N - 1): n = (CAP, CAP, CAP + 1, CAP + 1, CAP - 1, CAP - 1, 0, 1)[i]
            if r == 1 and i in (2, 6): n = W - H
            n = min(n, 16 * len(p), W - H)
            a = np.concatenate([z, p]); s = np.stack([rng.permutation(H)[:len(a)] for k in range(16)])
            c = s[:, len(z):].copy().reshape(-1); c[rng.permutation(len(c))[:n]] = H + rng.permutation(W - H)[:n]
            s[:, len(z):] = c.reshape(16, -1)
            rest = np.ones(W, bool); rest[a] = False
            for k in range(16):
                free = np.ones(W, bool); free[s[k]] = False
                co[r, i, k, a] = s[k]; co[r, i, k, rest] = rng.permutation(np.flatnonzero(free))
    return pack(x, su, co, dl, la, lb, wt, th)
def setup_inputs_crowd(rng):
    x, su, co, dl, la, lb, wt, th = parts(rng)
    dl[:, :2] = 126 * rng.integers(0, 2, (N, 2, 16, L)) - 63
    for i in range(8):
        m = (1, 1, 2, 1, 4, 1, 2, 1)[i]; s = rng.integers(0, m, L); z = int(rng.integers(1, L - 1))
        if i % 2: s[z] = m
        la[:, i] = la[:, i][:, s]; lb[:, i] = lb[:, i][:, s]; dl[:, i] = dl[:, i][:, :, s]
    for r in range(N):
        n = spots(dl[r], wt[r])
        put(co[r, 0], int(n[0, 0]), np.full(16, W - 1)); put(co[r, 1], int(n[1, 0]), np.full(16, H))
        if r % 3 < 2: th[r] = 0
        if r % 3 == 0: dl[r, 5, :, L - 1] = 0; lb[r, 5, L - 1] = la[r, 5, L - 1]
        if r % 3 == 1: th[r, 3] = 1; dl[r, 3, :, L - 1] = 0; lb[r, 3, L - 1] = la[r, 3, L - 1]
    return pack(x, su, co, dl, la, lb, wt, th)
def setup_inputs_ties(rng):
    x, su, co, dl, la, lb, wt, th = parts(rng)
    x = 8 * (x >> 4); x[:, 1::2] = 63 - x[:, 1::2]; dl = 8 * rng.integers(-1, 2, (N, 8, 16, L))
    x[:, 3] = 63; x[:, 3, :7] = 62 + np.minimum(rng.integers(0, 4, (N, 7, W)), 1); dl[:, 3] = -63; dl[2, 3, :, 48:] = 0
    put(co[2, 3], 0, H + np.arange(16)); su[2, 3, :, H:H + 16] = H + ((np.arange(16) + 1) & 15)
    su[:, ::2, :, :W // 2] = su[:, ::2, :1, :W // 2].copy()
    la[:, :, 16:32] = la[:, :, :16].copy(); lb[:, :, 16:32] = lb[:, :, :16].copy(); dl[:, :, :, 16:32] = dl[:, :, :, :16].copy()
    lb[:, :, 32:48] = la[:, :, 32:48].copy(); dl[:, :, :, 32:48] = 0
    for r in range(N):
        dd = np.sum(np.abs(at(x[r], pick(co[r], lb[r])) - moved(at(x[r], pick(co[r], la[r])), dl[r])), axis=1)
        th[r] = np.sort(np.min(dd, axis=1), axis=1)[:, L // 2]; th[r, 4:] += rng.integers(0, 2, 4)
        if r == 2: th[r] = 1023; th[r, 3] = np.min(dd[3, :, :32])
    return pack(x, su, co, dl, la, lb, wt, th)
def check_inputs(d):
    bad = []
    for k, lo, hi in (("x0", 0, 63), ("su", 0, W - 1), ("co", 0, W - 1), ("dl", -63, 63), ("la", 0, W - 1), ("lb", 0, W - 1), ("wt", 0, 255), ("th", 0, 1023)):
        a = np.asarray(d[k]).astype(np.float64)
        if not (np.min(a) >= lo and np.max(a) <= hi): bad.append("range of " + k)
        if np.any(a != np.floor(a)): bad.append("whole numbers of " + k)
    if np.any(np.sort(np.asarray(d["co"]), axis=-1) != np.arange(W)): bad.append("a row of co holds every node once")
    return bad
def reference(x0, su, co, dl, la, lb, wt, th):
    x = x0.astype(np.float32).astype(np.int32).reshape(N, 8, 16, W); s = su.astype(np.int64).reshape(N, 8, 16, W); c = co.astype(np.int64).reshape(N, 8, 16, W)
    sh = dl.astype(np.float32).astype(np.int32).reshape(N, 8, 16, L); w = wt.astype(np.float32).astype(np.int32).reshape(N, 8, 16, 1, 1); lim = th.astype(np.int64).reshape(N, 8, 1)
    a = np.stack([gentries(v) for v in la]).astype(np.int64); b = np.stack([gentries(v) for v in lb]).astype(np.int64)
    flag = np.zeros((N, 8, W), bool); last = np.zeros(N, np.int64)
    for t in range(RO):
        for r in range(N):
            q = (r - t) % N
            d = pick(c[r], a[q]); f = pick(c[r], b[q])
            dist = np.sum(np.abs(at(x[r], f) - moved(at(x[r], d), sh[q])), axis=1)
            k = np.argmin(dist, axis=1)[:, None, :]
            dk = np.take_along_axis(d, k, 1)[:, 0]; fk = np.take_along_axis(f, k, 1)[:, 0]
            same = np.take_along_axis(dist, k, 1)[:, 0] < lim[r] + (last[r] & 63)
            e = moved(at(x[r], pick(s[r], dk)), sh[q])
            n = spot(np.sum(w[r] * e, axis=1).astype(np.int64) & 4095)
            j = np.argmax(np.sum(np.abs(at(x[r], n) - e), axis=1), axis=1)[:, None, :]
            nj = np.take_along_axis(n, j, 1)[:, 0]; ej = np.take_along_axis(e, j[:, None], 2)[:, :, 0]
            for i in range(8):
                lane = np.flatnonzero(~same[i]); place, first = np.unique(nj[i, lane], return_index=True)
                x[r, i][:, place] = ej[i][:, lane[first]]
                flag[r, i, c[r, i][:, place].reshape(-1)] = True; flag[r, i, :H] = False
                v = np.flatnonzero(flag[r, i])[:CAP]
                z = x[r, i][:, s[r, i][:, v]]
                x[r, i][:, v] = (np.max(z, axis=1) + np.min(z, axis=1)) >> 1
                flag[r, i, v] = False
            last[r] = np.sum(~same)
            a[q] = np.where(same, dk, a[q]); b[q] = np.where(same, fk, b[q])
    return {"yx": x.reshape(N, 128, W).astype(np.float32).astype(BF), "ya": np.stack([gtable(a[(r - RO + 1) % N]) for r in range(N)]).astype(np.float32),
            "yb": np.stack([gtable(b[(r - RO + 1) % N]) for r in range(N)]).astype(np.float32)}

@@ -1,0 +1,584 @@
+from concourse.mybir import dt, AluOpType as A, AxisListType, ActivationFunctionType as F
+
+XW = 2752
+CW = 2688
+NA = 64
+RO = 4
+ZS1, ZS2 = (1, 3), (1, 3)
+FAR1, FAR2 = (2, 3), (2, 3)
+NS = 12
+NV = 4
+RC = (48, 80, 64)
+
+_B, _F, _I, _U = "bfloat16", "float32", "int32", "uint16"
+_S = {
+    "X": (XW, _B), "cot": (CW, _I), "sut": (CW, _I), "dls": (512, _B), "dx0": (2048, _B), "dx1": (2048, _B),
+    "abt": (64, _U), "abo": (64, _U), "lab": (16, _I), "wtc": (1, _B), "thi": (1, _I),
+    "dfk": (256, _U), "f2": (256, _F), "xf": (2048, _B), "xn": (2048, _B), "z": (2048, _B), "z2": (2048, _B), "e1": (2048, _B), "e": (2048, _B),
+    "da": (2048, _B), "db": (2048, _B),
+    "key": (128, _F), "sc": (128, _F), "oh": (128, _F), "pr": (128, _F), "ds": (128, _F), "prf": (128, _F), "fs": (128, _F),
+    "key2": (128, _F), "sc2": (128, _F), "d16": (16, _U), "sj": (128, _U), "ui": (128, _I), "uv": (128, _I), "w1": (128, _F), "w2": (128, _F), "nn": (128, _I),
+    "ni": (128, _I), "n16": (128, _U), "nf": (128, _F), "pay": (128, _F),
+    "k8": (8, _I), "n8": (8, _I), "j8": (8, _I), "nm": (8, _F), "nl": (8, _U), "jf": (8, _F), "jl": (8, _U),
+    "m128": (8, _F), "q": (8, _F), "nb": (8, _F), "cg": (128, _F), "nlx": (128, _F), "esel": (128, _B),
+    "hi": (128, _B), "hs": (128, _B), "lo": (128, _B), "sh": (2048, _B), "ohl": (4096, _B), "ohh": (6144, _B),
+    "ab1": (1024, _F), "rl": (1024, _F), "los": (8, _F), "lt": (8, _F), "tg": (8, _F), "tg16": (8, _U),
+    "Fq": (256, _B), "Fl": (96, _B), "Sx": (96, _F), "P2": (112, _B), "sg": (1152, _B), "xa": (12, _F), "xb": (12, _B), "xl": (12, _U),
+    "cm": (192, _B), "no16": (12, _U), "s4": (192, _U),
+    "R": (3072, _B), "mx": (3072, _B), "mn": (3072, _B), "sm": (192, _F), "vi": (192, _I),
+    "iv": (12, _F), "vl": (12, _F), "vl16": (12, _U), "g2": (96, _B), "old": (96, _B),
+    "al": (8, _F), "alT": (8, _F), "af": (16, _F), "u8": (16, _F), "abf": (16, _F),
+    "cnt": (1, _F), "ai": (1, _I), "thb": (1, _F), "thv": (1, _F), "th8": (1, _F),
+    "pc": (24, _F), "ci": (160, _I), "cf": (1408, _F), "mf": (1024, _F), "mb": (3024, _B), "rr": (3072, _B), "tmp": (256, _F), "jr": (192, _B),
+    "ks": (128, _F), "k4": (128, _F),
+}
+SCRATCH = {k: ("sbuf", [128, n], d) for k, (n, d) in _S.items()}
+SCRATCH["a3"] = ("sbuf", [128, 8, 256], _B)
+SCRATCH["b3"] = ("sbuf", [128, 8, 256], _B)
+SCRATCH["t3"] = ("sbuf", [128, 8, 32], _F)
+PSUM = ("pX0", "pX1", "pX2", "pD0", "pD1", "pF", "pM", "pQ")
+for _k in PSUM[:7]:
+    SCRATCH[_k] = ("psum", [128, 512], _F)
+SCRATCH["pQ"] = ("psum", [128, 16, 32], _F)
+BANK = ("pX2", "pM", "pX0", "pX1")
+LOADS = ["ldla", "ldlb", "ldco", "ldsu", "lddl", "ldx", "ldwt", "ldth"]
+STORES = ["stx0", "stx1", "sta", "stb"]
+SEMAPHORES = ["sV", "sS", "sP", "sG", "loc", "ab1a", "ab2a", "ab3a", "dl1a", "dl2a", "dl3a"] + LOADS + STORES
+CY, PCY, GAT, SCT, WAKE = 0.00104, 0.0005, 1.5, 3.5, 0.12
+
+
+def rank_program(g, core, T, topo):
+    rank = T.rank_of(core)
+    if rank is None:
+        return
+    N = len(T.cores)
+    que = {"V": g.vector, "S": g.scalar, "P": g.tensor, "G": g, "Y": g.sync}
+    cnt = {"V": 0, "S": 0, "P": 0, "G": 0}
+    known = {k: {} for k in que}
+    snap, hist, ops = {}, {}, []
+
+    def v(name, lo=0, hi=None, step=1, p=None):
+        hi = (_S[name][0] if name in _S else 512) if hi is None else hi
+        ps = slice(0, 128) if p is None else slice(p[0], p[1])
+        ap = T[name][ps, lo:hi] if step == 1 else T[name][ps, lo:hi:step]
+        return (ap, [(name, lo, hi, step == 1 and p is None)], -(-(hi - lo) // step))
+
+    def v3(name, w, c0, c1, k0=0, k1=None):
+        k1 = w if k1 is None else k1
+        return (T[name][:, c0:c1, k0:k1], [(name, w * c0, w * c1, k0 == 0 and k1 == w)], (c1 - c0) * (k1 - k0))
+
+    def ind(win, off):
+        return (win[0].indirect(off[0]), win[1] + off[1], 16 * off[2])
+
+    def clash(eng, b, lo, hi, isw, e2, w2, l2, h2):
+        if b in PSUM and e2 != eng:
+            return 2
+        if b in PSUM and e2 == "P":
+            return 1
+        return 2 if (isw or w2) and lo < h2 and l2 < hi else 0
+
+    def need_of(eng, acc):
+        need = {}
+        for (b, lo, hi, _c, isw) in acc:
+            for (e2, c2, w2, l2, h2) in hist.get(b, ()):
+                if need.get(e2, 0) < c2 and clash(eng, b, lo, hi, isw, e2, w2, l2, h2) == 2:
+                    need[e2] = c2
+        return need
+
+    def sem_of(e):
+        return T.sem["s" + e] if e in ("V", "S", "P", "G") else T.sem[e]
+
+    def wait(eng, need):
+        for e2 in sorted(need, key=lambda e: (e != eng, e)):
+            c2 = need[e2]
+            if known[eng].get(e2, 0) < c2:
+                que[eng].wait_ge(sem_of(e2), c2)
+                for k, n in snap.get((e2, c2), {}).items():
+                    if known[eng].get(k, 0) < n:
+                        known[eng][k] = n
+                known[eng][e2] = c2
+
+    def note(e, c, acc):
+        for (b, lo, hi, full, isw) in acc:
+            h = hist.setdefault(b, [])
+            h[:] = [x for x in h if not (((isw and full) or (x[0] == e and x[2] == isw)) and lo <= x[3] and x[4] <= hi)]
+            h.append((e, c, isw, lo, hi))
+
+    def accs(rd, wr):
+        return [a + (False,) for x in rd for a in x[1]] + [a + (True,) for x in wr for a in x[1]]
+
+    def rec(eng, fns, rd, wr, cost, sem=None):
+        ops.append((eng, fns, accs(rd, wr), cost, sem))
+
+    def issue(op):
+        eng, fns, acc, cost, sem = op
+        wait(eng, need_of(eng, acc))
+        if sem is None:
+            for fn in fns:
+                cnt[eng] += 1
+                fn().then_inc(sem_of(eng), 1)
+            s = dict(known[eng])
+            s[eng] = cnt[eng] - 1
+            snap[(eng, cnt[eng])] = s
+            note(eng, cnt[eng], acc)
+        elif sem == "remote":
+            fns[0]()
+        else:
+            fns[0]().then_inc(T.sem[sem], 16)
+            snap[(sem, 16)] = dict(known[eng])
+            note(sem, 16, acc)
+
+    def flush():
+        n = len(ops)
+        succ, npred, h2 = [[] for _ in range(n)], [0] * n, {}
+        for i, (eng, _f, acc, cost, _s) in enumerate(ops):
+            pred = {}
+            for (b, lo, hi, _c, isw) in acc:
+                for (j, e2, w2, l2, hh) in h2.get(b, ()):
+                    c = clash(eng, b, lo, hi, isw, e2, w2, l2, hh)
+                    if c and pred.get(j, 0) < c:
+                        pred[j] = c
+            for (b, lo, hi, full, isw) in acc:
+                h = h2.setdefault(b, [])
+                if isw and full and b not in PSUM:
+                    h[:] = [x for x in h if not (lo <= x[3] and x[4] <= hi)]
+                elif b in PSUM and len(h) > 60:
+                    del h[:-60]
+                h.append((i, eng, isw, lo, hi))
+            for j, c in pred.items():
+                if j != i:
+                    succ[j].append((i, WAKE if c == 2 else 0.0))
+                    npred[i] += 1
+        prio = [0.0] * n
+        for i in range(n - 1, -1, -1):
+            prio[i] = ops[i][3] + max([prio[j] + w for j, w in succ[i]] + [0.0])
+        ready, free = [0.0] * n, {k: 0.0 for k in que}
+        avail = {k: [] for k in que}
+        for i in range(n):
+            if not npred[i]:
+                avail[ops[i][0]].append(i)
+        done = 0
+        while done < n:
+            best = None
+            for e in que:
+                if avail[e]:
+                    t0 = max(free[e], min(ready[i] for i in avail[e]))
+                    i = max((i for i in avail[e] if ready[i] <= t0), key=lambda i: (prio[i], -i))
+                    if best is None or t0 < best[0]:
+                        best = (t0, e, i)
+            t0, e, i = best
+            avail[e].remove(i)
+            free[e] = t0 + (ops[i][3] if ops[i][4] is None else 0.1)
+            for j, w in succ[i]:
+                ready[j] = max(ready[j], t0 + ops[i][3] + w)
+                npred[j] -= 1
+                if not npred[j]:
+                    avail[ops[j][0]].append(j)
+            issue(ops[i])
+            done += 1
+        del ops[:]
+
+    isv = lambda x: isinstance(x, tuple)
+    raw = lambda x: x[0] if isv(x) else x
+    vec, sca, ten = g.vector, g.scalar, g.tensor
+    small = lambda *xs: all(SCRATCH[x[1][0][0]][2] in (_B, _U) for x in xs)
+    isind = lambda x: len(x[1]) > 1
+    inps = lambda x: x[1][0][0] in PSUM
+
+    def vcost(o, a, k=1.0):
+        if isind(a):
+            return 0.05 + GAT * CY * o[2]
+        return max(64, k * o[2]) * CY
+
+    def tt(o, a, b, op):
+        k = 1 if inps(a) or inps(b) else 2
+        rec("V", [lambda: vec.tensor_tensor(o[0], a[0], b[0], op)], [a, b], [o], vcost(o, a, k))
+
+    def ts(o, a, s1, op0, s2=None, op1=None):
+        rd = [a] + [x for x in (s1, s2) if isv(x)]
+        c = vcost(o, a, 0.5 if small(o, a) else 1)
+        if op1 is None:
+            rec("V", [lambda: vec.tensor_scalar(o[0], a[0], raw(s1), None, op0)], rd, [o], c)
+        else:
+            rec("V", [lambda: vec.tensor_scalar(o[0], a[0], raw(s1), raw(s2), op0, op1)], rd, [o], c)
+
+    def cp(o, a, after=()):
+        rec("V", [lambda: vec.tensor_copy(o[0], a[0])], [a] + list(after), [o], vcost(o, a, 0.5 if small(o, a) else 1))
+
+    def scatter(win, off, a):
+        rec("V", [lambda: vec.tensor_copy(win[0].indirect(off[0]), a[0])], [a, off], [win], 0.05 + SCT * CY * a[2])
+
+    def ms(o, c):
+        rec("V", [lambda: vec.memset(o[0], c)], [], [o], max(64, o[2]) * CY)
+
+    def total(o, a):
+        rec("V", [lambda: vec.tensor_reduce(o[0], a[0], AxisListType.X, A.add)], [a], [o], max(64, a[2]) * CY)
+
+    def scan(o, a, b, op0, op1):
+        rec("V", [lambda: vec.tensor_tensor_scan(o[0], a[0], b[0], 0.0, op0, op1)], [a, b], [o], vcost(o, b, 0.5 if small(o, a, b) else 1))
+
+    def act(o, a, f=F.Copy, bias=None, scale=None, acc=None):
+        rd = [a] + [x for x in (bias, scale) if isv(x)]
+        kw = {}
+        if bias is not None:
+            kw["bias"] = raw(bias)
+        if scale is not None:
+            kw["scale"] = raw(scale)
+        if acc is not None:
+            kw["accum_out"] = acc[0]
+        rec("S", [lambda: sca.activation(o[0], a[0], f, **kw)], rd, [o] + ([acc] if acc is not None else []), vcost(o, a))
+
+    def mms(o, pairs, start=True, stop=True, f32=False):
+        n = len(pairs)
+        fns = [(lambda l=l, r=r, i=i: ten.matmul(o[0], l[0], r[0], start and i == 0, stop and i == n - 1)) for i, (l, r) in enumerate(pairs)]
+        rd = {}
+        for l, r in pairs:
+            for x in (l, r):
+                for (b, lo, hi, c) in x[1]:
+                    q = rd.get(b, (lo, hi))
+                    rd[b] = (min(lo, q[0]), max(hi, q[1]))
+        cost = sum(max(min(64, l[2]), r[2]) for l, r in pairs) * PCY * (4 if f32 else 1)
+        rec("P", fns, [(None, [(b, lo, hi, False)], 0) for b, (lo, hi) in rd.items()], [o], cost)
+
+    def iota(o, pat, base, cm, **kw):
+        rec("G", [lambda: g.iota(o[0], pat, base, cm, **kw)], [], [o], 0.13 + 2 * CY * o[2])
+
+    def load(eng, name, o, src, after=()):
+        rec(eng, [lambda: que[eng].dma_start(o[0], src[:])], list(after), [o], 3.0 + o[2] * 0.0015, name)
+
+    def store(name, dst, a):
+        rec("Y", [lambda: g.sync.dma_start(dst, a[0])], [a], [], 3.0, name)
+
+    locs = [0]
+    trip = lambda s: (None, [("~" + s, 0, 1, True)], 0)
+
+    def remote(dst, name, lo, hi, a, rsem):
+        rid, pid = topo.addr(dst)[:2]
+        en = topo.engines(core, dst)[:4]
+        locs[0] += len(en)
+        rec("G", [lambda: g.remote_dma(T[name][:, lo:hi], a[0], T.sem[rsem], T.sem.loc, pid, rid, sum(1 << x for x in en))], [a], [trip(rsem)], 14.0, "remote")
+        return len(en)
+
+    lab = v("lab")
+    load("Y", "ldla", v("lab", 0, 8), T.la)
+    load("Y", "ldlb", v("lab", 8, 16), T.lb)
+    load("Y", "ldco", v("cot", 0, 2560), T.co)
+    load("S", "lddl", v("dls", 0, 128), T.dl)
+    load("S", "ldx", v("X", 0, 2560), T.x0)
+    load("Y", "ldth", (T.thi[0:8, 0:1], [("thi", 0, 1, True)], 1), T.th)
+    load("Y", "ldwt", v("wtc"), T.wt)
+    load("Y", "ldsu", v("sut", 0, 2560), T.su, [v("cot", 0, 2560)])
+    landed = {}
+    for s in range(1, RO):
+        dst = T.cores[(rank + s) % N]
+        k = remote(dst, "dls", 128 * s, 128 * s + 128, v("dls", 0, 128), "dl%da" % s)
+        landed["dl%da" % s], landed["ab%da" % s] = k, k
+        note("dl%da" % s, k, [("dls", 128 * s, 128 * s + 128, True, True)])
+        note("ab%da" % s, k, [("abt", 16 * s, 16 * s + 16, True, True)])
+
+    def spread(t):
+        for k in range(16):
+            act(v("dx%d" % (t % 2), k, 2048, 16), v("dls", 128 * t, 128 * t + 128))
+
+    spread(0)
+
+    CF, at = {}, [0]
+
+    def cf(k, n):
+        CF[k] = (at[0], n)
+        at[0] += n
+        return v("cf", CF[k][0], CF[k][0] + n)
+
+    C = lambda k, lo=0, hi=None: v("cf", CF[k][0] + lo, CF[k][0] + (CF[k][1] if hi is None else hi))
+    SM = {"allow_small_or_imprecise_dtypes": True}
+    iota(v("tmp"), [[1, 256]], 0, 0, **SM)
+    iota(v("ci", 128, 129), [[0, 1]], 0, 1)
+    iota(cf("kc", 128), [[0, 8], [1, 16]], 0, 0, **SM)
+    iota(cf("c4", 128), [[1, 8], [0, 16]], 0, 0, **SM)
+    iota(v("jr"), [[1, 192]], 0, 0, **SM)
+    col = lambda n: v("tmp", 0, n)
+    cp(v("abt", 0, 16), lab)
+    ms(v("cot", 2560, CW), 0)
+    ms(v("sut", 2560, CW), 0)
+    P = lambda i: v("pc", i, i + 1)
+    cp(P(0), v("ci", 128, 129))
+    for d, s1, op in ((129, 4, A.arith_shift_right), (130, 15, A.bitwise_and), (131, 5, A.arith_shift_right), (132, 16, A.bitwise_and)):
+        ts(v("ci", d, d + 1), v("ci", 128, 129), s1, op)
+    for d, s in ((1, 129), (2, 130), (3, 131)):
+        cp(P(d), v("ci", s, s + 1))
+    ts(P(5), v("ci", 132, 133), 1.0 / 16, A.mult)
+    ts(P(4), P(5), -1.0, A.mult, 1.0, A.add)
+    ts(P(6), P(3), 4.0, A.add)
+    tt(P(9), P(0), P(2), A.subtract)
+    ts(P(10), P(9), 15.0, A.add)
+    MB = {"B1": 0, "B16k": 144, "W": 288, "I16": 432, "E": 560, "I": 720, "nI": 848, "U": 976}
+    for i, k in enumerate(("T", "O", "C")):
+        for b in range(4):
+            MB[k + str(b)] = 1488 + 128 * (4 * i + b)
+    mb = lambda k, n=128: v("mb", MB[k], MB[k] + n)
+    slide = lambda k, m: v("mb", MB[k] + 15 - m, MB[k] + 143 - m)
+    MF = {"I": 0, "BO": 128, "ON": 256, "E8": 384, "SW00": 512, "SW01": 640, "SW10": 768, "SW11": 896}
+    mf = lambda k: v("mf", MF[k], MF[k] + 128)
+    ts(mb("B1", 144), col(144), P(10), A.is_equal)
+    act(cf("k16", 128), C("kc"), scale=1.0 / 16)
+    ts(cf("R1", 128), C("kc"), 0.0, A.is_equal, 32768.0, A.mult)
+    ts(cf("R3", 128), C("kc"), 0.0, A.is_gt)
+    ts(mf("I"), col(128), P(0), A.is_equal)
+    for cpx in range(2):
+        for gp in range(2):
+            ts(P(11 + 2 * cpx + gp), P(0), 16.0 * (gp - cpx), A.add)
+            ts(mf("SW%d%d" % (cpx, gp)), col(128), P(11 + 2 * cpx + gp), A.is_equal, P(4 + cpx), A.mult)
+    act(mb("I"), mf("I"))
+    act(mb("nI"), mf("I"), scale=-1.0)
+    ts(mb("W", 144), mb("B1", 144), v("wtc"), A.mult)
+    ts(mf("E8"), C("c4"), P(0), A.is_equal)
+    th8 = v("th8", 0, 1, 1, (0, 8))
+    cp(th8, v("thi", 0, 1, 1, (0, 8)))
+    mms(v("pM", 0, 1), [(v("mf", MF["E8"], MF["E8"] + 128, 1, (0, 8)), th8)], f32=True)
+    cp(v("thb"), v("pM", 0, 1))
+    cp(v("thv"), v("thb"))
+    ts(cf("R2", 128), C("kc"), 0.0, A.is_gt, 16777216.0, A.mult)
+    act(cf("pc2", 128), C("kc"), F.Identity, bias=15360.0, scale=-1024.0)
+    act(mb("B16k", 144), mb("B1", 144), scale=16384.0)
+    ts(mf("BO"), C("c4"), P(1), A.is_equal)
+    ms(mf("ON"), 1.0)
+    ts(cf("M16", 16), C("kc", 0, 16), P(2), A.is_equal)
+    ts(cf("lf", 8), col(8), 16.0, A.mult, P(2), A.add)
+    ts(cf("cT", 8), C("lf"), 2560.0, A.add)
+    ts(cf("c15", 8), C("lf"), 16.0, A.mult, 15.0, A.add)
+    ts(cf("hl", 8), C("lf"), 0.5, A.mult)
+    ts(cf("c2", 8), C("lf"), -0.5, A.mult, 0.5, A.add)
+    act(mb("I16"), mf("I"), scale=16.0)
+    ts(v("ks"), C("kc"), P(2), A.is_lt, -1.0, A.mult)
+    ts(P(18), P(3), 16.0, A.mult, P(2), A.add)
+    ts(P(19), P(18), 64.0, A.add)
+    for Q in range(2):
+        for b in range(2):
+            i = str(2 * Q + b)
+            ts(mb("O" + i), C("c4"), P(6 if Q else 3), A.is_equal, P(4 + b), A.mult)
+            ts(mb("C" + i), col(128), P(18 + Q), A.is_equal, P(4 + b), A.mult)
+            tt(mb("T" + i), mb("O" + i), v("ks"), A.mult)
+    ts(P(16), P(1), 32.0, A.mult, P(2), A.add)
+    ts(P(17), P(16), 16.0, A.add)
+    for b in range(2):
+        ts(v("mb", MB["U"] + 256 * b, MB["U"] + 256 * b + 256), col(256), P(16 + b), A.is_equal)
+    for Q in range(2):
+        ts(v("k4", 48 * Q, 48 * Q + 48), col(48), 2.0, A.mult, float(Q), A.add)
+        ts(v("mb", MB["E"] + 48 * Q, MB["E"] + 48 * Q + 48), v("k4", 48 * Q, 48 * Q + 48), P(0), A.is_equal)
+    ms(v("P2", 96, 112), 4096.0)
+    ms(cf("one", 96), 1.0)
+    ts(cf("jl", 12), col(12), 16.0, A.mult, P(2), A.add)
+    ts(cf("bj", 12), C("jl"), 0.5, A.add)
+    ts(cf("jT", 12), C("jl"), 1536.0, A.add)
+    for x, op in ((0, A.is_gt), (1536, A.is_equal)):
+        ts(v("rr", x, x + 128), C("kc"), 0.0, op, 64.0, A.mult)
+        for n, m in ((128, 128), (256, 256), (512, 512), (1024, 512)):
+            act(v("rr", x + n, x + n + m), v("rr", x, x + m))
+
+    ADD, SUB, MUL, MAX, MIN = A.add, A.subtract, A.mult, A.max, A.min
+    X, cot, sut = v("X", 0, 2560), v("cot"), v("sut")
+    PART = {0: (0, NA), 1: (NA, 128)}
+    PU = {1: "pF", 0: "pM"}
+    qv = lambda name, i, j=None: v(name, 512 * i, 512 * (i if j is None else j) + 512)
+
+    def turn(src, nblk):
+        o, i = v3("t3", 32, 0, nblk), v(src, 0, 32 * nblk)
+        rec("V", [lambda: vec.transpose(o[0], i[0])], [i], [o], 32 * nblk * CY)
+
+    def swap(nblk):
+        for cpx in range(2):
+            mms(v3("pQ", 32, 0, nblk, 16 * cpx, 16 * cpx + 16),
+                [(mf("SW%d%d" % (cpx, gp)), v3("t3", 32, 0, nblk, 16 * gp, 16 * gp + 16)) for gp in range(2)], f32=True)
+
+    def with_q(o, lo, hi, q0, b, op):
+        tt(v(o, lo, hi), v3("pQ", 32, (q0 + lo) // 32, (q0 + hi) // 32), b, op)
+
+    def distance(pd, w, buf, part):
+        c0 = 4 * part
+        mms(v(pd, 0, NA), [(slide(w, m), v3(buf, 256, c0, c0 + 4, 16 * m, 16 * m + 16)) for m in range(16)])
+
+    def shifted(o, z, lists, dx, part, zs):
+        qs = [i for i in (2 * part, 2 * part + 1) if i not in zs]
+        for i in (2 * part, 2 * part + 1):
+            if i in zs:
+                act(qv(z, i), ind(X, v(lists, 32 * i, 32 * i + 32)))
+                mms(v(BANK[i]), [(mb("I"), qv(z, i)), (mb("I"), qv(dx, i))])
+                ts(qv(o, i), v(BANK[i]), 0.0, MAX, 63.0, MIN)
+        if qs:
+            i, j = qs[0], qs[-1]
+            tt(qv(z, i, j), ind(X, v(lists, 32 * i, 32 * j + 32)), qv(dx, i, j), ADD)
+            ts(qv(o, i, j), qv(z, i, j), 0.0, MAX, 63.0, MIN)
+
+    def apart(xb, db, eb, ab, lists, l0, quarters):
+        for i in quarters:
+            act(qv(xb, i), ind(X, v(lists, l0 + 32 * i, l0 + 32 * i + 32)))
+        for i in quarters:
+            mms(v(BANK[i]), [(mb("I"), qv(xb, i)), (mb("nI"), qv(eb, i))])
+            act(v3(ab, 256, 2 * i, 2 * i + 2), v(BANK[i]), F.Abs)
+        for i in (3, 2, 0, 1):
+            if i not in quarters:
+                tt(qv(db, i), ind(X, v(lists, l0 + 32 * i, l0 + 32 * i + 32)), qv(eb, i), SUB)
+                act(v3(ab, 256, 2 * i, 2 * i + 2), qv(db, i), F.Abs)
+
+    for t in range(RO):
+        dx = "dx%d" % (t % 2)
+        last = t == RO - 1
+        ab, here = v("abt", 16 * t, 16 * t + 16), [trip("ab%da" % t)]
+        cp(v("dfk"), ind(cot, ab), here)
+        for part in (1, 0):
+            shifted("e1", "z", "dfk", dx, part, ZS1)
+        cp(v("f2"), v("dfk"))
+        turn("f2", 8)
+        apart("xf", "da", "e1", "a3", "dfk", 128, FAR1)
+        swap(8)
+        distance("pD1", "B1", "a3", 1)
+        distance("pD0", "B1", "a3", 0)
+        for part in (1, 0):
+            lo, hi = PART[part]
+            tt(v("key", lo, hi), v("pD%d" % part, 0, NA), C("k16", lo, hi), ADD)
+            scan(v("sc", lo, hi), C("R1", lo, hi), v("key", lo, hi), MAX, MIN)
+            for c in range(lo // 16, hi // 16):
+                ts(v("oh", 16 * c, 16 * c + 16), v("key", 16 * c, 16 * c + 16), v("sc", 16 * c + 15, 16 * c + 16), A.is_equal)
+            with_q("pr", lo, hi, 0, v("oh", lo, hi), MUL)
+            scan(v("ds", lo, hi), C("R3", lo, hi), v("pr", lo, hi), MUL, ADD)
+            cp(v("d16", 4 * part, 4 * part + 4), v("ds", lo + 15, hi, 16))
+            cp(v("sj", lo, hi), ind(sut, v("d16", 4 * part, 4 * part + 4)))
+            shifted("e", "z2", "sj", dx, part, ZS2)
+            mms(v(PU[part], 0, NA), [(slide("W", j), v("e", 16 * lo + j, 16 * hi, 16)) for j in range(16)])
+            r = lambda k: v(k, lo, hi)
+            cp(r("ui"), v(PU[part], 0, NA))
+            ts(r("uv"), r("ui"), 4095, A.bitwise_and)
+            ts(r("w1"), r("uv"), -2048.0, ADD)
+            ts(r("w2"), r("uv"), 3232.0, ADD)
+            tt(r("nn"), r("w1"), r("w2"), MUL)
+            ts(r("ni"), r("nn"), 5, A.arith_shift_right, 1023, A.bitwise_and)
+            cp(r("n16"), r("ni"))
+            cp(r("nf"), r("ni"))
+        with_q("prf", 0, 128, 128, v("oh"), MUL)
+        scan(v("fs"), C("R3"), v("prf"), MUL, ADD)
+        ts(v("al"), v("sc", 15, 128, 16), v("thv"), A.is_lt)
+        tt(v("alT"), v("al"), C("cT"), MUL)
+        apart("xn", "db", "e", "b3", "n16", 0, FAR2)
+        turn("nf", 4)
+        swap(4)
+        distance("pD1", "B16k", "b3", 1)
+        distance("pD0", "B16k", "b3", 0)
+        with_q("pay", 0, 128, 0, C("pc2"), ADD)
+        for part in (1, 0):
+            lo, hi = PART[part]
+            tt(v("key2", lo, hi), v("pD%d" % part, 0, NA), v("pay", lo, hi), ADD)
+            scan(v("sc2", lo, hi), C("R2", lo, hi), v("key2", lo, hi), MIN, MAX)
+        cp(v("af"), ab, here)
+        tt(v("u8", 0, 8), v("ds", 15, 128, 16), v("af", 0, 8), SUB)
+        tt(v("u8", 8, 16), v("fs", 15, 128, 16), v("af", 8, 16), SUB)
+        for h in (0, 8):
+            tt(v("u8", h, h + 8), v("u8", h, h + 8), v("al"), MUL)
+        tt(v("abf"), v("u8"), v("af"), ADD)
+        if not last:
+            cp(v("abo", 16 * t, 16 * t + 16), v("abf"))
+            remote(T.cores[(rank + 1) % N], "abt", 16 * t + 16, 16 * t + 32, v("abo", 16 * t, 16 * t + 16), "ab%da" % (t + 1))
+            total(v("cnt"), v("al"))
+        else:
+            store("sta", T.ya[:], v("abf", 0, 8))
+            store("stb", T.yb[:], v("abf", 8, 16))
+        cp(v("k8"), v("sc2", 15, 128, 16))
+        ts(v("n8"), v("k8"), 1023, A.bitwise_and)
+        ts(v("j8"), v("k8"), 10, A.arith_shift_right, 15, A.bitwise_and)
+        tt(v("nm"), v("n8"), v("alT"), MAX)
+        cp(v("nl"), v("nm"))
+        cp(v("cg"), ind(cot, v("nl")))
+        rec("P", [lambda: ten.transpose(T.pX2[:, 0:128], T.cg[:, 0:128], mf("I")[0])], [v("cg"), mf("I")], [v("pX2", 0, 128)], 512 * PCY)
+        ts(v("m128"), v("nm"), 128.0, MUL)
+        tt(v("q"), v("m128"), C("lf"), ADD)
+        tt(v("nb"), C("c2"), v("m128"), SUB)
+        for c in range(8):
+            act(v("nlx", 16 * c, 16 * c + 16), C("M16"), F.Copy, scale=v("q", c, c + 1))
+        mms(v("pM", 0, 128), [(mf("BO"), v("nlx"))], f32=True)
+        for c in range(8):
+            act(v("ab1", 128 * c, 128 * c + 16 * c + 16), v("pM", 0, 16 * c + 16), F.Abs, bias=v("nb", c, c + 1))
+        for c in range(8):
+            act(v("rl", 128 * c, 128 * c + 16 * c + 16), v("ab1", 128 * c, 128 * c + 16 * c + 16), F.Relu, bias=C("hl", c, c + 1), scale=-1.0, acc=v("los", c, c + 1))
+        ts(v("lt"), v("los"), 0.0, A.is_gt)
+        tt(v("lt"), v("lt"), C("cT"), MUL)
+        tt(v("tg"), v("lt"), v("nm"), MAX)
+        cp(v("tg16"), v("tg"))
+        tt(v("jf"), C("c15"), v("j8"), SUB)
+        cp(v("jl"), v("jf"))
+        cp(v("esel"), ind(v("e"), v("jl")))
+        scatter(v("X"), v("tg16"), v("esel"))
+        if last:
+            store("stx0", T.yx[:, 0:1024], v("X", 0, 1024))
+        ts(v("hi"), v("pX2", 0, 128), 1.0 / 32, MUL, 128.0 - 31.0 / 64, ADD)
+        ts(v("hs"), v("hi"), -32.0, MUL, 4096.0, ADD)
+        tt(v("lo"), v("pX2", 0, 128), v("hs"), ADD)
+        for h in range(48 - NS, 48):
+            act(v("sh", 128 * (h - 48 + NS), 128 * (h - 47 + NS)), v("hi"), F.Abs, bias=-160.0 - h)
+        for h in range(48 - NS, 48):
+            act(v("ohh", 128 * h, 128 * h + 128), v("sh", 128 * (h - 48 + NS), 128 * (h - 47 + NS)), F.Relu, bias=1.0, scale=-1.0)
+        for h in range(48 - NS):
+            ts(v("ohh", 128 * h, 128 * h + 128), v("hi"), 160.0 + h, A.is_equal)
+        for h in range(32):
+            ts(v("ohl", 128 * h, 128 * h + 128), v("lo"), float(h), A.is_equal)
+        for pr in range(4):
+            o, fq = v(("pF", "pX0", "pX1", "pD0")[pr], 0, 64, 1, (0, 96)), v("Fq", 64 * pr, 64 * pr + 64, 1, (0, 96))
+            mms(o, [(v("ohh", 16 * pr + k, 6144, 64), v("ohl", 16 * pr + k, 4096, 64)) for k in range(16)])
+            ts(fq, o, 0.0, A.is_gt)
+        for gi in (0, 4, 1, 5, 2, 6, 3, 7):
+            Q, q4 = divmod(gi, 4)
+            pairs = [(v("Fq", 64 * q4 + Q, 64 * q4 + 64, 2, (0, 96)), v("mb", MB["E"] + 48 * Q, MB["E"] + 48 * Q + 48, 1, (0, 96)))]
+            if t:
+                pairs = [(v("mb", MB["U"] + 256 * b + 32 * gi, MB["U"] + 256 * b + 32 * gi + 32), v("old", b, 96, 2)) for b in range(2)] + pairs
+            mms(v("pD1", 48 * Q, 48 * Q + 48, 1, (32 * q4, 32 * q4 + 32)), pairs)
+        if not last:
+            spread(t + 1)
+            mms(v("pM", 0, 1), [(mf("ON"), v("cnt"))], f32=True)
+            ts(v("ai"), v("pM", 0, 1), -1.0, MUL, 1024.0, ADD)
+            ts(v("ai"), v("ai"), 63, A.bitwise_and)
+            tt(v("thv"), v("thb"), v("ai"), ADD)
+        ts(v("Fl"), v("pD1", 0, 96), 0.0, A.is_gt)
+        for mi, bank in (("O", "pX0"), ("T", "pX1")) + ((("C", "pD0"),) if not last else ()):
+            for b in range(2):
+                mms(v(bank, b, 96, 2), [(mb(mi + str(2 * Q + b)), v("Fl", 48 * Q, 48 * Q + 48)) for Q in range(2)])
+        scan(v("Sx"), C("one"), v("pX0", 0, 96), MUL, ADD)
+        for c in range(12 - NV, 12):
+            ts(v("sg", 96 * c, 96 * c + 96), v("Sx"), C("bj", c, c + 1), A.is_lt)
+            total(v("xa", c, c + 1), v("sg", 96 * c, 96 * c + 96))
+        for c in range(12 - NV):
+            act(v("sg", 96 * c, 96 * c + 96), v("Sx"), F.Sign, bias=C("bj", c, c + 1), scale=-1.0, acc=v("xa", c, c + 1))
+        tt(v("P2", 0, 96), v("Sx"), v("pX1", 0, 96), ADD)
+        for x in ("xl", "xb"):
+            ts(v(x, 0, 12 - NV), v("xa", 0, 12 - NV), 0.5, MUL, 48.0, ADD)
+            cp(v(x, 12 - NV, 12), v("xa", 12 - NV, 12))
+        tt(v("cm"), ind(v("P2"), v("xl")), v("jr"), A.is_le)
+        mms(v("pD1", 0, 12), [(mb("I16"), v("xb"))] + [(slide("B1", m), v("cm", m, 192, 16)) for m in range(16)])
+        ts(v("no16"), v("pD1", 0, 12), 1024.0, ADD)
+        cp(v("s4"), ind(sut, v("no16")))
+        cut = [sum(RC[:i]) for i in range(len(RC) + 1)]
+        for lo, hi in zip(cut[1:], cut[2:]):
+            act(v("R", 16 * lo, 16 * hi), ind(X, v("s4", lo, hi)))
+        cp(v("R", 0, 16 * cut[1]), ind(X, v("s4", 0, cut[1])))
+        ts(v("iv"), C("jl"), v("Sx", 95, 96), A.is_ge)
+        tt(v("iv"), v("iv"), C("jT"), MUL)
+        tt(v("vl"), v("pD1", 0, 12), v("iv"), MAX)
+        cp(v("vl16"), v("vl"))
+        if not last:
+            ts(v("g2"), v("P2", 0, 96), 192.0, A.is_gt)
+            tt(v("old"), v("pD0", 0, 96), v("g2"), MUL)
+        for lo, hi in zip(cut, cut[1:]):
+            n, r = 16 * (hi - lo), v("R", 16 * lo, 16 * hi)
+            scan(v("mx", 16 * lo, 16 * hi), v("rr", 0, n), r, MIN, MAX)
+            scan(v("mn", 16 * lo, 16 * hi), v("rr", 1536, 1536 + n), r, MAX, MIN)
+            tt(v("sm", lo, hi), v("mx", 16 * lo + 15, 16 * hi, 16), v("mn", 16 * lo + 15, 16 * hi, 16), ADD)
+            ts(v("vi", lo, hi), v("sm", lo, hi), 0.5, MUL, -0.25, ADD)
+        scatter(v("X", 1024, XW), v("vl16"), v("vi"))
+    store("stx1", T.yx[:, 1024:2560], v("X", 1024, 2560))
+    flush()
+
+    for e in ("V", "S", "P", "G"):
+        wait("G", {e: cnt[e]})
+    for k in LOADS:
+        wait("G", {k: 16})
+    for k in STORES:
+        g.sync.wait_ge(T.sem[k], 16)
+    g.wait_ge(T.sem.loc, locs[0])
+    wait("G", landed)

@@ -1,50 +1,65 @@
 from concourse.mybir import dt, AluOpType as A, AxisListType, ActivationFunctionType as F
 
-XW = 2752
-CW = 2688
+PAD = 16
+XW = PAD + 2560 + 192
 NA = 64
 RO = 4
-ZS1, ZS2 = (1, 3), (1, 3)
-FAR1, FAR2 = (2, 3), (2, 3)
-NS = 12
-NV = 4
-RC = (48, 80, 64)
+CFG = {
+    "z1": "VVVV", "z2": "VVVV", "f1": "SSSS", "f2": "SSSS",
+    "nq": 4,
+    "hs": 6,
+    "hc": "S",
+    "fq": "V",
+    "sv": (8, 9, 10, 11),
+    "pre": ((0, 12),),
+    "rc": ((0, 3, "V"), (3, 8, "S"), (8, 12, "S")),
+    "vi": "S",
+    "sc": ((0, 12),),
+    "look": 0.0, "wake": 0.12, "passes": 6,
+}
+CFG.update({'passes': 3, 'look': 0.15, 'z1': 'PVVV', 'f1': 'ASSS', 'z2': 'RVVR', 'f2': 'AASS', 'sc': ((0, 6), (6, 12)), 'rc': ((0, 1, 'V'), (1, 4, 'S'), (4, 7, 'S'), (7, 10, 'S'), (10, 12, 'S')), 'pre': ((0, 4), (4, 8), (8, 12)), 'sv': (0, 1, 2, 3), 'hc': 'V', 'fq': 'S'})
 
-_B, _F, _I, _U = "bfloat16", "float32", "int32", "uint16"
+_B, _F, _I, _U, _H = "bfloat16", "float32", "int32", "uint16", "float16"
 _S = {
-    "X": (XW, _B), "cot": (CW, _I), "sut": (CW, _I), "dls": (512, _B), "dx0": (2048, _B), "dx1": (2048, _B),
-    "abt": (64, _U), "abo": (64, _U), "lab": (16, _I), "wtc": (1, _B), "thi": (1, _I),
+    "X": (XW, _B), "cot": (PAD + 2560, _I), "sut": (2576, _I), "dls": (512, _B), "dx0": (2048, _B), "dx1": (2048, _B),
+    "ab16": (64, _U), "pt": (32, _I), "po": (32, _I), "abi": (16, _I), "lab": (16, _I), "wtc": (1, _B), "thi": (1, _I),
     "dfk": (256, _U), "f2": (256, _F), "xf": (2048, _B), "xn": (2048, _B), "z": (2048, _B), "z2": (2048, _B), "e1": (2048, _B), "e": (2048, _B),
-    "da": (2048, _B), "db": (2048, _B),
-    "key": (128, _F), "sc": (128, _F), "oh": (128, _F), "pr": (128, _F), "ds": (128, _F), "prf": (128, _F), "fs": (128, _F),
-    "key2": (128, _F), "sc2": (128, _F), "d16": (16, _U), "sj": (128, _U), "ui": (128, _I), "uv": (128, _I), "w1": (128, _F), "w2": (128, _F), "nn": (128, _I),
-    "ni": (128, _I), "n16": (128, _U), "nf": (128, _F), "pay": (128, _F),
-    "k8": (8, _I), "n8": (8, _I), "j8": (8, _I), "nm": (8, _F), "nl": (8, _U), "jf": (8, _F), "jl": (8, _U),
-    "m128": (8, _F), "q": (8, _F), "nb": (8, _F), "cg": (128, _F), "nlx": (128, _F), "esel": (128, _B),
-    "hi": (128, _B), "hs": (128, _B), "lo": (128, _B), "sh": (2048, _B), "ohl": (4096, _B), "ohh": (6144, _B),
+    "sc": (128, _F), "gp": (128, _F), "qq": (128, _F), "ds": (128, _F),
+    "key2": (128, _F), "sc2": (128, _F), "d16": (16, _U), "sj": (128, _U), "ui": (128, _I), "uv": (128, _I), "w2": (128, _F), "nn": (128, _I),
+    "ni": (128, _I), "n16": (128, _U), "pay": (128, _F),
+    "k8": (8, _I), "n8": (8, _I), "j8": (8, _I), "nl": (8, _U), "jf": (8, _F), "jl": (8, _U),
+    "qb": (128, _F), "nb": (8, _F), "cg": (128, _F), "esel": (128, _B), "tabn": (1040, _F),
+    "hs": (128, _B), "ohl": (4096, _B), "ohh": (6400, _B),
     "ab1": (1024, _F), "rl": (1024, _F), "los": (8, _F), "lt": (8, _F), "tg": (8, _F), "tg16": (8, _U),
-    "Fq": (256, _B), "Fl": (96, _B), "Sx": (96, _F), "P2": (112, _B), "sg": (1152, _B), "xa": (12, _F), "xb": (12, _B), "xl": (12, _U),
+    "Fq": (256, _H), "Eh": (96, _H), "Fl": (96, _B), "Sx": (96, _B), "P2": (112, _B), "sg": (1152, _B), "sv": (1152, _B), "rv": (1152, _B),
+    "xa": (12, _F), "xb": (12, _B), "xl": (12, _U),
     "cm": (192, _B), "no16": (12, _U), "s4": (192, _U),
-    "R": (3072, _B), "mx": (3072, _B), "mn": (3072, _B), "sm": (192, _F), "vi": (192, _I),
+    "R": (3072, _B), "mx": (3072, _B), "mn": (3072, _B), "vb": (192, _B), "m128": (192, _B),
     "iv": (12, _F), "vl": (12, _F), "vl16": (12, _U), "g2": (96, _B), "old": (96, _B),
-    "al": (8, _F), "alT": (8, _F), "af": (16, _F), "u8": (16, _F), "abf": (16, _F),
-    "cnt": (1, _F), "ai": (1, _I), "thb": (1, _F), "thv": (1, _F), "th8": (1, _F),
-    "pc": (24, _F), "ci": (160, _I), "cf": (1408, _F), "mf": (1024, _F), "mb": (3024, _B), "rr": (3072, _B), "tmp": (256, _F), "jr": (192, _B),
-    "ks": (128, _F), "k4": (128, _F),
+    "dv": (8, _B), "u8": (8, _F), "abf": (16, _F), "a8": (8, _F), "az": (1, _F), "ay": (1, _B), "thb": (1, _F), "thv": (1, _F), "th8": (1, _F),
+    "pc": (32, _F), "ci": (160, _I), "cf": (1408, _F), "mf": (1024, _F), "mb": (3840, _B), "rr": (3072, _B), "tmp": (256, _F), "jr": (192, _B),
+    "ks": (128, _F), "k4": (192, _F),
 }
 SCRATCH = {k: ("sbuf", [128, n], d) for k, (n, d) in _S.items()}
-SCRATCH["a3"] = ("sbuf", [128, 8, 256], _B)
-SCRATCH["b3"] = ("sbuf", [128, 8, 256], _B)
+for _k in ("a3", "b3", "da", "db"):
+    SCRATCH[_k] = ("sbuf", [128, 8, 256], _B)
 SCRATCH["t3"] = ("sbuf", [128, 8, 32], _F)
-PSUM = ("pX0", "pX1", "pX2", "pD0", "pD1", "pF", "pM", "pQ")
+SCRATCH["t4"] = ("sbuf", [128, 4, 32], _F)
+SCRATCH["k3"] = ("sbuf", [128, 8, 16], _B)
+SCRATCH["hi4"] = ("sbuf", [128, 4, 128], _B)
+SCRATCH["lo4"] = ("sbuf", [128, 4, 128], _B)
+PSUM = ("pA", "pB", "pC", "pE", "pU", "pD0", "pD1", "pQ")
+SCRATCH["nf"] = ("sbuf", [128, 4, 32], _F)
 for _k in PSUM[:7]:
     SCRATCH[_k] = ("psum", [128, 512], _F)
-SCRATCH["pQ"] = ("psum", [128, 16, 32], _F)
-BANK = ("pX2", "pM", "pX0", "pX1")
+for _k in PSUM[7:]:
+    SCRATCH[_k] = ("psum", [128, 32, 16], _F)
+BANK = ("pA", "pB", "pC", "pE")
 LOADS = ["ldla", "ldlb", "ldco", "ldsu", "lddl", "ldx", "ldwt", "ldth"]
 STORES = ["stx0", "stx1", "sta", "stb"]
 SEMAPHORES = ["sV", "sS", "sP", "sG", "loc", "ab1a", "ab2a", "ab3a", "dl1a", "dl2a", "dl3a"] + LOADS + STORES
-CY, PCY, GAT, SCT, WAKE = 0.00104, 0.0005, 1.5, 3.5, 0.12
+CY, PCY, GAT, SCT = 0.00104, 0.00052, 1.56, 3.8
+ORDER = []
 
 
 def rank_program(g, core, T, topo):
@@ -52,6 +67,7 @@ def rank_program(g, core, T, topo):
     if rank is None:
         return
     N = len(T.cores)
+    WAKE, LOOK = CFG["wake"], CFG["look"]
     que = {"V": g.vector, "S": g.scalar, "P": g.tensor, "G": g, "Y": g.sync}
     cnt = {"V": 0, "S": 0, "P": 0, "G": 0}
     known = {k: {} for k in que}
@@ -63,9 +79,11 @@ def rank_program(g, core, T, topo):
         ap = T[name][ps, lo:hi] if step == 1 else T[name][ps, lo:hi:step]
         return (ap, [(name, lo, hi, step == 1 and p is None)], -(-(hi - lo) // step))
 
-    def v3(name, w, c0, c1, k0=0, k1=None):
+    def v3(name, c0, c1, k0=0, k1=None, step=1):
+        w = SCRATCH[name][1][2]
         k1 = w if k1 is None else k1
-        return (T[name][:, c0:c1, k0:k1], [(name, w * c0, w * c1, k0 == 0 and k1 == w)], (c1 - c0) * (k1 - k0))
+        ap = T[name][:, c0:c1, k0:k1] if step == 1 else T[name][:, c0:c1:step, k0:k1]
+        return (ap, [(name, w * c0, w * c1, k0 == 0 and k1 == w and step == 1)], -(-(c1 - c0) // step) * (k1 - k0))
 
     def ind(win, off):
         return (win[0].indirect(off[0]), win[1] + off[1], 16 * off[2])
@@ -149,39 +167,54 @@ def rank_program(g, core, T, topo):
                 if j != i:
                     succ[j].append((i, WAKE if c == 2 else 0.0))
                     npred[i] += 1
-        prio = [0.0] * n
-        for i in range(n - 1, -1, -1):
-            prio[i] = ops[i][3] + max([prio[j] + w for j, w in succ[i]] + [0.0])
-        ready, free = [0.0] * n, {k: 0.0 for k in que}
-        avail = {k: [] for k in que}
+        before = [[] for _ in range(n)]
         for i in range(n):
-            if not npred[i]:
-                avail[ops[i][0]].append(i)
-        done = 0
-        while done < n:
-            best = None
-            for e in que:
-                if avail[e]:
-                    t0 = max(free[e], min(ready[i] for i in avail[e]))
-                    i = max((i for i in avail[e] if ready[i] <= t0), key=lambda i: (prio[i], -i))
-                    if best is None or t0 < best[0]:
-                        best = (t0, e, i)
-            t0, e, i = best
-            avail[e].remove(i)
-            free[e] = t0 + (ops[i][3] if ops[i][4] is None else 0.1)
             for j, w in succ[i]:
-                ready[j] = max(ready[j], t0 + ops[i][3] + w)
-                npred[j] -= 1
-                if not npred[j]:
-                    avail[ops[j][0]].append(j)
+                before[j].append((i, w))
+
+        def plan(nxt, prv, prio):
+            left, ready, free, end, order = [len(x) for x in prv], [0.0] * n, {k: 0.0 for k in que}, [0.0] * n, []
+            avail = {k: [i for i in range(n) if not left[i] and ops[i][0] == k] for k in que}
+            while len(order) < n:
+                best = None
+                for e in que:
+                    if avail[e]:
+                        t0 = max(free[e], min(ready[i] for i in avail[e]))
+                        i = max((i for i in avail[e] if ready[i] <= t0 + LOOK), key=lambda i: (max(0, len(LOADS) - i), prio[i] - max(0.0, ready[i] - t0), -i))
+                        t0 = max(t0, ready[i])
+                        if best is None or t0 < best[0]:
+                            best = (t0, e, i)
+                t0, e, i = best
+                avail[e].remove(i)
+                free[e] = t0 + (ops[i][3] if ops[i][4] is None else 0.1)
+                end[i] = t0 + ops[i][3]
+                order.append(i)
+                for j, w in nxt[i]:
+                    ready[j] = max(ready[j], end[i] + w)
+                    left[j] -= 1
+                    if not left[j]:
+                        avail[ops[j][0]].append(j)
+            return order, end
+
+        if not ORDER:
+            prio = [0.0] * n
+            for i in range(n - 1, -1, -1):
+                prio[i] = ops[i][3] + max([prio[j] + w for j, w in succ[i]] + [0.0])
+            best = None
+            for _ in range(CFG["passes"]):
+                order, end = plan(succ, before, prio)
+                if best is None or max(end) < best[0]:
+                    best = (max(end), order)
+                prio = plan(before, succ, end)[1]
+            ORDER.extend(best[1])
+        for i in ORDER:
             issue(ops[i])
-            done += 1
         del ops[:]
 
     isv = lambda x: isinstance(x, tuple)
     raw = lambda x: x[0] if isv(x) else x
     vec, sca, ten = g.vector, g.scalar, g.tensor
-    small = lambda *xs: all(SCRATCH[x[1][0][0]][2] in (_B, _U) for x in xs)
+    small = lambda *xs: all(SCRATCH[x[1][0][0]][2] in (_B, _U, _H) for x in xs)
     isind = lambda x: len(x[1]) > 1
     inps = lambda x: x[1][0][0] in PSUM
 
@@ -194,8 +227,8 @@ def rank_program(g, core, T, topo):
         k = 1 if inps(a) or inps(b) else 2
         rec("V", [lambda: vec.tensor_tensor(o[0], a[0], b[0], op)], [a, b], [o], vcost(o, a, k))
 
-    def ts(o, a, s1, op0, s2=None, op1=None):
-        rd = [a] + [x for x in (s1, s2) if isv(x)]
+    def ts(o, a, s1, op0, s2=None, op1=None, after=()):
+        rd = [a] + [x for x in (s1, s2) if isv(x)] + list(after)
         c = vcost(o, a, 0.5 if small(o, a) else 1)
         if op1 is None:
             rec("V", [lambda: vec.tensor_scalar(o[0], a[0], raw(s1), None, op0)], rd, [o], c)
@@ -205,17 +238,20 @@ def rank_program(g, core, T, topo):
     def cp(o, a, after=()):
         rec("V", [lambda: vec.tensor_copy(o[0], a[0])], [a] + list(after), [o], vcost(o, a, 0.5 if small(o, a) else 1))
 
-    def scatter(win, off, a):
-        rec("V", [lambda: vec.tensor_copy(win[0].indirect(off[0]), a[0])], [a, off], [win], 0.05 + SCT * CY * a[2])
+    def scatter(win, off, a, b=None):
+        if b is None:
+            rec("V", [lambda: vec.tensor_copy(win[0].indirect(off[0]), a[0])], [a, off], [win], 0.05 + SCT * CY * a[2])
+        else:
+            rec("V", [lambda: vec.tensor_tensor(win[0].indirect(off[0]), a[0], b[0], A.add)], [a, b, off], [win], 0.05 + SCT * CY * a[2])
 
     def ms(o, c):
         rec("V", [lambda: vec.memset(o[0], c)], [], [o], max(64, o[2]) * CY)
 
-    def total(o, a):
-        rec("V", [lambda: vec.tensor_reduce(o[0], a[0], AxisListType.X, A.add)], [a], [o], max(64, a[2]) * CY)
-
     def scan(o, a, b, op0, op1):
         rec("V", [lambda: vec.tensor_tensor_scan(o[0], a[0], b[0], 0.0, op0, op1)], [a, b], [o], vcost(o, b, 0.5 if small(o, a, b) else 1))
+
+    def turn(o, i):
+        rec("V", [lambda: vec.transpose(o[0], i[0])], [i], [o], max(64, i[2]) * CY)
 
     def act(o, a, f=F.Copy, bias=None, scale=None, acc=None):
         rd = [a] + [x for x in (bias, scale) if isv(x)]
@@ -226,7 +262,8 @@ def rank_program(g, core, T, topo):
             kw["scale"] = raw(scale)
         if acc is not None:
             kw["accum_out"] = acc[0]
-        rec("S", [lambda: sca.activation(o[0], a[0], f, **kw)], rd, [o] + ([acc] if acc is not None else []), vcost(o, a))
+        rec("S", [lambda: sca.activation(o[0], a[0], f, **kw)], rd, [o] + ([acc] if acc is not None else []),
+            vcost(o, a) + (0.0 if acc is None else 0.02))
 
     def mms(o, pairs, start=True, stop=True, f32=False):
         n = len(pairs)
@@ -242,6 +279,9 @@ def rank_program(g, core, T, topo):
 
     def iota(o, pat, base, cm, **kw):
         rec("G", [lambda: g.iota(o[0], pat, base, cm, **kw)], [], [o], 0.13 + 2 * CY * o[2])
+
+    def gcopy(o, a, after=()):
+        rec("G", [lambda: g.affine_select(o[0], a[0], [[0, a[2]]], A.is_ge, 0.0, 0, 0)], [a] + list(after), [o], 0.17 + 2 * CY * o[2])
 
     def load(eng, name, o, src, after=()):
         rec(eng, [lambda: que[eng].dma_start(o[0], src[:])], list(after), [o], 3.0 + o[2] * 0.0015, name)
@@ -259,26 +299,39 @@ def rank_program(g, core, T, topo):
         rec("G", [lambda: g.remote_dma(T[name][:, lo:hi], a[0], T.sem[rsem], T.sem.loc, pid, rid, sum(1 << x for x in en))], [a], [trip(rsem)], 14.0, "remote")
         return len(en)
 
+    ADD, SUB, MUL, MAX, MIN = A.add, A.subtract, A.mult, A.max, A.min
+    SHR, AND = A.arith_shift_right, A.bitwise_and
+    X, cot, sut = v("X", PAD, PAD + 2560), v("cot", PAD), v("sut")
+    NQ = CFG["nq"]
+    WQ, HR, LR = 128 // NQ, 48 // NQ, 32 // NQ
+    HV = HR - CFG["hs"]
+    HB = 128 + NQ - 1
+    HW = 128 * HR + WQ
+
     lab = v("lab")
     load("Y", "ldla", v("lab", 0, 8), T.la)
     load("Y", "ldlb", v("lab", 8, 16), T.lb)
-    load("Y", "ldco", v("cot", 0, 2560), T.co)
+    load("Y", "ldco", cot, T.co)
     load("S", "lddl", v("dls", 0, 128), T.dl)
-    load("S", "ldx", v("X", 0, 2560), T.x0)
-    load("Y", "ldth", (T.thi[0:8, 0:1], [("thi", 0, 1, True)], 1), T.th)
-    load("Y", "ldwt", v("wtc"), T.wt)
-    load("Y", "ldsu", v("sut", 0, 2560), T.su, [v("cot", 0, 2560)])
+    load("S", "ldth", (T.thi[0:8, 0:1], [("thi", 0, 1, True)], 1), T.th)
+    load("S", "ldwt", v("wtc"), T.wt)
+    load("S", "ldx", X, T.x0)
+    load("Y", "ldsu", v("sut", 0, 2560), T.su, [cot])
     landed = {}
     for s in range(1, RO):
         dst = T.cores[(rank + s) % N]
         k = remote(dst, "dls", 128 * s, 128 * s + 128, v("dls", 0, 128), "dl%da" % s)
         landed["dl%da" % s], landed["ab%da" % s] = k, k
         note("dl%da" % s, k, [("dls", 128 * s, 128 * s + 128, True, True)])
-        note("ab%da" % s, k, [("abt", 16 * s, 16 * s + 16, True, True)])
+        note("ab%da" % s, k, [("pt", 8 * s, 8 * s + 8, True, True)])
 
     def spread(t):
         for k in range(16):
-            act(v("dx%d" % (t % 2), k, 2048, 16), v("dls", 128 * t, 128 * t + 128))
+            o, a = v("dx%d" % (t % 2), k, 2048, 16), v("dls", 128 * t, 128 * t + 128)
+            if t:
+                gcopy(o, a, [trip("dl%da" % t)])
+            else:
+                act(o, a)
 
     spread(0)
 
@@ -296,282 +349,344 @@ def rank_program(g, core, T, topo):
     iota(cf("kc", 128), [[0, 8], [1, 16]], 0, 0, **SM)
     iota(cf("c4", 128), [[1, 8], [0, 16]], 0, 0, **SM)
     iota(v("jr"), [[1, 192]], 0, 0, **SM)
+    iota(v("tabn"), [[1, 1040]], 0, 0, **SM)
     col = lambda n: v("tmp", 0, n)
-    cp(v("abt", 0, 16), lab)
-    ms(v("cot", 2560, CW), 0)
-    ms(v("sut", 2560, CW), 0)
+    cp(v("ab16", 0, 16), lab)
+    ts(v("u8"), v("lab", 0, 8), 4096.0, MUL)
+    tt(v("pt", 0, 8), v("u8"), v("lab", 8, 16), ADD)
+    ms(v("cot", 0, PAD), 0)
+    ms(v("sut", 2560), 0)
     P = lambda i: v("pc", i, i + 1)
     cp(P(0), v("ci", 128, 129))
-    for d, s1, op in ((129, 4, A.arith_shift_right), (130, 15, A.bitwise_and), (131, 5, A.arith_shift_right), (132, 16, A.bitwise_and)):
+    for d, s1, op in ((129, 4, SHR), (130, 15, AND), (131, 5, SHR), (132, 16, AND)):
         ts(v("ci", d, d + 1), v("ci", 128, 129), s1, op)
     for d, s in ((1, 129), (2, 130), (3, 131)):
         cp(P(d), v("ci", s, s + 1))
-    ts(P(5), v("ci", 132, 133), 1.0 / 16, A.mult)
-    ts(P(4), P(5), -1.0, A.mult, 1.0, A.add)
-    ts(P(6), P(3), 4.0, A.add)
-    tt(P(9), P(0), P(2), A.subtract)
-    ts(P(10), P(9), 15.0, A.add)
-    MB = {"B1": 0, "B16k": 144, "W": 288, "I16": 432, "E": 560, "I": 720, "nI": 848, "U": 976}
-    for i, k in enumerate(("T", "O", "C")):
-        for b in range(4):
-            MB[k + str(b)] = 1488 + 128 * (4 * i + b)
+    ts(P(5), v("ci", 132, 133), 1.0 / 16, MUL)
+    ts(P(4), P(5), -1.0, MUL, 1.0, ADD)
+    ts(P(6), P(3), 4.0, ADD)
+    tt(P(9), P(0), P(2), SUB)
+    ts(P(10), P(9), 15.0, ADD)
+    MB, nb_ = {}, 0
+    for k, n in ([(k, 144) for k in ("B1", "K1", "nK1", "K2", "nK2", "W")] + [(k, 128) for k in ("I16", "I", "nI", "Ih", "ON")] + [("U", 512), ("c240", 96)]
+                 + [(k + str(b), 128) for k in "TOC" for b in range(4)]):
+        MB[k], nb_ = nb_, nb_ + n
     mb = lambda k, n=128: v("mb", MB[k], MB[k] + n)
     slide = lambda k, m: v("mb", MB[k] + 15 - m, MB[k] + 143 - m)
-    MF = {"I": 0, "BO": 128, "ON": 256, "E8": 384, "SW00": 512, "SW01": 640, "SW10": 768, "SW11": 896}
+    MF = {"I": 0, "E8": 384, "SW00": 512, "SW01": 640, "SW10": 768, "SW11": 896}
     mf = lambda k: v("mf", MF[k], MF[k] + 128)
+    U1, U2 = 2.0 ** 28, 2.0 ** 15
     ts(mb("B1", 144), col(144), P(10), A.is_equal)
-    act(cf("k16", 128), C("kc"), scale=1.0 / 16)
-    ts(cf("R1", 128), C("kc"), 0.0, A.is_equal, 32768.0, A.mult)
-    ts(cf("R3", 128), C("kc"), 0.0, A.is_gt)
+    act(mb("K1", 144), mb("B1", 144), scale=U1)
+    act(v3("k3", 0, 4), C("kc", 0, 64), scale=U1 / 16)
+    ms(v3("k3", 4, 8), -2.0 ** 24)
+    ts(cf("R1", 128), C("kc"), 0.0, A.is_equal, 2.0 ** 45, MUL)
     ts(mf("I"), col(128), P(0), A.is_equal)
     for cpx in range(2):
         for gp in range(2):
-            ts(P(11 + 2 * cpx + gp), P(0), 16.0 * (gp - cpx), A.add)
-            ts(mf("SW%d%d" % (cpx, gp)), col(128), P(11 + 2 * cpx + gp), A.is_equal, P(4 + cpx), A.mult)
+            ts(P(11 + 2 * cpx + gp), P(0), 16.0 * (gp - cpx), ADD)
+            ts(mf("SW%d%d" % (cpx, gp)), col(128), P(11 + 2 * cpx + gp), A.is_equal, P(4 + cpx), MUL)
     act(mb("I"), mf("I"))
     act(mb("nI"), mf("I"), scale=-1.0)
-    ts(mb("W", 144), mb("B1", 144), v("wtc"), A.mult)
+    act(mb("nK1", 144), mb("B1", 144), scale=-U1)
+    ts(mb("W", 144), mb("B1", 144), v("wtc"), MUL)
     ts(mf("E8"), C("c4"), P(0), A.is_equal)
     th8 = v("th8", 0, 1, 1, (0, 8))
     cp(th8, v("thi", 0, 1, 1, (0, 8)))
-    mms(v("pM", 0, 1), [(v("mf", MF["E8"], MF["E8"] + 128, 1, (0, 8)), th8)], f32=True)
-    cp(v("thb"), v("pM", 0, 1))
-    cp(v("thv"), v("thb"))
-    ts(cf("R2", 128), C("kc"), 0.0, A.is_gt, 16777216.0, A.mult)
-    act(cf("pc2", 128), C("kc"), F.Identity, bias=15360.0, scale=-1024.0)
-    act(mb("B16k", 144), mb("B1", 144), scale=16384.0)
-    ts(mf("BO"), C("c4"), P(1), A.is_equal)
-    ms(mf("ON"), 1.0)
-    ts(cf("M16", 16), C("kc", 0, 16), P(2), A.is_equal)
-    ts(cf("lf", 8), col(8), 16.0, A.mult, P(2), A.add)
-    ts(cf("cT", 8), C("lf"), 2560.0, A.add)
-    ts(cf("c15", 8), C("lf"), 16.0, A.mult, 15.0, A.add)
-    ts(cf("hl", 8), C("lf"), 0.5, A.mult)
-    ts(cf("c2", 8), C("lf"), -0.5, A.mult, 0.5, A.add)
+    mms(v("pU", 0, 1), [(v("mf", MF["E8"], MF["E8"] + 128, 1, (0, 8)), th8)], f32=True)
+    cp(v("thb"), v("pU", 0, 1))
+    ts(v("thv"), v("thb"), U1, MUL)
+    ts(P(20), v("thb"), 10240.0, ADD, U1 / 8, MUL)
+    ts(P(21), v("thb"), -1.0 / 64, MUL, -63.0 / 128, ADD)
+    ts(P(22), P(2), -2048.0, MUL, 15.0 * 2048 + PAD, ADD)
+    ts(cf("R2", 128), C("kc"), 0.0, A.is_gt, 2.0 ** 26, MUL)
+    ts(C("R2"), C("R2"), -2.0 ** 25, ADD)
+    act(mb("K2", 144), mb("B1", 144), scale=U2)
+    act(mb("nK2", 144), mb("B1", 144), scale=-U2)
+    ms(mb("ON"), 1.0)
+    ts(cf("lf", 8), col(8), 16.0, MUL, P(2), ADD)
+    ts(cf("cT", 8), C("lf"), PAD + 2560.0, ADD)
+    ts(cf("c15", 8), C("lf"), 16.0, MUL, 15.0, ADD)
+    ts(cf("hl", 8), C("lf"), 8192.0, MUL)
+    ts(cf("c2", 8), C("lf"), -1.0 / 256, MUL, 1.0 / 256, ADD)
+    act(cf("lfr", 128), col(128), scale=1.0 / 128)
     act(mb("I16"), mf("I"), scale=16.0)
-    ts(v("ks"), C("kc"), P(2), A.is_lt, -1.0, A.mult)
-    ts(P(18), P(3), 16.0, A.mult, P(2), A.add)
-    ts(P(19), P(18), 64.0, A.add)
+    act(mb("Ih"), mf("I"), scale=0.5)
+    ts(v("ks"), C("kc"), P(2), A.is_lt, -1.0, MUL)
+    ts(P(18), P(3), 16.0, MUL, P(2), ADD)
+    ts(P(19), P(18), 64.0, ADD)
     for Q in range(2):
         for b in range(2):
             i = str(2 * Q + b)
-            ts(mb("O" + i), C("c4"), P(6 if Q else 3), A.is_equal, P(4 + b), A.mult)
-            ts(mb("C" + i), col(128), P(18 + Q), A.is_equal, P(4 + b), A.mult)
-            tt(mb("T" + i), mb("O" + i), v("ks"), A.mult)
-    ts(P(16), P(1), 32.0, A.mult, P(2), A.add)
-    ts(P(17), P(16), 16.0, A.add)
+            ts(mb("O" + i), C("c4"), P(6 if Q else 3), A.is_equal, P(4 + b), MUL)
+            ts(mb("C" + i), col(128), P(18 + Q), A.is_equal, P(4 + b), MUL)
+            tt(mb("T" + i), mb("O" + i), v("ks"), MUL)
+    ts(P(16), P(1), 32.0, MUL, P(2), ADD)
+    ts(P(17), P(16), 16.0, ADD)
     for b in range(2):
         ts(v("mb", MB["U"] + 256 * b, MB["U"] + 256 * b + 256), col(256), P(16 + b), A.is_equal)
     for Q in range(2):
-        ts(v("k4", 48 * Q, 48 * Q + 48), col(48), 2.0, A.mult, float(Q), A.add)
-        ts(v("mb", MB["E"] + 48 * Q, MB["E"] + 48 * Q + 48), v("k4", 48 * Q, 48 * Q + 48), P(0), A.is_equal)
+        a, b = v("k4", 48 * Q, 48 * Q + 48), v("k4", 96 + 48 * Q, 144 + 48 * Q)
+        ts(a, col(48), 2.0, MUL, float(Q), ADD)
+        ts(b, col(48), NQ * HV - 0.5, A.is_lt, 512.0, MUL)
+        tt(b, b, a, ADD)
+        ts(b, b, 2.0, ADD, P(0), A.is_equal)
+        ts(a, a, P(0), A.is_equal)
+    tt(v("Eh"), v("k4", 0, 96), v("k4", 96, 192), SUB)
+    for s in range(NQ):
+        ms(v("ohh", HW * s + 128 * HR, HW * s + HW), -1.0)
     ms(v("P2", 96, 112), 4096.0)
-    ms(cf("one", 96), 1.0)
-    ts(cf("jl", 12), col(12), 16.0, A.mult, P(2), A.add)
-    ts(cf("bj", 12), C("jl"), 0.5, A.add)
-    ts(cf("jT", 12), C("jl"), 1536.0, A.add)
+    ms(mb("c240", 96), 240.0)
+    ms(v("m128"), -128.0)
+    ts(cf("jl", 12), col(12), 16.0, MUL, P(2), ADD)
+    ts(cf("bj", 12), C("jl"), 0.5, ADD)
+    ts(cf("jT", 12), C("jl"), 1536.0, ADD)
+    SV = CFG["sv"]
+    if SV:
+        ms(v("rv", 0, 96 * len(SV)), 1.0)
+        ms(v("rv", 0, 96 * len(SV), 96), 0.0)
     for x, op in ((0, A.is_gt), (1536, A.is_equal)):
-        ts(v("rr", x, x + 128), C("kc"), 0.0, op, 64.0, A.mult)
+        ts(v("rr", x, x + 128), C("kc"), 0.0, op, 64.0, MUL)
         for n, m in ((128, 128), (256, 256), (512, 512), (1024, 512)):
             act(v("rr", x + n, x + n + m), v("rr", x, x + m))
 
-    ADD, SUB, MUL, MAX, MIN = A.add, A.subtract, A.mult, A.max, A.min
-    X, cot, sut = v("X", 0, 2560), v("cot"), v("sut")
     PART = {0: (0, NA), 1: (NA, 128)}
-    PU = {1: "pF", 0: "pM"}
+    PU = {1: v("pU", 0, NA), 0: v3("pQ", 0, 4)}
     qv = lambda name, i, j=None: v(name, 512 * i, 512 * (i if j is None else j) + 512)
+    q3 = lambda name, i, j=None: v3(name, 2 * i, 2 * (i if j is None else j) + 2)
 
-    def turn(src, nblk):
-        o, i = v3("t3", 32, 0, nblk), v(src, 0, 32 * nblk)
-        rec("V", [lambda: vec.transpose(o[0], i[0])], [i], [o], 32 * nblk * CY)
+    def runs(part, how, kinds):
+        i, j = 2 * part, 2 * part + 1
+        if how[i] == how[j]:
+            return [(i, j)] if how[i] in kinds else []
+        return [(x, x) for x in (i, j) if how[x] in kinds]
 
-    def swap(nblk):
+    def swap(out, nblk, srcs, start=True, stop=True):
         for cpx in range(2):
-            mms(v3("pQ", 32, 0, nblk, 16 * cpx, 16 * cpx + 16),
-                [(mf("SW%d%d" % (cpx, gp)), v3("t3", 32, 0, nblk, 16 * gp, 16 * gp + 16)) for gp in range(2)], f32=True)
+            mms(out(cpx),
+                [(mf("SW%d%d" % (cpx, gp)), v3(t, a0, a0 + nblk, 16 * gp, 16 * gp + 16)) for t, a0 in srcs for gp in range(2)], start, stop, True)
 
-    def with_q(o, lo, hi, q0, b, op):
-        tt(v(o, lo, hi), v3("pQ", 32, (q0 + lo) // 32, (q0 + hi) // 32), b, op)
+    def distance(part, w, ab, db, how, start):
+        pd = "pD%d" % part
+        for i, j in runs(part, how, "V"):
+            c0, c1 = 2 * i, 2 * j + 2
+            mms(v(pd, 16 * c0 - NA * part, 16 * c1 - NA * part), [(slide("n" + w, m), v3(db, c0, c1, 16 * m, 16 * m + 16)) for m in range(16)], False, False)
+        mms(v(pd, 0, NA), [(slide(w, m), v3(ab, 4 * part, 4 * part + 4, 16 * m, 16 * m + 16)) for m in range(16)], start, True)
 
-    def distance(pd, w, buf, part):
-        c0 = 4 * part
-        mms(v(pd, 0, NA), [(slide(w, m), v3(buf, 256, c0, c0 + 4, 16 * m, 16 * m + 16)) for m in range(16)])
-
-    def shifted(o, z, lists, dx, part, zs):
-        qs = [i for i in (2 * part, 2 * part + 1) if i not in zs]
+    def shifted(o, z, lists, dx, part, how):
         for i in (2 * part, 2 * part + 1):
-            if i in zs:
+            if how[i] != "V":
                 act(qv(z, i), ind(X, v(lists, 32 * i, 32 * i + 32)))
-                mms(v(BANK[i]), [(mb("I"), qv(z, i)), (mb("I"), qv(dx, i))])
-                ts(qv(o, i), v(BANK[i]), 0.0, MAX, 63.0, MIN)
-        if qs:
-            i, j = qs[0], qs[-1]
-            tt(qv(z, i, j), ind(X, v(lists, 32 * i, 32 * j + 32)), qv(dx, i, j), ADD)
-            ts(qv(o, i, j), qv(z, i, j), 0.0, MAX, 63.0, MIN)
+                mms(v(BANK[i]), [(mb("I"), qv(dx, i)), (mb("I"), qv(z, i))])
+                if how[i] == "P":
+                    ts(qv(o, i), v(BANK[i]), 0.0, MAX, 63.0, MIN)
+                else:
+                    act(qv(z, i), v(BANK[i]), F.Relu)
+                    ts(qv(o, i), qv(z, i), 63.0, MIN)
+        for i in (2 * part + 1, 2 * part):
+            if how[i] == "V":
+                tt(qv(z, i), ind(X, v(lists, 32 * i, 32 * i + 32)), qv(dx, i), ADD)
+                ts(qv(o, i), qv(z, i), 0.0, MAX, 63.0, MIN)
 
-    def apart(xb, db, eb, ab, lists, l0, quarters):
-        for i in quarters:
-            act(qv(xb, i), ind(X, v(lists, l0 + 32 * i, l0 + 32 * i + 32)))
-        for i in quarters:
-            mms(v(BANK[i]), [(mb("I"), qv(xb, i)), (mb("nI"), qv(eb, i))])
-            act(v3(ab, 256, 2 * i, 2 * i + 2), v(BANK[i]), F.Abs)
-        for i in (3, 2, 0, 1):
-            if i not in quarters:
-                tt(qv(db, i), ind(X, v(lists, l0 + 32 * i, l0 + 32 * i + 32)), qv(eb, i), SUB)
-                act(v3(ab, 256, 2 * i, 2 * i + 2), qv(db, i), F.Abs)
+    def apart(xb, db, eb, ab, lists, l0, part, how):
+        for i in (2 * part + 1, 2 * part):
+            lst = v(lists, l0 + 32 * i, l0 + 32 * i + 32)
+            if how[i] == "S":
+                act(qv(xb, i), ind(X, lst))
+                mms(v(BANK[i]), [(mb("I"), qv(xb, i)), (mb("nI"), qv(eb, i))])
+                act(q3(ab, i), v(BANK[i]), F.Abs)
+            elif how[i] == "A":
+                tt(qv(xb, i), ind(X, lst), qv(eb, i), SUB)
+                act(q3(ab, i), qv(xb, i), F.Abs)
+            else:
+                for c in (2 * i, 2 * i + 1):
+                    tt((T[db][:, c, :],) + v3(db, c, c + 1)[1:], ind(X, v(lists, l0 + 16 * c, l0 + 16 * c + 16)), v(eb, 256 * c, 256 * c + 256), SUB)
+                ts(q3(ab, i), q3(db, i), 0.0, MAX, 2.0, MUL)
+
+    def unpack(o, p, after=()):
+        ts(v("abi", 0, 8), p, 12, SHR, after=after)
+        ts(v("abi", 8, 16), p, 4095, AND, after=after)
+        cp(o, v("abi"))
 
     for t in range(RO):
         dx = "dx%d" % (t % 2)
         last = t == RO - 1
-        ab, here = v("abt", 16 * t, 16 * t + 16), [trip("ab%da" % t)]
-        cp(v("dfk"), ind(cot, ab), here)
+        ab, pt = v("ab16", 16 * t, 16 * t + 16), v("pt", 8 * t, 8 * t + 8)
+        if t:
+            unpack(ab, pt, [trip("ab%da" % t)])
+        cp(v("dfk"), ind(cot, ab))
+        ts(v("f2", 0, 128), v("dfk", 0, 128), 4096.0, MUL)
+        cp(v("f2", 128, 256), v("dfk", 128, 256))
+        turn(v3("t3", 0, 8), v("f2"))
+        swap(lambda cpx: v3("pQ", cpx, 8, step=2), 4, (("t3", 0), ("t3", 4)))
         for part in (1, 0):
-            shifted("e1", "z", "dfk", dx, part, ZS1)
-        cp(v("f2"), v("dfk"))
-        turn("f2", 8)
-        apart("xf", "da", "e1", "a3", "dfk", 128, FAR1)
-        swap(8)
-        distance("pD1", "B1", "a3", 1)
-        distance("pD0", "B1", "a3", 0)
+            shifted("e1", "z", "dfk", dx, part, CFG["z1"])
+            apart("xf", "da", "e1", "a3", "dfk", 128, part, CFG["f1"])
+            mms(v("pD%d" % part, 0, NA), [(mb("I"), v3("k3", 0, 4))], True, False)
+            distance(part, "K1", "a3", "da", CFG["f1"], False)
         for part in (1, 0):
             lo, hi = PART[part]
-            tt(v("key", lo, hi), v("pD%d" % part, 0, NA), C("k16", lo, hi), ADD)
-            scan(v("sc", lo, hi), C("R1", lo, hi), v("key", lo, hi), MAX, MIN)
-            for c in range(lo // 16, hi // 16):
-                ts(v("oh", 16 * c, 16 * c + 16), v("key", 16 * c, 16 * c + 16), v("sc", 16 * c + 15, 16 * c + 16), A.is_equal)
-            with_q("pr", lo, hi, 0, v("oh", lo, hi), MUL)
-            scan(v("ds", lo, hi), C("R3", lo, hi), v("pr", lo, hi), MUL, ADD)
-            cp(v("d16", 4 * part, 4 * part + 4), v("ds", lo + 15, hi, 16))
-            cp(v("sj", lo, hi), ind(sut, v("d16", 4 * part, 4 * part + 4)))
-            shifted("e", "z2", "sj", dx, part, ZS2)
-            mms(v(PU[part], 0, NA), [(slide("W", j), v("e", 16 * lo + j, 16 * hi, 16)) for j in range(16)])
             r = lambda k: v(k, lo, hi)
-            cp(r("ui"), v(PU[part], 0, NA))
-            ts(r("uv"), r("ui"), 4095, A.bitwise_and)
-            ts(r("w1"), r("uv"), -2048.0, ADD)
-            ts(r("w2"), r("uv"), 3232.0, ADD)
-            tt(r("nn"), r("w1"), r("w2"), MUL)
-            ts(r("ni"), r("nn"), 5, A.arith_shift_right, 1023, A.bitwise_and)
-            cp(r("n16"), r("ni"))
-            cp(r("nf"), r("ni"))
-        with_q("prf", 0, 128, 128, v("oh"), MUL)
-        scan(v("fs"), C("R3"), v("prf"), MUL, ADD)
-        ts(v("al"), v("sc", 15, 128, 16), v("thv"), A.is_lt)
-        tt(v("alT"), v("al"), C("cT"), MUL)
-        apart("xn", "db", "e", "b3", "n16", 0, FAR2)
-        turn("nf", 4)
-        swap(4)
-        distance("pD1", "B16k", "b3", 1)
-        distance("pD0", "B16k", "b3", 0)
-        with_q("pay", 0, 128, 0, C("pc2"), ADD)
+            key = v("pD%d" % part, 0, NA)
+            scan(r("sc"), C("R1", lo, hi), key, MAX, MIN)
+            tt(r("gp"), key, r("sc"), SUB)
+            tt(r("qq"), v3("pQ", 4 * part, 4 * part + 4), r("gp"), SUB)
+            scan(r("ds"), r("gp"), r("qq"), MIN, MAX)
+            ts(v("d16", 4 * part, 4 * part + 4), v("ds", lo + 15, hi, 16), 1.0 / 4096, MUL, -0.3125, ADD)
         for part in (1, 0):
             lo, hi = PART[part]
-            tt(v("key2", lo, hi), v("pD%d" % part, 0, NA), v("pay", lo, hi), ADD)
-            scan(v("sc2", lo, hi), C("R2", lo, hi), v("key2", lo, hi), MIN, MAX)
-        cp(v("af"), ab, here)
-        tt(v("u8", 0, 8), v("ds", 15, 128, 16), v("af", 0, 8), SUB)
-        tt(v("u8", 8, 16), v("fs", 15, 128, 16), v("af", 8, 16), SUB)
-        for h in (0, 8):
-            tt(v("u8", h, h + 8), v("u8", h, h + 8), v("al"), MUL)
-        tt(v("abf"), v("u8"), v("af"), ADD)
+            r = lambda k: v(k, lo, hi)
+            cp(r("sj"), ind(sut, v("d16", 4 * part, 4 * part + 4)))
+            shifted("e", "z2", "sj", dx, part, CFG["z2"])
+            mms(PU[part], [(slide("W", j), v("e", 16 * lo + j, 16 * hi, 16)) for j in range(16)])
+            cp(r("ui"), PU[part])
+            ts(r("uv"), r("ui"), 4095, AND)
+            ts(r("w2"), r("uv"), 1184.0, ADD)
+            tt(r("nn"), r("w2"), r("uv"), MUL)
+            ts(r("ni"), r("nn"), 5, SHR, 1023, AND)
+            cp(r("n16"), r("ni"))
+            for cpx in range(2):
+                ts(v3("nf", 2 * part, 2 * part + 2, 16 * cpx, 16 * cpx + 16), v("ni", lo + 32 * cpx, lo + 32 * cpx + 32), P(22), ADD)
+            turn(v3("t4", 2 * part, 2 * part + 2), v3("nf", 2 * part, 2 * part + 2))
+        ts(v("dv"), v("sc", 15, 128, 16), v("thv"), A.is_ge)
+        for part in (1, 0):
+            lo, hi = PART[part]
+            r = lambda k: v(k, lo, hi)
+            pd = "pD%d" % part
+            direct = not runs(part, CFG["f2"], "V")
+            mms(v(pd, 0, NA), [(mb("I"), v3("k3", 4, 8))], True, False)
+            if direct:
+                swap(lambda cpx: v(pd, 32 * cpx, 32 * cpx + 32), 2, (("t4", 2 * part),), False, False)
+            else:
+                swap(lambda cpx: v3("pQ", 8 + 4 * part + 2 * cpx, 10 + 4 * part + 2 * cpx), 2, (("t4", 2 * part),))
+                act(r("pay"), v3("pQ", 8 + 4 * part, 12 + 4 * part))
+            apart("xn", "db", "e", "b3", "n16", 0, part, CFG["f2"])
+            distance(part, "K2", "b3", "db", CFG["f2"], False)
+            if direct:
+                scan(r("sc2"), C("R2", lo, hi), v(pd, 0, NA), MIN, MAX)
+            else:
+                tt(r("key2"), v(pd, 0, NA), r("pay"), ADD)
+                scan(r("sc2"), C("R2", lo, hi), r("key2"), MIN, MAX)
+        dsl, po = v("ds", 15, 128, 16), v("po", 8 * t, 8 * t + 8)
+        tt(v("u8"), pt, dsl, SUB)
+        tt(v("u8"), v("u8"), v("dv"), MUL)
+        tt(po, v("u8"), dsl, ADD)
         if not last:
-            cp(v("abo", 16 * t, 16 * t + 16), v("abf"))
-            remote(T.cores[(rank + 1) % N], "abt", 16 * t + 16, 16 * t + 32, v("abo", 16 * t, 16 * t + 16), "ab%da" % (t + 1))
-            total(v("cnt"), v("al"))
+            remote(T.cores[(rank + 1) % N], "pt", 8 * t + 8, 8 * t + 16, po, "ab%da" % (t + 1))
         else:
+            unpack(v("abf"), po)
             store("sta", T.ya[:], v("abf", 0, 8))
             store("stb", T.yb[:], v("abf", 8, 16))
-        cp(v("k8"), v("sc2", 15, 128, 16))
-        ts(v("n8"), v("k8"), 1023, A.bitwise_and)
-        ts(v("j8"), v("k8"), 10, A.arith_shift_right, 15, A.bitwise_and)
-        tt(v("nm"), v("n8"), v("alT"), MAX)
-        cp(v("nl"), v("nm"))
-        cp(v("cg"), ind(cot, v("nl")))
-        rec("P", [lambda: ten.transpose(T.pX2[:, 0:128], T.cg[:, 0:128], mf("I")[0])], [v("cg"), mf("I")], [v("pX2", 0, 128)], 512 * PCY)
-        ts(v("m128"), v("nm"), 128.0, MUL)
-        tt(v("q"), v("m128"), C("lf"), ADD)
-        tt(v("nb"), C("c2"), v("m128"), SUB)
+        tt(v("k8"), v("sc2", 15, 128, 16), v("dv"), MUL)
+        ts(v("n8"), v("k8"), 2047, AND)
+        cp(v("nl"), v("n8"))
+        cp(v("cg"), ind(v("cot"), v("nl")))
+        rec("P", [lambda: ten.transpose(T.pA[:, 0:128], T.cg[:, 0:128], mf("I")[0])], [v("cg"), mf("I")], [v("pA", 0, 128)], 512 * PCY)
+        tt(v("qb"), ind(v("tabn"), v("nl")), C("lfr"), ADD)
+        tt(v("nb"), C("c2"), v("n8"), SUB)
         for c in range(8):
-            act(v("nlx", 16 * c, 16 * c + 16), C("M16"), F.Copy, scale=v("q", c, c + 1))
-        mms(v("pM", 0, 128), [(mf("BO"), v("nlx"))], f32=True)
+            act(v("ab1", 128 * c, 128 * c + 16 * c + 16), v("qb", 0, 16 * c + 16), F.Abs, bias=v("nb", c, c + 1))
         for c in range(8):
-            act(v("ab1", 128 * c, 128 * c + 16 * c + 16), v("pM", 0, 16 * c + 16), F.Abs, bias=v("nb", c, c + 1))
-        for c in range(8):
-            act(v("rl", 128 * c, 128 * c + 16 * c + 16), v("ab1", 128 * c, 128 * c + 16 * c + 16), F.Relu, bias=C("hl", c, c + 1), scale=-1.0, acc=v("los", c, c + 1))
-        ts(v("lt"), v("los"), 0.0, A.is_gt)
-        tt(v("lt"), v("lt"), C("cT"), MUL)
-        tt(v("tg"), v("lt"), v("nm"), MAX)
+            act(v("rl", 128 * c, 128 * c + 16 * c + 16), v("ab1", 128 * c, 128 * c + 16 * c + 16), F.Relu, bias=C("hl", c, c + 1), scale=-2.0 ** 21, acc=v("los", c, c + 1))
+        tt(v("lt"), v("los"), C("cT"), MIN)
+        tt(v("tg"), v("lt"), v("n8"), MAX)
         cp(v("tg16"), v("tg"))
+        ts(v("j8"), v("k8"), 11, SHR, 15, AND)
         tt(v("jf"), C("c15"), v("j8"), SUB)
         cp(v("jl"), v("jf"))
         cp(v("esel"), ind(v("e"), v("jl")))
-        scatter(v("X"), v("tg16"), v("esel"))
+        scatter(v("X", 0, PAD + 2560 + 128), v("tg16"), v("esel"))
         if last:
-            store("stx0", T.yx[:, 0:1024], v("X", 0, 1024))
-        ts(v("hi"), v("pX2", 0, 128), 1.0 / 32, MUL, 128.0 - 31.0 / 64, ADD)
-        ts(v("hs"), v("hi"), -32.0, MUL, 4096.0, ADD)
-        tt(v("lo"), v("pX2", 0, 128), v("hs"), ADD)
-        for h in range(48 - NS, 48):
-            act(v("sh", 128 * (h - 48 + NS), 128 * (h - 47 + NS)), v("hi"), F.Abs, bias=-160.0 - h)
-        for h in range(48 - NS, 48):
-            act(v("ohh", 128 * h, 128 * h + 128), v("sh", 128 * (h - 48 + NS), 128 * (h - 47 + NS)), F.Relu, bias=1.0, scale=-1.0)
-        for h in range(48 - NS):
-            ts(v("ohh", 128 * h, 128 * h + 128), v("hi"), 160.0 + h, A.is_equal)
-        for h in range(32):
-            ts(v("ohl", 128 * h, 128 * h + 128), v("lo"), float(h), A.is_equal)
-        for pr in range(4):
-            o, fq = v(("pF", "pX0", "pX1", "pD0")[pr], 0, 64, 1, (0, 96)), v("Fq", 64 * pr, 64 * pr + 64, 1, (0, 96))
-            mms(o, [(v("ohh", 16 * pr + k, 6144, 64), v("ohl", 16 * pr + k, 4096, 64)) for k in range(16)])
-            ts(fq, o, 0.0, A.is_gt)
-        for gi in (0, 4, 1, 5, 2, 6, 3, 7):
-            Q, q4 = divmod(gi, 4)
-            pairs = [(v("Fq", 64 * q4 + Q, 64 * q4 + 64, 2, (0, 96)), v("mb", MB["E"] + 48 * Q, MB["E"] + 48 * Q + 48, 1, (0, 96)))]
-            if t:
-                pairs = [(v("mb", MB["U"] + 256 * b + 32 * gi, MB["U"] + 256 * b + 32 * gi + 32), v("old", b, 96, 2)) for b in range(2)] + pairs
-            mms(v("pD1", 48 * Q, 48 * Q + 48, 1, (32 * q4, 32 * q4 + 32)), pairs)
+            store("stx0", T.yx[:, 0:1024], v("X", PAD, PAD + 1024))
+        sec = lambda k, s: v3(k, 0, NQ, WQ * s, WQ * s + WQ)
+        ts(sec("hi4", 0), v("pA", 0, 128), 1.0 / 32, MUL, HB - 31.0 / 64, ADD)
+        ts(v("hs"), sec("hi4", 0), -32.0, MUL, 32.0 * HB, ADD)
+        tt(sec("lo4", 0), v("pA", 0, 128), v("hs"), ADD)
+        for s in range(1, NQ):
+            if CFG["hc"] == "S":
+                act(sec("hi4", s), sec("hi4", 0), F.Identity, bias=-float(s))
+            else:
+                ts(sec("hi4", s), sec("hi4", 0), -float(s), ADD)
+            ts(sec("lo4", s), sec("lo4", 0), -float(s), ADD)
+        for s in range(NQ):
+            for h in range(HR):
+                o, x = v("ohh", HW * s + 128 * h, HW * s + 128 * h + 128), HB + 32.0 + NQ * h
+                if h < HV:
+                    ts(o, v3("hi4", s, s + 1), x, A.is_equal)
+                else:
+                    act(o, v3("hi4", s, s + 1), F.Sign, bias=0.5 - x)
+            for h in range(LR):
+                ts(v("ohl", 128 * (LR * s + h), 128 * (LR * s + h) + 128), v3("lo4", s, s + 1), float(NQ * h), A.is_equal)
+            for pp in range(WQ // 32):
+                pr = s * (WQ // 32) + pp
+                o, fq = v(("pB", "pC")[pr % 2], 0, 64, 1, (0, 98)), v("Fq", 64 * pr, 64 * pr + 64, 1, (0, 98))
+                mms(o, [(v("ohh", HW * s + 16 * pp + k, HW * s + HW, WQ // 2), v("ohl", 128 * LR * s + 16 * pp + k, 128 * LR * (s + 1), WQ // 2)) for k in range(16)])
+                cp(fq, o)
+                for Q in range(2):
+                    gi = s * (8 // NQ) + pp + Q * (WQ // 32)
+                    pairs = [(v("Fq", 64 * pr + Q, 64 * pr + 64, 2, (0, 98)), v("Eh", 48 * Q, 48 * Q + 48, 1, (0, 98)))]
+                    if t:
+                        pairs = [(v("mb", MB["U"] + 256 * b + 32 * gi, MB["U"] + 256 * b + 32 * gi + 32), v("old", b, 96, 2)) for b in range(2)] + pairs
+                    mms(v("pU", 48 * (gi // 4), 48 * (gi // 4) + 48, 1, (32 * (gi % 4), 32 * (gi % 4) + 32)), pairs)
         if not last:
             spread(t + 1)
-            mms(v("pM", 0, 1), [(mf("ON"), v("cnt"))], f32=True)
-            ts(v("ai"), v("pM", 0, 1), -1.0, MUL, 1024.0, ADD)
-            ts(v("ai"), v("ai"), 63, A.bitwise_and)
-            tt(v("thv"), v("thb"), v("ai"), ADD)
-        ts(v("Fl"), v("pD1", 0, 96), 0.0, A.is_gt)
-        for mi, bank in (("O", "pX0"), ("T", "pX1")) + ((("C", "pD0"),) if not last else ()):
+            cn = v("pD0", 0, 8)
+            mms(cn, [(mb("ON"), v("dv"))])
+            act(v("a8"), cn, F.Identity, bias=P(20), scale=U1, acc=v("az"))
+            act(v("ay"), v("az"), F.Identity, bias=P(21), scale=1.0 / (64 * U1))
+            act(v("thv"), v("ay"), F.Identity, bias=v("az"), scale=-64 * U1)
+        if CFG["fq"] == "S":
+            act(v("Fl"), v("pU", 0, 96), F.Sign)
+        else:
+            ts(v("Fl"), v("pU", 0, 96), 0.0, A.is_gt)
+        for mi, bank in (("O", "pA"), ("T", "pB")) + ((("C", "pC"),) if not last else ()):
             for b in range(2):
                 mms(v(bank, b, 96, 2), [(mb(mi + str(2 * Q + b)), v("Fl", 48 * Q, 48 * Q + 48)) for Q in range(2)])
-        scan(v("Sx"), C("one"), v("pX0", 0, 96), MUL, ADD)
-        for c in range(12 - NV, 12):
-            ts(v("sg", 96 * c, 96 * c + 96), v("Sx"), C("bj", c, c + 1), A.is_lt)
-            total(v("xa", c, c + 1), v("sg", 96 * c, 96 * c + 96))
-        for c in range(12 - NV):
-            act(v("sg", 96 * c, 96 * c + 96), v("Sx"), F.Sign, bias=C("bj", c, c + 1), scale=-1.0, acc=v("xa", c, c + 1))
-        tt(v("P2", 0, 96), v("Sx"), v("pX1", 0, 96), ADD)
-        for x in ("xl", "xb"):
-            ts(v(x, 0, 12 - NV), v("xa", 0, 12 - NV), 0.5, MUL, 48.0, ADD)
-            cp(v(x, 12 - NV, 12), v("xa", 12 - NV, 12))
-        tt(v("cm"), ind(v("P2"), v("xl")), v("jr"), A.is_le)
-        mms(v("pD1", 0, 12), [(mb("I16"), v("xb"))] + [(slide("B1", m), v("cm", m, 192, 16)) for m in range(16)])
-        ts(v("no16"), v("pD1", 0, 12), 1024.0, ADD)
-        cp(v("s4"), ind(sut, v("no16")))
-        cut = [sum(RC[:i]) for i in range(len(RC) + 1)]
-        for lo, hi in zip(cut[1:], cut[2:]):
-            act(v("R", 16 * lo, 16 * hi), ind(X, v("s4", lo, hi)))
-        cp(v("R", 0, 16 * cut[1]), ind(X, v("s4", 0, cut[1])))
+        scan(v("Sx"), v("pA", 0, 96), mb("c240", 96), ADD, MIN)
+        tt(v("P2", 0, 96), v("Sx"), v("pB", 0, 96), ADD)
         ts(v("iv"), C("jl"), v("Sx", 95, 96), A.is_ge)
         tt(v("iv"), v("iv"), C("jT"), MUL)
-        tt(v("vl"), v("pD1", 0, 12), v("iv"), MAX)
+        for n, (c0, c1) in enumerate(CFG["pre"]):
+            mine = [c for c in range(c0, c1) if c in SV]
+            rest = [c for c in range(c0, c1) if c not in SV]
+            if rest:
+                for c in rest:
+                    act(v("sg", 96 * c, 96 * c + 96), v("Sx"), F.Sign, bias=C("bj", c, c + 1), scale=-1.0, acc=v("xa", c, c + 1))
+                a, b = rest[0], rest[-1] + 1
+                ts(v("xl", a, b), v("xa", a, b), 0.5, MUL, 48.0, ADD)
+                act(v("xb", a, b), v("xa", a, b), F.Identity, bias=48.0, scale=0.5)
+            if mine:
+                for c in mine:
+                    ts(v("sg", 96 * c, 96 * c + 96), v("Sx"), C("bj", c, c + 1), A.is_lt)
+                a, b = mine[0], mine[-1] + 1
+                scan(v("sv", 96 * a, 96 * b), v("rv", 0, 96 * (b - a)), v("sg", 96 * a, 96 * b), MUL, ADD)
+                cp(v("xl", a, b), v("sv", 96 * a + 95, 96 * b, 96))
+                act(v("xb", a, b), v("sv", 96 * a + 95, 96 * b, 96))
+            pn = v(("pE", "pU")[n % 2], c0, c1)
+            tt(v("cm", 16 * c0, 16 * c1), ind(v("P2"), v("xl", c0, c1)), v("jr", 16 * c0, 16 * c1), A.is_le)
+            mms(pn, [(mb("I16"), v("xb", c0, c1))] + [(slide("B1", m), v("cm", 16 * c0 + m, 16 * c1, 16)) for m in range(16)])
+            ts(v("no16", c0, c1), pn, 1024.0, ADD)
+            cp(v("s4", 16 * c0, 16 * c1), ind(sut, v("no16", c0, c1)))
+            tt(v("vl", c0, c1), pn, v("iv", c0, c1), MAX)
         cp(v("vl16"), v("vl"))
         if not last:
             ts(v("g2"), v("P2", 0, 96), 192.0, A.is_gt)
-            tt(v("old"), v("pD0", 0, 96), v("g2"), MUL)
-        for lo, hi in zip(cut, cut[1:]):
-            n, r = 16 * (hi - lo), v("R", 16 * lo, 16 * hi)
-            scan(v("mx", 16 * lo, 16 * hi), v("rr", 0, n), r, MIN, MAX)
-            scan(v("mn", 16 * lo, 16 * hi), v("rr", 1536, 1536 + n), r, MAX, MIN)
-            tt(v("sm", lo, hi), v("mx", 16 * lo + 15, 16 * hi, 16), v("mn", 16 * lo + 15, 16 * hi, 16), ADD)
-            ts(v("vi", lo, hi), v("sm", lo, hi), 0.5, MUL, -0.25, ADD)
-        scatter(v("X", 1024, XW), v("vl16"), v("vi"))
-    store("stx1", T.yx[:, 1024:2560], v("X", 1024, 2560))
+            tt(v("old"), v("pC", 0, 96), v("g2"), MUL)
+        for c0, c1, e in CFG["rc"]:
+            (act if e == "S" else cp)(v("R", 256 * c0, 256 * c1), ind(X, v("s4", 16 * c0, 16 * c1)))
+        for n, (c0, c1, e) in enumerate(CFG["rc"]):
+            lo, hi = 256 * c0, 256 * c1
+            scan(v("mx", lo, hi), v("rr", 0, hi - lo), v("R", lo, hi), MIN, MAX)
+            scan(v("mn", lo, hi), v("rr", 1536, 1536 + hi - lo), v("R", lo, hi), MAX, MIN)
+            ps, vb = v(("pA", "pB")[n % 2], 16 * c0, 16 * c1), v("vb", 16 * c0, 16 * c1)
+            mms(ps, [(mb("Ih"), v(k, lo + 15, hi, 16)) for k in ("mx", "mn")])
+            if CFG["vi"] == "S":
+                act(vb, ps, F.Identity, bias=127.75)
+            else:
+                ts(vb, ps, 127.75, ADD)
+        for c0, c1 in CFG["sc"]:
+            scatter(v("X", PAD + 1024, XW), v("vl16", c0, c1), v("vb", 16 * c0, 16 * c1), v("m128", 16 * c0, 16 * c1))
+    store("stx1", T.yx[:, 1024:2560], v("X", PAD + 1024, PAD + 2560))
     flush()
 
     for e in ("V", "S", "P", "G"):

@@ -15,13 +15,16 @@ CFG = {
     "rc": ((0, 3, "V"), (3, 8, "S"), (8, 12, "S")),
     "vi": "S",
     "sc": ((0, 12),),
-    "look": 0.0, "wake": 0.12, "passes": 6,
+    "look": 0.0, "wake": 0.18, "passes": 6, "inorder": "", "tries": 0, "frac": 30, "amp": 1.0,
 }
-CFG.update({'passes': 3, 'look': 0.15, 'z1': 'PVVV', 'f1': 'ASSS', 'z2': 'RVVR', 'f2': 'AASS', 'sc': ((0, 6), (6, 12)), 'rc': ((0, 1, 'V'), (1, 4, 'S'), (4, 7, 'S'), (7, 10, 'S'), (10, 12, 'S')), 'pre': ((0, 4), (4, 8), (8, 12)), 'sv': (0, 1, 2, 3), 'hc': 'V', 'fq': 'S'})
+CFG.update({'passes': 3, 'look': 0.1, 'f2': 'ASAAAaSS', 'z2': 'PPvVPVRP', 'z1': 'PPVVVVvV', 'f1': 'aASSSSSS', "lift": "S", 'sc': ((0, 8), (8, 12)),
+            'rc': ((0, 2, 'S'), (2, 4, 'V'), (4, 8, 'S'), (8, 11, 'S'), (11, 12, 'S')), 'pre': ((0, 4), (4, 8), (8, 12)), 'sv': (0, 1, 2, 3), 'hc': 'S', 'fq': 'S',
+            "p1": ((4, 8), (0, 4)), "p2": ((4, 8), (0, 4)), "p3": ((4, 8), (0, 4)), "fb": ("pB", "pC", "pE", "pD1"), "nb": ("pE", "pU", "pD0")})
+CFG.update({'hs': 6, 'hc': 'V', 'fq': 'S', 'lift': 'V', 'sv': (10, 11), 'pre': ((0, 4), (4, 8), (8, 12)), 'rc': ((0, 2, 'S'), (2, 4, 'S'), (4, 6, 'V'), (6, 8, 'S'), (8, 10, 'S'), (10, 11, 'S'), (11, 12, 'S')), 'sc': ((0, 6), (6, 12)), 'look': 0.1, 'z1': 'vPVVVVvV', 'z2': 'PPvVPVRP', 'f1': 'aSSSSSSS', 'f2': 'ASAAAaSS'})
 
 _B, _F, _I, _U, _H = "bfloat16", "float32", "int32", "uint16", "float16"
 _S = {
-    "X": (XW, _B), "cot": (PAD + 2560, _I), "sut": (2576, _I), "dls": (512, _B), "dx0": (2048, _B), "dx1": (2048, _B),
+    "X": (XW, _B), "X0": (XW, _B), "cot": (PAD + 2560, _I), "sut": (2576, _I), "dls": (512, _B), "dx0": (2048, _B), "dx1": (2048, _B),
     "ab16": (64, _U), "pt": (32, _I), "po": (32, _I), "abi": (16, _I), "lab": (16, _I), "wtc": (1, _B), "thi": (1, _I),
     "dfk": (256, _U), "f2": (256, _F), "xf": (2048, _B), "xn": (2048, _B), "z": (2048, _B), "z2": (2048, _B), "e1": (2048, _B), "e": (2048, _B),
     "sc": (128, _F), "gp": (128, _F), "qq": (128, _F), "ds": (128, _F),
@@ -45,7 +48,7 @@ for _k in ("a3", "b3", "da", "db"):
     SCRATCH[_k] = ("sbuf", [128, 8, 256], _B)
 SCRATCH["t3"] = ("sbuf", [128, 8, 32], _F)
 SCRATCH["t4"] = ("sbuf", [128, 4, 32], _F)
-SCRATCH["k3"] = ("sbuf", [128, 8, 16], _B)
+SCRATCH["k3"] = ("sbuf", [128, 16, 16], _B)
 SCRATCH["hi4"] = ("sbuf", [128, 4, 128], _B)
 SCRATCH["lo4"] = ("sbuf", [128, 4, 128], _B)
 PSUM = ("pA", "pB", "pC", "pE", "pU", "pD0", "pD1", "pQ")
@@ -58,7 +61,7 @@ BANK = ("pA", "pB", "pC", "pE")
 LOADS = ["ldla", "ldlb", "ldco", "ldsu", "lddl", "ldx", "ldwt", "ldth"]
 STORES = ["stx0", "stx1", "sta", "stb"]
 SEMAPHORES = ["sV", "sS", "sP", "sG", "loc", "ab1a", "ab2a", "ab3a", "dl1a", "dl2a", "dl3a"] + LOADS + STORES
-CY, PCY, GAT, SCT = 0.00104, 0.00052, 1.56, 3.8
+CY, PCY, GAT, SCT = 0.00095, 0.00048, 1.56, 3.8
 ORDER = []
 
 
@@ -71,7 +74,7 @@ def rank_program(g, core, T, topo):
     que = {"V": g.vector, "S": g.scalar, "P": g.tensor, "G": g, "Y": g.sync}
     cnt = {"V": 0, "S": 0, "P": 0, "G": 0}
     known = {k: {} for k in que}
-    snap, hist, ops = {}, {}, []
+    snap, hist, ops, marks = {}, {}, [], []
 
     def v(name, lo=0, hi=None, step=1, p=None):
         hi = (_S[name][0] if name in _S else 512) if hi is None else hi
@@ -83,17 +86,21 @@ def rank_program(g, core, T, topo):
         w = SCRATCH[name][1][2]
         k1 = w if k1 is None else k1
         ap = T[name][:, c0:c1, k0:k1] if step == 1 else T[name][:, c0:c1:step, k0:k1]
-        return (ap, [(name, w * c0, w * c1, k0 == 0 and k1 == w and step == 1)], -(-(c1 - c0) // step) * (k1 - k0))
+        if k0 == 0 and k1 == w and step == 1:
+            return (ap, [(name, w * c0, w * c1, True)], (c1 - c0) * w)
+        return (ap, [(name, w * c + k0, w * c + k1, True) for c in range(c0, c1, step)], -(-(c1 - c0) // step) * (k1 - k0))
 
     def ind(win, off):
-        return (win[0].indirect(off[0]), win[1] + off[1], 16 * off[2])
+        return (win[0].indirect(off[0]), win[1] + off[1], 16 * off[2], True)
 
     def clash(eng, b, lo, hi, isw, e2, w2, l2, h2):
         if b in PSUM and e2 != eng:
             return 2
         if b in PSUM and e2 == "P":
             return 1
-        return 2 if (isw or w2) and lo < h2 and l2 < hi else 0
+        if not ((isw or w2) and lo < h2 and l2 < hi):
+            return 0
+        return 1 if isw and e2 == eng and eng in CFG["inorder"] else 2
 
     def need_of(eng, acc):
         need = {}
@@ -205,7 +212,10 @@ def rank_program(g, core, T, topo):
                 order, end = plan(succ, before, prio)
                 if best is None or max(end) < best[0]:
                     best = (max(end), order)
+                    keep = prio
                 prio = plan(before, succ, end)[1]
+            if "hook" in CFG:
+                best = CFG["hook"](ops, marks, plan, succ, before, keep, best)
             ORDER.extend(best[1])
         for i in ORDER:
             issue(ops[i])
@@ -215,7 +225,7 @@ def rank_program(g, core, T, topo):
     raw = lambda x: x[0] if isv(x) else x
     vec, sca, ten = g.vector, g.scalar, g.tensor
     small = lambda *xs: all(SCRATCH[x[1][0][0]][2] in (_B, _U, _H) for x in xs)
-    isind = lambda x: len(x[1]) > 1
+    isind = lambda x: len(x) > 3
     inps = lambda x: x[1][0][0] in PSUM
 
     def vcost(o, a, k=1.0):
@@ -247,8 +257,8 @@ def rank_program(g, core, T, topo):
     def ms(o, c):
         rec("V", [lambda: vec.memset(o[0], c)], [], [o], max(64, o[2]) * CY)
 
-    def scan(o, a, b, op0, op1):
-        rec("V", [lambda: vec.tensor_tensor_scan(o[0], a[0], b[0], 0.0, op0, op1)], [a, b], [o], vcost(o, b, 0.5 if small(o, a, b) else 1))
+    def scan(o, a, b, op0, op1, first=0.0):
+        rec("V", [lambda: vec.tensor_tensor_scan(o[0], a[0], b[0], first, op0, op1)], [a, b], [o], vcost(o, b, 0.5 if small(o, a, b) else 1))
 
     def turn(o, i):
         rec("V", [lambda: vec.transpose(o[0], i[0])], [i], [o], max(64, i[2]) * CY)
@@ -269,13 +279,13 @@ def rank_program(g, core, T, topo):
         n = len(pairs)
         fns = [(lambda l=l, r=r, i=i: ten.matmul(o[0], l[0], r[0], start and i == 0, stop and i == n - 1)) for i, (l, r) in enumerate(pairs)]
         rd = {}
-        for l, r in pairs:
-            for x in (l, r):
-                for (b, lo, hi, c) in x[1]:
-                    q = rd.get(b, (lo, hi))
-                    rd[b] = (min(lo, q[0]), max(hi, q[1]))
+        for side in range(2):
+            for x in pairs:
+                for (b, lo, hi, c) in x[side][1]:
+                    q = rd.get((b, side), (lo, hi))
+                    rd[(b, side)] = (min(lo, q[0]), max(hi, q[1]))
         cost = sum(max(min(64, l[2]), r[2]) for l, r in pairs) * PCY * (4 if f32 else 1)
-        rec("P", fns, [(None, [(b, lo, hi, False)], 0) for b, (lo, hi) in rd.items()], [o], cost)
+        rec("P", fns, [(None, [(b, lo, hi, False)], 0) for (b, _s), (lo, hi) in rd.items()], [o], cost)
 
     def iota(o, pat, base, cm, **kw):
         rec("G", [lambda: g.iota(o[0], pat, base, cm, **kw)], [], [o], 0.13 + 2 * CY * o[2])
@@ -301,7 +311,7 @@ def rank_program(g, core, T, topo):
 
     ADD, SUB, MUL, MAX, MIN = A.add, A.subtract, A.mult, A.max, A.min
     SHR, AND = A.arith_shift_right, A.bitwise_and
-    X, cot, sut = v("X", PAD, PAD + 2560), v("cot", PAD), v("sut")
+    XH, cot, sut = v("X", PAD, PAD + 2560), v("cot", PAD), v("sut")
     NQ = CFG["nq"]
     WQ, HR, LR = 128 // NQ, 48 // NQ, 32 // NQ
     HV = HR - CFG["hs"]
@@ -315,7 +325,7 @@ def rank_program(g, core, T, topo):
     load("S", "lddl", v("dls", 0, 128), T.dl)
     load("S", "ldth", (T.thi[0:8, 0:1], [("thi", 0, 1, True)], 1), T.th)
     load("S", "ldwt", v("wtc"), T.wt)
-    load("S", "ldx", X, T.x0)
+    load("S", "ldx", v("X0", PAD, PAD + 2560), T.x0)
     load("Y", "ldsu", v("sut", 0, 2560), T.su, [cot])
     landed = {}
     for s in range(1, RO):
@@ -378,8 +388,8 @@ def rank_program(g, core, T, topo):
     U1, U2 = 2.0 ** 28, 2.0 ** 15
     ts(mb("B1", 144), col(144), P(10), A.is_equal)
     act(mb("K1", 144), mb("B1", 144), scale=U1)
-    act(v3("k3", 0, 4), C("kc", 0, 64), scale=U1 / 16)
-    ms(v3("k3", 4, 8), -2.0 ** 24)
+    act(v3("k3", 0, 8), C("kc"), scale=U1 / 16)
+    ms(v3("k3", 8, 16), -2.0 ** 24)
     ts(cf("R1", 128), C("kc"), 0.0, A.is_equal, 2.0 ** 45, MUL)
     ts(mf("I"), col(128), P(0), A.is_equal)
     for cpx in range(2):
@@ -438,6 +448,8 @@ def rank_program(g, core, T, topo):
     ms(v("P2", 96, 112), 4096.0)
     ms(mb("c240", 96), 240.0)
     ms(v("m128"), -128.0)
+    mms(v("pU", 0, 1), [(slide("W", j), v("m128", 0, 1)) for j in range(16)])
+    cp(P(23), v("pU", 0, 1))
     ts(cf("jl", 12), col(12), 16.0, MUL, P(2), ADD)
     ts(cf("bj", 12), C("jl"), 0.5, ADD)
     ts(cf("jT", 12), C("jl"), 1536.0, ADD)
@@ -445,63 +457,74 @@ def rank_program(g, core, T, topo):
     if SV:
         ms(v("rv", 0, 96 * len(SV)), 1.0)
         ms(v("rv", 0, 96 * len(SV), 96), 0.0)
-    for x, op in ((0, A.is_gt), (1536, A.is_equal)):
-        ts(v("rr", x, x + 128), C("kc"), 0.0, op, 64.0, MUL)
+    for x, y in ((0, -32.25), (1536, 32.0)):
+        ts(v("rr", x, x + 128), C("kc"), 15.0, A.is_equal, y, MUL)
         for n, m in ((128, 128), (256, 256), (512, 512), (1024, 512)):
             act(v("rr", x + n, x + n + m), v("rr", x, x + m))
 
-    PART = {0: (0, NA), 1: (NA, 128)}
-    PU = {1: v("pU", 0, NA), 0: v3("pQ", 0, 4)}
-    qv = lambda name, i, j=None: v(name, 512 * i, 512 * (i if j is None else j) + 512)
-    q3 = lambda name, i, j=None: v3(name, 2 * i, 2 * (i if j is None else j) + 2)
+    cv = lambda name, a, b, w=256, o=0: v(name, o + w * a, o + w * b)
+    bank = lambda a, b: v(BANK[a // 2], 256 * (a % 2), 256 * (a % 2 + b - a))
 
     def runs(part, how, kinds):
-        i, j = 2 * part, 2 * part + 1
-        if how[i] == how[j]:
-            return [(i, j)] if how[i] in kinds else []
-        return [(x, x) for x in (i, j) if how[x] in kinds]
+        out = []
+        for a in range(part[1] - 2, part[0] - 2, -2):
+            two = [(a, a + 2)] if how[a] == how[a + 1] and how[a].isupper() else [(a + 1, a + 2), (a, a + 1)]
+            out += [x + (how[x[0]].upper(),) for x in two if how[x[0]].upper() in kinds]
+        return out
 
     def swap(out, nblk, srcs, start=True, stop=True):
         for cpx in range(2):
             mms(out(cpx),
                 [(mf("SW%d%d" % (cpx, gp)), v3(t, a0, a0 + nblk, 16 * gp, 16 * gp + 16)) for t, a0 in srcs for gp in range(2)], start, stop, True)
 
-    def distance(part, w, ab, db, how, start):
-        pd = "pD%d" % part
-        for i, j in runs(part, how, "V"):
-            c0, c1 = 2 * i, 2 * j + 2
-            mms(v(pd, 16 * c0 - NA * part, 16 * c1 - NA * part), [(slide("n" + w, m), v3(db, c0, c1, 16 * m, 16 * m + 16)) for m in range(16)], False, False)
-        mms(v(pd, 0, NA), [(slide(w, m), v3(ab, 4 * part, 4 * part + 4, 16 * m, 16 * m + 16)) for m in range(16)], start, True)
+    def distance(pd, part, w, ab, db, how):
+        p0, p1 = part
+        vs = [c for c in range(p0, p1) if how[c].upper() == "V"]
+        if vs:
+            c0, c1 = vs[0], vs[-1] + 1
+            assert c1 - c0 == len(vs)
+            mms(cv(pd, c0 - p0, c1 - p0, 16), [(slide("n" + w, m), v3(db, c0, c1, 16 * m, 16 * m + 16)) for m in range(16)], False, False)
+        mms(cv(pd, 0, p1 - p0, 16), [(slide(w, m), v3(ab, p0, p1, 16 * m, 16 * m + 16)) for m in range(16)], False, True)
+
+    def two(o, first, then):
+        mms(o, [first], True, False)
+        mms(o, [then], False, True)
 
     def shifted(o, z, lists, dx, part, how):
-        for i in (2 * part, 2 * part + 1):
-            if how[i] != "V":
-                act(qv(z, i), ind(X, v(lists, 32 * i, 32 * i + 32)))
-                mms(v(BANK[i]), [(mb("I"), qv(dx, i)), (mb("I"), qv(z, i))])
-                if how[i] == "P":
-                    ts(qv(o, i), v(BANK[i]), 0.0, MAX, 63.0, MIN)
-                else:
-                    act(qv(z, i), v(BANK[i]), F.Relu)
-                    ts(qv(o, i), qv(z, i), 63.0, MIN)
-        for i in (2 * part + 1, 2 * part):
-            if how[i] == "V":
-                tt(qv(z, i), ind(X, v(lists, 32 * i, 32 * i + 32)), qv(dx, i), ADD)
-                ts(qv(o, i), qv(z, i), 0.0, MAX, 63.0, MIN)
-
-    def apart(xb, db, eb, ab, lists, l0, part, how):
-        for i in (2 * part + 1, 2 * part):
-            lst = v(lists, l0 + 32 * i, l0 + 32 * i + 32)
-            if how[i] == "S":
-                act(qv(xb, i), ind(X, lst))
-                mms(v(BANK[i]), [(mb("I"), qv(xb, i)), (mb("nI"), qv(eb, i))])
-                act(q3(ab, i), v(BANK[i]), F.Abs)
-            elif how[i] == "A":
-                tt(qv(xb, i), ind(X, lst), qv(eb, i), SUB)
-                act(q3(ab, i), qv(xb, i), F.Abs)
+        for a, b, h in runs(part, how, "PRV"):
+            if h == "V":
+                tt(cv(z, a, b), ind(X, cv(lists, a, b, 16)), cv(dx, a, b), ADD)
+                ts(cv(o, a, b), cv(z, a, b), off, MAX, off + 63.0, MIN)
+                continue
+            act(cv(z, a, b), ind(X, cv(lists, a, b, 16)))
+            two(bank(a, b), (mb("I"), cv(dx, a, b)), (mb("I"), cv(z, a, b)))
+            if h == "P":
+                ts(cv(o, a, b), bank(a, b), off, MAX, off + 63.0, MIN)
             else:
-                for c in (2 * i, 2 * i + 1):
-                    tt((T[db][:, c, :],) + v3(db, c, c + 1)[1:], ind(X, v(lists, l0 + 16 * c, l0 + 16 * c + 16)), v(eb, 256 * c, 256 * c + 256), SUB)
-                ts(q3(ab, i), q3(db, i), 0.0, MAX, 2.0, MUL)
+                act(cv(z, a, b), bank(a, b), F.Relu, bias=-off)
+                ts(cv(o, a, b), cv(z, a, b), 63.0, MIN, off, ADD)
+
+    def apart(xb, db, eb, ab, lists, l0, part, how, early):
+        for a, b, h in runs(part, how, "SAV"):
+            lst = cv(lists, a, b, 16, l0)
+            if h == "S":
+                act(cv(xb, a, b), ind(X, lst))
+                pair = [(mb("I"), cv(xb, a, b)), (mb("nI"), cv(eb, a, b))]
+                two(bank(a, b), pair[1 - early], pair[early])
+                act(v3(ab, a, b), bank(a, b), F.Abs)
+            elif h == "A":
+                tt(cv(xb, a, b), ind(X, lst), cv(eb, a, b), SUB)
+                act(v3(ab, a, b), cv(xb, a, b), F.Abs)
+            else:
+                for c in range(b - 1, a - 1, -1):
+                    tt((T[db][:, c, :],) + v3(db, c, c + 1)[1:], ind(X, cv(lists, c, c + 1, 16, l0)), cv(eb, c, c + 1), SUB)
+                ts(v3(ab, a, b), v3(db, a, b), 0.0, MAX, 2.0, MUL)
+
+    def lift(o, a, x):
+        if CFG["lift"] == "S":
+            act(o, a, F.Identity, bias=x)
+        else:
+            ts(o, a, x, ADD)
 
     def unpack(o, p, after=()):
         ts(v("abi", 0, 8), p, 12, SHR, after=after)
@@ -511,6 +534,9 @@ def rank_program(g, core, T, topo):
     for t in range(RO):
         dx = "dx%d" % (t % 2)
         last = t == RO - 1
+        marks.append(len(ops))
+        off = 128.0 if t else 0.0
+        X = XH if t else v("X0", PAD, PAD + 2560)
         ab, pt = v("ab16", 16 * t, 16 * t + 16), v("pt", 8 * t, 8 * t + 8)
         if t:
             unpack(ab, pt, [trip("ab%da" % t)])
@@ -519,53 +545,61 @@ def rank_program(g, core, T, topo):
         cp(v("f2", 128, 256), v("dfk", 128, 256))
         turn(v3("t3", 0, 8), v("f2"))
         swap(lambda cpx: v3("pQ", cpx, 8, step=2), 4, (("t3", 0), ("t3", 4)))
-        for part in (1, 0):
-            shifted("e1", "z", "dfk", dx, part, CFG["z1"])
-            apart("xf", "da", "e1", "a3", "dfk", 128, part, CFG["f1"])
-            mms(v("pD%d" % part, 0, NA), [(mb("I"), v3("k3", 0, 4))], True, False)
-            distance(part, "K1", "a3", "da", CFG["f1"], False)
-        for part in (1, 0):
-            lo, hi = PART[part]
+        for n, part in enumerate(CFG["p1"]):
+            lo, hi = 16 * part[0], 16 * part[1]
             r = lambda k: v(k, lo, hi)
-            key = v("pD%d" % part, 0, NA)
+            pd = "pD%d" % (n % 2)
+            key = v(pd, 0, hi - lo)
+            shifted("e1", "z", "dfk", dx, part, CFG["z1"])
+            apart("xf", "da", "e1", "a3", "dfk", 128, part, CFG["f1"], 1)
+            mms(key, [(mb("I"), v3("k3", 0, part[1] - part[0]))], True, False)
+            distance(pd, part, "K1", "a3", "da", CFG["f1"])
             scan(r("sc"), C("R1", lo, hi), key, MAX, MIN)
             tt(r("gp"), key, r("sc"), SUB)
-            tt(r("qq"), v3("pQ", 4 * part, 4 * part + 4), r("gp"), SUB)
+            tt(r("qq"), v3("pQ", part[0], part[1]), r("gp"), SUB)
             scan(r("ds"), r("gp"), r("qq"), MIN, MAX)
-            ts(v("d16", 4 * part, 4 * part + 4), v("ds", lo + 15, hi, 16), 1.0 / 4096, MUL, -0.3125, ADD)
-        for part in (1, 0):
-            lo, hi = PART[part]
+            ts(v("d16", part[0], part[1]), v("ds", lo + 15, hi, 16), 1.0 / 4096, MUL, -0.3125, ADD)
+            cp(r("sj"), ind(sut, v("d16", part[0], part[1])))
+        for n, part in enumerate(CFG["p2"]):
+            lo, hi = 16 * part[0], 16 * part[1]
             r = lambda k: v(k, lo, hi)
-            cp(r("sj"), ind(sut, v("d16", 4 * part, 4 * part + 4)))
+            pu = v3("pQ", 8, 8 + part[1] - part[0]) if n % 2 else v("pU", 0, hi - lo)
             shifted("e", "z2", "sj", dx, part, CFG["z2"])
-            mms(PU[part], [(slide("W", j), v("e", 16 * lo + j, 16 * hi, 16)) for j in range(16)])
-            cp(r("ui"), PU[part])
+            mms(pu, [(slide("W", j), v("e", 16 * lo + j, 16 * hi, 16)) for j in range(16)])
+            if t:
+                ts(r("ui"), pu, P(23), ADD)
+            else:
+                cp(r("ui"), pu)
             ts(r("uv"), r("ui"), 4095, AND)
             ts(r("w2"), r("uv"), 1184.0, ADD)
             tt(r("nn"), r("w2"), r("uv"), MUL)
             ts(r("ni"), r("nn"), 5, SHR, 1023, AND)
             cp(r("n16"), r("ni"))
-            for cpx in range(2):
-                ts(v3("nf", 2 * part, 2 * part + 2, 16 * cpx, 16 * cpx + 16), v("ni", lo + 32 * cpx, lo + 32 * cpx + 32), P(22), ADD)
-            turn(v3("t4", 2 * part, 2 * part + 2), v3("nf", 2 * part, 2 * part + 2))
         ts(v("dv"), v("sc", 15, 128, 16), v("thv"), A.is_ge)
-        for part in (1, 0):
-            lo, hi = PART[part]
+        for n, part in enumerate(CFG["p3"]):
+            lo, hi = 16 * part[0], 16 * part[1]
             r = lambda k: v(k, lo, hi)
-            pd = "pD%d" % part
+            pd, a0, nh = "pD%d" % (n % 2), part[0] // 2, (part[1] - part[0]) // 2
+            key = v(pd, 0, hi - lo)
+            if nh == 1:
+                ts(v3("nf", a0, a0 + 1), r("ni"), P(22), ADD)
+            else:
+                for cpx in range(2):
+                    ts(v3("nf", a0, a0 + nh, 16 * cpx, 16 * cpx + 16), cv("ni", cpx, cpx + 1, 16 * nh, lo), P(22), ADD)
+            turn(v3("t4", a0, a0 + nh), v3("nf", a0, a0 + nh))
             direct = not runs(part, CFG["f2"], "V")
-            mms(v(pd, 0, NA), [(mb("I"), v3("k3", 4, 8))], True, False)
+            mms(key, [(mb("I"), v3("k3", 8, 8 + 2 * nh))], True, False)
             if direct:
-                swap(lambda cpx: v(pd, 32 * cpx, 32 * cpx + 32), 2, (("t4", 2 * part),), False, False)
+                swap(lambda cpx: cv(pd, cpx, cpx + 1, 16 * nh), nh, (("t4", a0),), False, False)
             else:
-                swap(lambda cpx: v3("pQ", 8 + 4 * part + 2 * cpx, 10 + 4 * part + 2 * cpx), 2, (("t4", 2 * part),))
-                act(r("pay"), v3("pQ", 8 + 4 * part, 12 + 4 * part))
-            apart("xn", "db", "e", "b3", "n16", 0, part, CFG["f2"])
-            distance(part, "K2", "b3", "db", CFG["f2"], False)
+                swap(lambda cpx: v3("pQ", 16 + nh * cpx, 16 + nh * cpx + nh), nh, (("t4", a0),))
+                act(r("pay"), v3("pQ", 16, 16 + 2 * nh))
+            apart("xn", "db", "e", "b3", "n16", 0, part, CFG["f2"], 0)
+            distance(pd, part, "K2", "b3", "db", CFG["f2"])
             if direct:
-                scan(r("sc2"), C("R2", lo, hi), v(pd, 0, NA), MIN, MAX)
+                scan(r("sc2"), C("R2", lo, hi), key, MIN, MAX)
             else:
-                tt(r("key2"), v(pd, 0, NA), r("pay"), ADD)
+                tt(r("key2"), key, r("pay"), ADD)
                 scan(r("sc2"), C("R2", lo, hi), r("key2"), MIN, MAX)
         dsl, po = v("ds", 15, 128, 16), v("po", 8 * t, 8 * t + 8)
         tt(v("u8"), pt, dsl, SUB)
@@ -594,10 +628,15 @@ def rank_program(g, core, T, topo):
         ts(v("j8"), v("k8"), 11, SHR, 15, AND)
         tt(v("jf"), C("c15"), v("j8"), SUB)
         cp(v("jl"), v("jf"))
-        cp(v("esel"), ind(v("e"), v("jl")))
+        ts(v("esel"), ind(v("e"), v("jl")), 128.0 - off, ADD)
+        if t in (0, RO - 1):
+            for lo in range(PAD + (1024 if last else 0), PAD + 2560, 512):
+                lift(v("X0" if last else "X", lo, lo + 512), v("X" if last else "X0", lo, lo + 512), -128.0 if last else 128.0)
         scatter(v("X", 0, PAD + 2560 + 128), v("tg16"), v("esel"))
         if last:
-            store("stx0", T.yx[:, 0:1024], v("X", PAD, PAD + 1024))
+            for lo in (PAD, PAD + 512):
+                lift(v("X0", lo, lo + 512), v("X", lo, lo + 512), -128.0)
+            store("stx0", T.yx[:, 0:1024], v("X0", PAD, PAD + 1024))
         sec = lambda k, s: v3(k, 0, NQ, WQ * s, WQ * s + WQ)
         ts(sec("hi4", 0), v("pA", 0, 128), 1.0 / 32, MUL, HB - 31.0 / 64, ADD)
         ts(v("hs"), sec("hi4", 0), -32.0, MUL, 32.0 * HB, ADD)
@@ -619,7 +658,7 @@ def rank_program(g, core, T, topo):
                 ts(v("ohl", 128 * (LR * s + h), 128 * (LR * s + h) + 128), v3("lo4", s, s + 1), float(NQ * h), A.is_equal)
             for pp in range(WQ // 32):
                 pr = s * (WQ // 32) + pp
-                o, fq = v(("pB", "pC")[pr % 2], 0, 64, 1, (0, 98)), v("Fq", 64 * pr, 64 * pr + 64, 1, (0, 98))
+                o, fq = v(CFG["fb"][pr], 0, 64, 1, (0, 98)), v("Fq", 64 * pr, 64 * pr + 64, 1, (0, 98))
                 mms(o, [(v("ohh", HW * s + 16 * pp + k, HW * s + HW, WQ // 2), v("ohl", 128 * LR * s + 16 * pp + k, 128 * LR * (s + 1), WQ // 2)) for k in range(16)])
                 cp(fq, o)
                 for Q in range(2):
@@ -639,9 +678,9 @@ def rank_program(g, core, T, topo):
             act(v("Fl"), v("pU", 0, 96), F.Sign)
         else:
             ts(v("Fl"), v("pU", 0, 96), 0.0, A.is_gt)
-        for mi, bank in (("O", "pA"), ("T", "pB")) + ((("C", "pC"),) if not last else ()):
+        for mi, pb in (("O", "pA"), ("T", "pB")) + ((("C", "pC"),) if not last else ()):
             for b in range(2):
-                mms(v(bank, b, 96, 2), [(mb(mi + str(2 * Q + b)), v("Fl", 48 * Q, 48 * Q + 48)) for Q in range(2)])
+                mms(v(pb, b, 96, 2), [(mb(mi + str(2 * Q + b)), v("Fl", 48 * Q, 48 * Q + 48)) for Q in range(2)])
         scan(v("Sx"), v("pA", 0, 96), mb("c240", 96), ADD, MIN)
         tt(v("P2", 0, 96), v("Sx"), v("pB", 0, 96), ADD)
         ts(v("iv"), C("jl"), v("Sx", 95, 96), A.is_ge)
@@ -649,6 +688,7 @@ def rank_program(g, core, T, topo):
         for n, (c0, c1) in enumerate(CFG["pre"]):
             mine = [c for c in range(c0, c1) if c in SV]
             rest = [c for c in range(c0, c1) if c not in SV]
+            assert all(x[-1] - x[0] < len(x) for x in (mine, rest) if x)
             if rest:
                 for c in rest:
                     act(v("sg", 96 * c, 96 * c + 96), v("Sx"), F.Sign, bias=C("bj", c, c + 1), scale=-1.0, acc=v("xa", c, c + 1))
@@ -662,7 +702,7 @@ def rank_program(g, core, T, topo):
                 scan(v("sv", 96 * a, 96 * b), v("rv", 0, 96 * (b - a)), v("sg", 96 * a, 96 * b), MUL, ADD)
                 cp(v("xl", a, b), v("sv", 96 * a + 95, 96 * b, 96))
                 act(v("xb", a, b), v("sv", 96 * a + 95, 96 * b, 96))
-            pn = v(("pE", "pU")[n % 2], c0, c1)
+            pn = v(CFG["nb"][n % 3], c0, c1)
             tt(v("cm", 16 * c0, 16 * c1), ind(v("P2"), v("xl", c0, c1)), v("jr", 16 * c0, 16 * c1), A.is_le)
             mms(pn, [(mb("I16"), v("xb", c0, c1))] + [(slide("B1", m), v("cm", 16 * c0 + m, 16 * c1, 16)) for m in range(16)])
             ts(v("no16", c0, c1), pn, 1024.0, ADD)
@@ -673,20 +713,23 @@ def rank_program(g, core, T, topo):
             ts(v("g2"), v("P2", 0, 96), 192.0, A.is_gt)
             tt(v("old"), v("pC", 0, 96), v("g2"), MUL)
         for c0, c1, e in CFG["rc"]:
-            (act if e == "S" else cp)(v("R", 256 * c0, 256 * c1), ind(X, v("s4", 16 * c0, 16 * c1)))
+            o, a = v("R", 256 * c0, 256 * c1), ind(XH, v("s4", 16 * c0, 16 * c1))
+            if e == "S":
+                act(o, a, scale=0.5)
+            else:
+                ts(o, a, 0.5, MUL)
         for n, (c0, c1, e) in enumerate(CFG["rc"]):
             lo, hi = 256 * c0, 256 * c1
-            scan(v("mx", lo, hi), v("rr", 0, hi - lo), v("R", lo, hi), MIN, MAX)
-            scan(v("mn", lo, hi), v("rr", 1536, 1536 + hi - lo), v("R", lo, hi), MAX, MIN)
-            ps, vb = v(("pA", "pB")[n % 2], 16 * c0, 16 * c1), v("vb", 16 * c0, 16 * c1)
-            mms(ps, [(mb("Ih"), v(k, lo + 15, hi, 16)) for k in ("mx", "mn")])
-            if CFG["vi"] == "S":
-                act(vb, ps, F.Identity, bias=127.75)
-            else:
-                ts(vb, ps, 127.75, ADD)
+            scan(v("mx", lo, hi), v("R", lo, hi), v("rr", 0, hi - lo), MAX, ADD)
+            scan(v("mn", lo, hi), v("R", lo, hi), v("rr", 1536, 1536 + hi - lo), MIN, ADD, 128.0)
         for c0, c1 in CFG["sc"]:
-            scatter(v("X", PAD + 1024, XW), v("vl16", c0, c1), v("vb", 16 * c0, 16 * c1), v("m128", 16 * c0, 16 * c1))
-    store("stx1", T.yx[:, 1024:2560], v("X", PAD + 1024, PAD + 2560))
+            a, b = v("mx", 256 * c0 + 15, 256 * c1, 16), v("mn", 256 * c0 + 15, 256 * c1, 16)
+            if not last:
+                scatter(v("X", PAD + 1024, XW), v("vl16", c0, c1), a, b)
+            else:
+                tt(v("vb", 16 * c0, 16 * c1), a, b, ADD)
+                scatter(v("X0", PAD + 1024, XW), v("vl16", c0, c1), v("vb", 16 * c0, 16 * c1), v("m128", 16 * c0, 16 * c1))
+    store("stx1", T.yx[:, 1024:2560], v("X0", PAD + 1024, PAD + 2560))
     flush()
 
     for e in ("V", "S", "P", "G"):

@@ -1,7 +1,7 @@
 from concourse.mybir import dt, AluOpType as A, AxisListType, ActivationFunctionType as F
 
 PAD = 16
-XW = PAD + 2560 + 192
+XW = PAD + 2560 + 208
 NA = 64
 RO = 4
 CFG = {
@@ -15,16 +15,18 @@ CFG = {
     "rc": ((0, 3, "V"), (3, 8, "S"), (8, 12, "S")),
     "vi": "S",
     "sc": ((0, 12),),
-    "look": 0.0, "wake": 0.18, "passes": 6, "inorder": "", "tries": 0, "frac": 30, "amp": 1.0,
+    "look": 0.0, "wake": 0.2, "idle": 1.0, "fit": 0.0, "passes": 6, "inorder": "", "tries": 0, "frac": 30, "amp": 1.0,
 }
 CFG.update({'passes': 3, 'look': 0.1, 'f2': 'ASAAAaSS', 'z2': 'PPvVPVRP', 'z1': 'PPVVVVvV', 'f1': 'aASSSSSS', "lift": "S", 'sc': ((0, 8), (8, 12)),
             'rc': ((0, 2, 'S'), (2, 4, 'V'), (4, 8, 'S'), (8, 11, 'S'), (11, 12, 'S')), 'pre': ((0, 4), (4, 8), (8, 12)), 'sv': (0, 1, 2, 3), 'hc': 'S', 'fq': 'S',
             "p1": ((4, 8), (0, 4)), "p2": ((4, 8), (0, 4)), "p3": ((4, 8), (0, 4)), "fb": ("pB", "pC", "pE", "pD1"), "nb": ("pE", "pU", "pD0")})
-CFG.update({'hs': 6, 'hc': 'V', 'fq': 'S', 'lift': 'V', 'sv': (10, 11), 'pre': ((0, 4), (4, 8), (8, 12)), 'rc': ((0, 2, 'S'), (2, 4, 'S'), (4, 6, 'V'), (6, 8, 'S'), (8, 10, 'S'), (10, 11, 'S'), (11, 12, 'S')), 'sc': ((0, 6), (6, 12)), 'look': 0.1, 'z1': 'vPVVVVvV', 'z2': 'PPvVPVRP', 'f1': 'aSSSSSSS', 'f2': 'ASAAAaSS'})
+CFG.update({'hs': 6, 'hc': 'VVVVVVV', 'kh': 2, 'es': 'V', 'g2': 'V', 'fq': 'S', 'lift': 'V', 'sv': (10, 11), 'pre': ((0, 4), (4, 8), (8, 12)), 'rc': ((0, 2, 'S'), (2, 4, 'S'), (4, 6, 'V'), (6, 8, 'S'), (8, 10, 'S'), (10, 11, 'S'), (11, 12, 'S')), 'sc': ((0, 6), (6, 12)), 'look': 0.1, 'z1': 'vPVVVVvV', 'z2': 'PPvVPVRP', 'f1': 'aSSSSSSS', 'f2': 'ASAAAaSS'})
+CFG.update({'rem': 8.0, 'cof': 1, 'pk': 1, 'l1': ((0, 8),), 'l2': ((0, 8),), 'l3': ((0, 8),), 'passes': 3, 'hs': 6, 'hc': 'SSSSSSS', 'fq': 'V', 'lift': 'S', 'es': 'V', 'g2': 'S', 'idle': 3, 'fit': 0.05, 'sv': (2, 3), 'pre': ((0, 4), (4, 8), (8, 12)), 'rc': ((0, 2, 'S'), (2, 4, 'V'), (4, 8, 'S'), (8, 11, 'S'), (11, 12, 'S')), 'sc': ((0, 6), (6, 12)), 'look': 0.15, 'p1': ((4, 8), (2, 4), (0, 2)), 'p2': ((4, 8), (2, 4), (0, 2)), 'p3': ((4, 8), (0, 4)), 'z1': 'RRpVvVVV', 'z2': 'vPVpppRV', 'f1': 'aSaaSSSa', 'f2': 'AaaSaAsA'})
+CFG.update({'hs': 6, 'hc': 'SSSSSSS', 'fq': 'V', 'lift': 'S', 'es': 'S', 'l1': ((0, 4), (4, 8)), 'l2': ((0, 8),), 'l3': ((0, 4), (4, 8)), 'cof': 1, 'pk': 1, 'idle': 6, 'fit': 0.05, 'sv': (2, 3), 'pre': ((0, 4), (4, 8), (8, 12)), 'rc': ((0, 2, 'S'), (2, 4, 'V'), (4, 6, 'S'), (6, 8, 'S'), (8, 10, 'S'), (10, 11, 'S'), (11, 12, 'V')), 'sc': ((0, 6), (6, 12)), 'look': 0.15, 'p1': ((0, 4), (4, 6), (6, 8)), 'p2': ((0, 4), (4, 8)), 'p3': ((0, 4), (4, 8)), 'z1': 'PPPvVpRR', 'z2': 'vRppPvpv', 'f1': 'aASVaaSa', 'f2': 'aASSasAa'})
 
 _B, _F, _I, _U, _H = "bfloat16", "float32", "int32", "uint16", "float16"
 _S = {
-    "X": (XW, _B), "X0": (XW, _B), "cot": (PAD + 2560, _I), "sut": (2576, _I), "dls": (512, _B), "dx0": (2048, _B), "dx1": (2048, _B),
+    "X": (XW, _B), "X0": (XW, _B), "cot": (PAD + 2560, _I), "sut": (XW - PAD, _I), "dls": (512, _B), "dx0": (2048, _B), "dx1": (2048, _B),
     "ab16": (64, _U), "pt": (32, _I), "po": (32, _I), "abi": (16, _I), "lab": (16, _I), "wtc": (1, _B), "thi": (1, _I),
     "dfk": (256, _U), "f2": (256, _F), "xf": (2048, _B), "xn": (2048, _B), "z": (2048, _B), "z2": (2048, _B), "e1": (2048, _B), "e": (2048, _B),
     "sc": (128, _F), "gp": (128, _F), "qq": (128, _F), "ds": (128, _F),
@@ -34,13 +36,13 @@ _S = {
     "qb": (128, _F), "nb": (8, _F), "cg": (128, _F), "esel": (128, _B), "tabn": (1040, _F),
     "hs": (128, _B), "ohl": (4096, _B), "ohh": (6400, _B),
     "ab1": (1024, _F), "rl": (1024, _F), "los": (8, _F), "lt": (8, _F), "tg": (8, _F), "tg16": (8, _U),
-    "Fq": (256, _H), "Eh": (96, _H), "Fl": (96, _B), "Sx": (96, _B), "P2": (112, _B), "sg": (1152, _B), "sv": (1152, _B), "rv": (1152, _B),
+    "Fq": (256, _H), "Eh": (96, _H), "Fl": (96, _B), "Sx": (120, _B), "P2": (112, _B), "sg": (1440, _B), "sq": (1296, _B), "sv": (1296, _B), "rv": (1296, _B),
     "xa": (12, _F), "xb": (12, _B), "xl": (12, _U),
     "cm": (192, _B), "no16": (12, _U), "s4": (192, _U),
     "R": (3072, _B), "mx": (3072, _B), "mn": (3072, _B), "vb": (192, _B), "m128": (192, _B),
-    "iv": (12, _F), "vl": (12, _F), "vl16": (12, _U), "g2": (96, _B), "old": (96, _B),
+    "vl16": (12, _U), "old": (96, _B), "cof": (2560, _F),
     "dv": (8, _B), "u8": (8, _F), "abf": (16, _F), "a8": (8, _F), "az": (1, _F), "ay": (1, _B), "thb": (1, _F), "thv": (1, _F), "th8": (1, _F),
-    "pc": (32, _F), "ci": (160, _I), "cf": (1408, _F), "mf": (1024, _F), "mb": (3840, _B), "rr": (3072, _B), "tmp": (256, _F), "jr": (192, _B),
+    "pc": (32, _F), "ci": (160, _I), "cf": (1408, _F), "mf": (1024, _F), "mb": (3872, _B), "rr": (3072, _B), "tmp": (256, _F), "jr": (192, _B),
     "ks": (128, _F), "k4": (192, _F),
 }
 SCRATCH = {k: ("sbuf", [128, n], d) for k, (n, d) in _S.items()}
@@ -61,7 +63,7 @@ BANK = ("pA", "pB", "pC", "pE")
 LOADS = ["ldla", "ldlb", "ldco", "ldsu", "lddl", "ldx", "ldwt", "ldth"]
 STORES = ["stx0", "stx1", "sta", "stb"]
 SEMAPHORES = ["sV", "sS", "sP", "sG", "loc", "ab1a", "ab2a", "ab3a", "dl1a", "dl2a", "dl3a"] + LOADS + STORES
-CY, PCY, GAT, SCT = 0.00095, 0.00048, 1.56, 3.8
+CY, PCY, GAT, SCT = 0.00091, 0.00046, 1.56, 3.8
 ORDER = []
 
 
@@ -70,7 +72,7 @@ def rank_program(g, core, T, topo):
     if rank is None:
         return
     N = len(T.cores)
-    WAKE, LOOK = CFG["wake"], CFG["look"]
+    WAKE, LOOK, IDLE, FIT = CFG["wake"], CFG["look"], CFG["idle"], CFG["fit"]
     que = {"V": g.vector, "S": g.scalar, "P": g.tensor, "G": g, "Y": g.sync}
     cnt = {"V": 0, "S": 0, "P": 0, "G": 0}
     known = {k: {} for k in que}
@@ -167,8 +169,8 @@ def rank_program(g, core, T, topo):
                 h = h2.setdefault(b, [])
                 if isw and full and b not in PSUM:
                     h[:] = [x for x in h if not (lo <= x[3] and x[4] <= hi)]
-                elif b in PSUM and len(h) > 60:
-                    del h[:-60]
+                elif b in PSUM and eng == "P":
+                    del h[:]
                 h.append((i, eng, isw, lo, hi))
             for j, c in pred.items():
                 if j != i:
@@ -182,16 +184,19 @@ def rank_program(g, core, T, topo):
         def plan(nxt, prv, prio):
             left, ready, free, end, order = [len(x) for x in prv], [0.0] * n, {k: 0.0 for k in que}, [0.0] * n, []
             avail = {k: [i for i in range(n) if not left[i] and ops[i][0] == k] for k in que}
+            prio = [x + 1000.0 * max(0, len(LOADS) - i) for i, x in enumerate(prio)]
+            pick = {}
             while len(order) < n:
-                best = None
                 for e in que:
-                    if avail[e]:
-                        t0 = max(free[e], min(ready[i] for i in avail[e]))
-                        i = max((i for i in avail[e] if ready[i] <= t0 + LOOK), key=lambda i: (max(0, len(LOADS) - i), prio[i] - max(0.0, ready[i] - t0), -i))
-                        t0 = max(t0, ready[i])
-                        if best is None or t0 < best[0]:
-                            best = (t0, e, i)
-                t0, e, i = best
+                    if avail[e] and e not in pick:
+                        t0 = max(free[e], min([ready[i] for i in avail[e]]))
+                        worth = lambda i: (prio[i] - IDLE * (ready[i] - t0) if ready[i] > t0 else prio[i], -i)
+                        i = max([i for i in avail[e] if ready[i] <= t0 + LOOK], key=worth)
+                        if ready[i] > t0:
+                            i = max([j for j in avail[e] if max(t0, ready[j]) + ops[j][3] <= ready[i] + FIT], key=worth, default=i)
+                        pick[e] = (max(t0, ready[i]), e, i)
+                t0, e, i = min(pick.values())
+                del pick[e]
                 avail[e].remove(i)
                 free[e] = t0 + (ops[i][3] if ops[i][4] is None else 0.1)
                 end[i] = t0 + ops[i][3]
@@ -201,6 +206,7 @@ def rank_program(g, core, T, topo):
                     left[j] -= 1
                     if not left[j]:
                         avail[ops[j][0]].append(j)
+                        pick.pop(ops[j][0], None)
             return order, end
 
         if not ORDER:
@@ -293,8 +299,8 @@ def rank_program(g, core, T, topo):
     def gcopy(o, a, after=()):
         rec("G", [lambda: g.affine_select(o[0], a[0], [[0, a[2]]], A.is_ge, 0.0, 0, 0)], [a] + list(after), [o], 0.17 + 2 * CY * o[2])
 
-    def load(eng, name, o, src, after=()):
-        rec(eng, [lambda: que[eng].dma_start(o[0], src[:])], list(after), [o], 3.0 + o[2] * 0.0015, name)
+    def load(eng, name, o, src, after=(), more=0.0):
+        rec(eng, [lambda: que[eng].dma_start(o[0], src[:])], list(after), [o], 3.0 + o[2] * 0.0015 + more, name)
 
     def store(name, dst, a):
         rec("Y", [lambda: g.sync.dma_start(dst, a[0])], [a], [], 3.0, name)
@@ -306,13 +312,13 @@ def rank_program(g, core, T, topo):
         rid, pid = topo.addr(dst)[:2]
         en = topo.engines(core, dst)[:4]
         locs[0] += len(en)
-        rec("G", [lambda: g.remote_dma(T[name][:, lo:hi], a[0], T.sem[rsem], T.sem.loc, pid, rid, sum(1 << x for x in en))], [a], [trip(rsem)], 14.0, "remote")
+        rec("G", [lambda: g.remote_dma(T[name][:, lo:hi], a[0], T.sem[rsem], T.sem.loc, pid, rid, sum(1 << x for x in en))], [a], [trip(rsem)], CFG["rem"], "remote")
         return len(en)
 
     ADD, SUB, MUL, MAX, MIN = A.add, A.subtract, A.mult, A.max, A.min
     SHR, AND = A.arith_shift_right, A.bitwise_and
     XH, cot, sut = v("X", PAD, PAD + 2560), v("cot", PAD), v("sut")
-    NQ = CFG["nq"]
+    NQ, KH = CFG["nq"], CFG["kh"]
     WQ, HR, LR = 128 // NQ, 48 // NQ, 32 // NQ
     HV = HR - CFG["hs"]
     HB = 128 + NQ - 1
@@ -325,7 +331,7 @@ def rank_program(g, core, T, topo):
     load("S", "lddl", v("dls", 0, 128), T.dl)
     load("S", "ldth", (T.thi[0:8, 0:1], [("thi", 0, 1, True)], 1), T.th)
     load("S", "ldwt", v("wtc"), T.wt)
-    load("S", "ldx", v("X0", PAD, PAD + 2560), T.x0)
+    load("S", "ldx", v("X0", PAD, PAD + 2560), T.x0, more=2.0)
     load("Y", "ldsu", v("sut", 0, 2560), T.su, [cot])
     landed = {}
     for s in range(1, RO):
@@ -338,6 +344,7 @@ def rank_program(g, core, T, topo):
     def spread(t):
         for k in range(16):
             o, a = v("dx%d" % (t % 2), k, 2048, 16), v("dls", 128 * t, 128 * t + 128)
+            o = (o[0], [(o[1][0][0], k, k + 1, True)], 128)
             if t:
                 gcopy(o, a, [trip("dl%da" % t)])
             else:
@@ -378,12 +385,12 @@ def rank_program(g, core, T, topo):
     tt(P(9), P(0), P(2), SUB)
     ts(P(10), P(9), 15.0, ADD)
     MB, nb_ = {}, 0
-    for k, n in ([(k, 144) for k in ("B1", "K1", "nK1", "K2", "nK2", "W")] + [(k, 128) for k in ("I16", "I", "nI", "Ih", "ON")] + [("U", 512), ("c240", 96)]
+    for k, n in ([(k, 144) for k in ("B1", "K1", "nK1", "K2", "nK2", "W")] + [(k, 128) for k in ("I16", "I", "nI", "Z", "ON")] + [("U", 512), ("c240", 112)]
                  + [(k + str(b), 128) for k in "TOC" for b in range(4)]):
         MB[k], nb_ = nb_, nb_ + n
     mb = lambda k, n=128: v("mb", MB[k], MB[k] + n)
     slide = lambda k, m: v("mb", MB[k] + 15 - m, MB[k] + 143 - m)
-    MF = {"I": 0, "E8": 384, "SW00": 512, "SW01": 640, "SW10": 768, "SW11": 896}
+    MF = {"I": 0, "SL": 128, "E8": 384, "SW00": 512, "SW01": 640, "SW10": 768, "SW11": 896}
     mf = lambda k: v("mf", MF[k], MF[k] + 128)
     U1, U2 = 2.0 ** 28, 2.0 ** 15
     ts(mb("B1", 144), col(144), P(10), A.is_equal)
@@ -414,6 +421,12 @@ def rank_program(g, core, T, topo):
     act(mb("K2", 144), mb("B1", 144), scale=U2)
     act(mb("nK2", 144), mb("B1", 144), scale=-U2)
     ms(mb("ON"), 1.0)
+    ms(mb("Z"), 0.0)
+    if KH > 1:
+        ts(P(24), P(2), 7.5, A.is_gt, 56.0, MUL)
+        ts(P(25), P(1), 8.0, MUL, P(2), ADD)
+        tt(P(24), P(24), P(25), ADD)
+        ts(mf("SL"), col(128), P(24), A.is_equal)
     ts(cf("lf", 8), col(8), 16.0, MUL, P(2), ADD)
     ts(cf("cT", 8), C("lf"), PAD + 2560.0, ADD)
     ts(cf("c15", 8), C("lf"), 16.0, MUL, 15.0, ADD)
@@ -421,16 +434,17 @@ def rank_program(g, core, T, topo):
     ts(cf("c2", 8), C("lf"), -1.0 / 256, MUL, 1.0 / 256, ADD)
     act(cf("lfr", 128), col(128), scale=1.0 / 128)
     act(mb("I16"), mf("I"), scale=16.0)
-    act(mb("Ih"), mf("I"), scale=0.5)
     ts(v("ks"), C("kc"), P(2), A.is_lt, -1.0, MUL)
     ts(P(18), P(3), 16.0, MUL, P(2), ADD)
     ts(P(19), P(18), 64.0, ADD)
+    ts(v("pc", 26, 28), v("pc", 4, 6), 256.0, MUL)
     for Q in range(2):
         for b in range(2):
             i = str(2 * Q + b)
             ts(mb("O" + i), C("c4"), P(6 if Q else 3), A.is_equal, P(4 + b), MUL)
-            ts(mb("C" + i), col(128), P(18 + Q), A.is_equal, P(4 + b), MUL)
+            ts(mb("C" + i), col(128), P(18 + Q), A.is_equal, P(26 + b), MUL)
             tt(mb("T" + i), mb("O" + i), v("ks"), MUL)
+            tt(mb("C" + i), mb("C" + i), mb("T" + i), ADD)
     ts(P(16), P(1), 32.0, MUL, P(2), ADD)
     ts(P(17), P(16), 16.0, ADD)
     for b in range(2):
@@ -445,24 +459,27 @@ def rank_program(g, core, T, topo):
     tt(v("Eh"), v("k4", 0, 96), v("k4", 96, 192), SUB)
     for s in range(NQ):
         ms(v("ohh", HW * s + 128 * HR, HW * s + HW), -1.0)
-    ms(v("P2", 96, 112), 4096.0)
-    ms(mb("c240", 96), 240.0)
+    ms(mb("c240", 108), 240.0)
+    ms(v("Sx", 0, 12), -1.0)
     ms(v("m128"), -128.0)
     mms(v("pU", 0, 1), [(slide("W", j), v("m128", 0, 1)) for j in range(16)])
     cp(P(23), v("pU", 0, 1))
     ts(cf("jl", 12), col(12), 16.0, MUL, P(2), ADD)
     ts(cf("bj", 12), C("jl"), 0.5, ADD)
-    ts(cf("jT", 12), C("jl"), 1536.0, ADD)
+    ms(v("P2", 96, 112), 0.0)
+    ts(v("P2", 97, 109), C("jl"), 1.0, ADD)
     SV = CFG["sv"]
     if SV:
-        ms(v("rv", 0, 96 * len(SV)), 1.0)
-        ms(v("rv", 0, 96 * len(SV), 96), 0.0)
+        ms(v("rv", 0, 108 * len(SV)), 1.0)
+        ms(v("rv", 0, 108 * len(SV), 108), 0.0)
+        ms(v("sq", 108 * SV[0], 108 * SV[-1] + 108), 0.0)
     for x, y in ((0, -32.25), (1536, 32.0)):
         ts(v("rr", x, x + 128), C("kc"), 15.0, A.is_equal, y, MUL)
         for n, m in ((128, 128), (256, 256), (512, 512), (1024, 512)):
             act(v("rr", x + n, x + n + m), v("rr", x, x + m))
 
     cv = lambda name, a, b, w=256, o=0: v(name, o + w * a, o + w * b)
+    shifts = lambda dx, a, b: (cv(dx, a, b)[0], [(dx, 0, 16, False)], 256 * (b - a))
     bank = lambda a, b: v(BANK[a // 2], 256 * (a % 2), 256 * (a % 2 + b - a))
 
     def runs(part, how, kinds):
@@ -493,11 +510,11 @@ def rank_program(g, core, T, topo):
     def shifted(o, z, lists, dx, part, how):
         for a, b, h in runs(part, how, "PRV"):
             if h == "V":
-                tt(cv(z, a, b), ind(X, cv(lists, a, b, 16)), cv(dx, a, b), ADD)
+                tt(cv(z, a, b), ind(X, cv(lists, a, b, 16)), shifts(dx, a, b), ADD)
                 ts(cv(o, a, b), cv(z, a, b), off, MAX, off + 63.0, MIN)
                 continue
             act(cv(z, a, b), ind(X, cv(lists, a, b, 16)))
-            two(bank(a, b), (mb("I"), cv(dx, a, b)), (mb("I"), cv(z, a, b)))
+            two(bank(a, b), (mb("I"), shifts(dx, a, b)), (mb("I"), cv(z, a, b)))
             if h == "P":
                 ts(cv(o, a, b), bank(a, b), off, MAX, off + 63.0, MIN)
             else:
@@ -520,7 +537,68 @@ def rank_program(g, core, T, topo):
                     tt((T[db][:, c, :],) + v3(db, c, c + 1)[1:], ind(X, cv(lists, c, c + 1, 16, l0)), cv(eb, c, c + 1), SUB)
                 ts(v3(ab, a, b), v3(db, a, b), 0.0, MAX, 2.0, MUL)
 
+    def shift(e, o, a, x, scale=None):
+        if e == "S":
+            act(o, a, F.Identity, bias=x, scale=scale)
+        elif scale is None:
+            ts(o, a, x, ADD)
+        else:
+            ts(o, a, scale, MUL, x, ADD)
+
+    def flags(hf, final, t):
+        nc, KK, NS = 8 // KH, 16 // KH, NQ // KH
+        c0, l0, nl, s0, PP = nc * hf, 16 * nc * hf, 16 * nc, NS * hf, 4 // NS
+        r8 = lambda k: v(k, c0, c0 + nc)
+        tt(r8("k8"), v("sc2", l0 + 15, l0 + nl, 16), r8("dv"), MUL)
+        ts(r8("n8"), r8("k8"), 2047, AND)
+        cp(r8("nl"), r8("n8"))
+        cg, tb = v("cg", l0, l0 + nl), BANK[2 * hf] if final else "pU"
+        cp(cg, ind(v("cot"), r8("nl")))
+        for kh in range(KH):
+            mms(v(tb, 0, nl, 1, (nl * kh, nl * kh + nl)), [(cg, v("mf", MF["SL"] + nl * kh, MF["SL"] + nl * kh + nl) if KH > 1 else mf("I"))], f32=True)
+        sec = lambda k, s: v3(k, s0, s0 + NS, WQ * s, WQ * s + WQ)
+        ts(sec("hi4", 0), v(tb, 0, nl), 1.0 / 32, MUL, HB - 31.0 / 64, ADD)
+        shift(CFG["hc"][0], v("hs", l0, l0 + nl), sec("hi4", 0), 32.0 * HB, -32.0)
+        tt(sec("lo4", 0), v(tb, 0, nl), v("hs", l0, l0 + nl), ADD)
+        for s in range(1, NQ):
+            shift(CFG["hc"][s], sec("hi4", s), sec("hi4", 0), -float(s))
+            shift(CFG["hc"][3 + s], sec("lo4", s), sec("lo4", 0), -float(s))
+        FB = BANK[2 * (hf != final):][:2] if KH > 1 else CFG["fb"]
+        if not final:
+            for b in FB:
+                mms(v(b, 0, 128, 1, (0, 98)), [(mb("Z", 98), mb("I"))], True, False)
+        else:
+            mms(v("pU", 0, 96), [(mb("Z"), mb("I", 96))], True, False)
+            for Q in range(2 if t else 0):
+                mms(v("pU", 48 * Q, 48 * Q + 48), [(v("mb", MB["U"] + 256 * b + 128 * Q, MB["U"] + 256 * b + 128 * Q + 128), v("old", b, 96, 2)) for b in range(2)], False, False)
+        for s in range(s0, s0 + NS):
+            for h in range(HR):
+                o, x = v("ohh", HW * s + 128 * h, HW * s + 128 * h + 128), HB + 32.0 + NQ * h
+                if h < HV:
+                    ts(o, v3("hi4", s, s + 1), x, A.is_equal)
+                else:
+                    act(o, v3("hi4", s, s + 1), F.Sign, bias=0.5 - x)
+            for h in range(LR):
+                ts(v("ohl", 128 * (LR * s + h), 128 * (LR * s + h) + 128), v3("lo4", s, s + 1), float(NQ * h), A.is_equal)
+            for pp in range(PP):
+                pr = (s - s0) * PP + pp
+                o = v(FB[pr // KH], 64 * (pr % KH), 64 * (pr % KH) + 64, 1, (0, 98))
+                mms(o, [(v("ohh", HW * s + KK * pp + k, HW * s + HW, WQ // 2), v("ohl", 128 * LR * s + KK * pp + k, 128 * LR * (s + 1), WQ // 2)) for k in range(KK)],
+                    KH == 1, KH == 1)
+                if final and (pr + 1) % KH == 0:
+                    if KH > 1:
+                        mms(v(FB[pr // KH], 0, 128, 1, (0, 98)), [(mb("Z", 98), mb("I"))], False, True)
+                    cp(v("Fq", 64 * (pr + 1 - KH), 64 * pr + 64, 1, (0, 98)), v(FB[pr // KH], 0, 64 * KH, 1, (0, 98)))
+                    for p2 in range(pr + 1 - KH, pr + 1):
+                        for Q in range(2):
+                            gi = 2 * PP * (p2 // PP) + p2 % PP + Q * PP
+                            mms(v("pU", 48 * (gi // 4), 48 * (gi // 4) + 48, 1, (32 * (gi % 4), 32 * (gi % 4) + 32)),
+                                [(v("Fq", 64 * p2 + Q, 64 * p2 + 64, 2, (0, 98)), v("Eh", 48 * Q, 48 * Q + 48, 1, (0, 98)))], False, False)
+        if final:
+            mms(v("pU", 0, 96), [(mb("Z"), mb("I", 96))], False, True)
+
     def lift(o, a, x):
+        a = (a[0], a[1] + v("sc")[1], a[2])
         if CFG["lift"] == "S":
             act(o, a, F.Identity, bias=x)
         else:
@@ -540,11 +618,25 @@ def rank_program(g, core, T, topo):
         ab, pt = v("ab16", 16 * t, 16 * t + 16), v("pt", 8 * t, 8 * t + 8)
         if t:
             unpack(ab, pt, [trip("ab%da" % t)])
-        cp(v("dfk"), ind(cot, ab))
-        ts(v("f2", 0, 128), v("dfk", 0, 128), 4096.0, MUL)
-        cp(v("f2", 128, 256), v("dfk", 128, 256))
-        turn(v3("t3", 0, 8), v("f2"))
-        swap(lambda cpx: v3("pQ", cpx, 8, step=2), 4, (("t3", 0), ("t3", 4)))
+        if t and CFG["cof"]:
+            act(v("f2", 0, 128), ind(v("cof"), v("ab16", 16 * t, 16 * t + 8)), scale=4096.0)
+            act(v("f2", 128, 256), ind(v("cof"), v("ab16", 16 * t + 8, 16 * t + 16)))
+            ts(v("dfk", 0, 128), v("f2", 0, 128), 1.0 / 4096, MUL)
+            cp(v("dfk", 128, 256), v("f2", 128, 256))
+        else:
+            cp(v("dfk"), ind(cot, ab))
+            ts(v("f2", 0, 128), v("dfk", 0, 128), 4096.0, MUL)
+            cp(v("f2", 128, 256), v("dfk", 128, 256))
+        if t == 0 and CFG["cof"]:
+            for lo in range(0, 2560, 320):
+                cp(v("cof", lo, lo + 320), v("cot", PAD + lo, PAD + lo + 320))
+        if CFG["pk"]:
+            mms(v3("pQ", 24, 32), [(mf("I"), v("f2", 0, 128)), (mf("I"), v("f2", 128, 256))], f32=True)
+            turn(v3("t3", 0, 4), v3("pQ", 24, 32))
+            swap(lambda cpx: v3("pQ", cpx, 8, step=2), 4, (("t3", 0),))
+        else:
+            turn(v3("t3", 0, 8), v("f2"))
+            swap(lambda cpx: v3("pQ", cpx, 8, step=2), 4, (("t3", 0), ("t3", 4)))
         for n, part in enumerate(CFG["p1"]):
             lo, hi = 16 * part[0], 16 * part[1]
             r = lambda k: v(k, lo, hi)
@@ -601,6 +693,9 @@ def rank_program(g, core, T, topo):
             else:
                 tt(r("key2"), key, r("pay"), ADD)
                 scan(r("sc2"), C("R2", lo, hi), r("key2"), MIN, MAX)
+            done = sum(b - a for a, b in CFG["p3"][:n + 1])
+            if done % (8 // KH) == 0:
+                flags(part[0] // (8 // KH), done == 8, t)
         dsl, po = v("ds", 15, 128, 16), v("po", 8 * t, 8 * t + 8)
         tt(v("u8"), pt, dsl, SUB)
         tt(v("u8"), v("u8"), v("dv"), MUL)
@@ -611,62 +706,32 @@ def rank_program(g, core, T, topo):
             unpack(v("abf"), po)
             store("sta", T.ya[:], v("abf", 0, 8))
             store("stb", T.yb[:], v("abf", 8, 16))
-        tt(v("k8"), v("sc2", 15, 128, 16), v("dv"), MUL)
-        ts(v("n8"), v("k8"), 2047, AND)
-        cp(v("nl"), v("n8"))
-        cp(v("cg"), ind(v("cot"), v("nl")))
-        rec("P", [lambda: ten.transpose(T.pA[:, 0:128], T.cg[:, 0:128], mf("I")[0])], [v("cg"), mf("I")], [v("pA", 0, 128)], 512 * PCY)
-        tt(v("qb"), ind(v("tabn"), v("nl")), C("lfr"), ADD)
-        tt(v("nb"), C("c2"), v("n8"), SUB)
+        for a, b in CFG["l1"]:
+            tt(cv("qb", a, b, 16), ind(v("tabn"), v("nl", a, b)), C("lfr", 16 * a, 16 * b), ADD)
+            tt(v("nb", a, b), C("c2", a, b), v("n8", a, b), SUB)
         for c in range(8):
             act(v("ab1", 128 * c, 128 * c + 16 * c + 16), v("qb", 0, 16 * c + 16), F.Abs, bias=v("nb", c, c + 1))
         for c in range(8):
             act(v("rl", 128 * c, 128 * c + 16 * c + 16), v("ab1", 128 * c, 128 * c + 16 * c + 16), F.Relu, bias=C("hl", c, c + 1), scale=-2.0 ** 21, acc=v("los", c, c + 1))
-        tt(v("lt"), v("los"), C("cT"), MIN)
-        tt(v("tg"), v("lt"), v("n8"), MAX)
-        cp(v("tg16"), v("tg"))
-        ts(v("j8"), v("k8"), 11, SHR, 15, AND)
-        tt(v("jf"), C("c15"), v("j8"), SUB)
-        cp(v("jl"), v("jf"))
-        ts(v("esel"), ind(v("e"), v("jl")), 128.0 - off, ADD)
         if t in (0, RO - 1):
             for lo in range(PAD + (1024 if last else 0), PAD + 2560, 512):
                 lift(v("X0" if last else "X", lo, lo + 512), v("X" if last else "X0", lo, lo + 512), -128.0 if last else 128.0)
-        scatter(v("X", 0, PAD + 2560 + 128), v("tg16"), v("esel"))
+        for a, b in CFG["l2"]:
+            r = lambda k: v(k, a, b)
+            ts(r("j8"), r("k8"), 11, SHR, 15, AND)
+            tt(r("jf"), C("c15", a, b), r("j8"), SUB)
+            cp(r("jl"), r("jf"))
+            shift(CFG["es"], cv("esel", a, b, 16), ind(v("e"), r("jl")), 128.0 - off)
+        for a, b in CFG["l3"]:
+            r = lambda k: v(k, a, b)
+            tt(r("lt"), r("los"), C("cT", a, b), MIN)
+            tt(r("tg"), r("lt"), r("n8"), MAX)
+            cp(r("tg16"), r("tg"))
+            scatter(v("X", 0, PAD + 2560 + 128), r("tg16"), cv("esel", a, b, 16))
         if last:
             for lo in (PAD, PAD + 512):
                 lift(v("X0", lo, lo + 512), v("X", lo, lo + 512), -128.0)
             store("stx0", T.yx[:, 0:1024], v("X0", PAD, PAD + 1024))
-        sec = lambda k, s: v3(k, 0, NQ, WQ * s, WQ * s + WQ)
-        ts(sec("hi4", 0), v("pA", 0, 128), 1.0 / 32, MUL, HB - 31.0 / 64, ADD)
-        ts(v("hs"), sec("hi4", 0), -32.0, MUL, 32.0 * HB, ADD)
-        tt(sec("lo4", 0), v("pA", 0, 128), v("hs"), ADD)
-        for s in range(1, NQ):
-            if CFG["hc"] == "S":
-                act(sec("hi4", s), sec("hi4", 0), F.Identity, bias=-float(s))
-            else:
-                ts(sec("hi4", s), sec("hi4", 0), -float(s), ADD)
-            ts(sec("lo4", s), sec("lo4", 0), -float(s), ADD)
-        for s in range(NQ):
-            for h in range(HR):
-                o, x = v("ohh", HW * s + 128 * h, HW * s + 128 * h + 128), HB + 32.0 + NQ * h
-                if h < HV:
-                    ts(o, v3("hi4", s, s + 1), x, A.is_equal)
-                else:
-                    act(o, v3("hi4", s, s + 1), F.Sign, bias=0.5 - x)
-            for h in range(LR):
-                ts(v("ohl", 128 * (LR * s + h), 128 * (LR * s + h) + 128), v3("lo4", s, s + 1), float(NQ * h), A.is_equal)
-            for pp in range(WQ // 32):
-                pr = s * (WQ // 32) + pp
-                o, fq = v(CFG["fb"][pr], 0, 64, 1, (0, 98)), v("Fq", 64 * pr, 64 * pr + 64, 1, (0, 98))
-                mms(o, [(v("ohh", HW * s + 16 * pp + k, HW * s + HW, WQ // 2), v("ohl", 128 * LR * s + 16 * pp + k, 128 * LR * (s + 1), WQ // 2)) for k in range(16)])
-                cp(fq, o)
-                for Q in range(2):
-                    gi = s * (8 // NQ) + pp + Q * (WQ // 32)
-                    pairs = [(v("Fq", 64 * pr + Q, 64 * pr + 64, 2, (0, 98)), v("Eh", 48 * Q, 48 * Q + 48, 1, (0, 98)))]
-                    if t:
-                        pairs = [(v("mb", MB["U"] + 256 * b + 32 * gi, MB["U"] + 256 * b + 32 * gi + 32), v("old", b, 96, 2)) for b in range(2)] + pairs
-                    mms(v("pU", 48 * (gi // 4), 48 * (gi // 4) + 48, 1, (32 * (gi % 4), 32 * (gi % 4) + 32)), pairs)
         if not last:
             spread(t + 1)
             cn = v("pD0", 0, 8)
@@ -678,40 +743,43 @@ def rank_program(g, core, T, topo):
             act(v("Fl"), v("pU", 0, 96), F.Sign)
         else:
             ts(v("Fl"), v("pU", 0, 96), 0.0, A.is_gt)
+        mms(v("pA", 96, 108), [(mb("Z"), mb("I", 12))])
         for mi, pb in (("O", "pA"), ("T", "pB")) + ((("C", "pC"),) if not last else ()):
+            if mi == "C":
+                mms(v(pb, 0, 96), [(mb("Z"), mb("I", 96))], True, False)
             for b in range(2):
-                mms(v(pb, b, 96, 2), [(mb(mi + str(2 * Q + b)), v("Fl", 48 * Q, 48 * Q + 48)) for Q in range(2)])
-        scan(v("Sx"), v("pA", 0, 96), mb("c240", 96), ADD, MIN)
-        tt(v("P2", 0, 96), v("Sx"), v("pB", 0, 96), ADD)
-        ts(v("iv"), C("jl"), v("Sx", 95, 96), A.is_ge)
-        tt(v("iv"), v("iv"), C("jT"), MUL)
+                mms(v(pb, b, 96, 2), [(mb(mi + str(2 * Q + b)), v("Fl", 48 * Q, 48 * Q + 48)) for Q in range(2)], mi != "C", mi != "C")
+        Sx = v("Sx", 12, 108)
+        scan(v("Sx", 12, 120), v("pA", 0, 108), mb("c240", 108), ADD, MIN)
+        tt(v("P2", 0, 96), Sx, v("pB", 0, 96), ADD)
         for n, (c0, c1) in enumerate(CFG["pre"]):
             mine = [c for c in range(c0, c1) if c in SV]
             rest = [c for c in range(c0, c1) if c not in SV]
             assert all(x[-1] - x[0] < len(x) for x in (mine, rest) if x)
             if rest:
                 for c in rest:
-                    act(v("sg", 96 * c, 96 * c + 96), v("Sx"), F.Sign, bias=C("bj", c, c + 1), scale=-1.0, acc=v("xa", c, c + 1))
+                    act(v("sg", 120 * c, 120 * c + 98 + 2 * c), v("Sx", 11 - c, 109 + c), F.Sign, bias=C("bj", c, c + 1), scale=-1.0, acc=v("xa", c, c + 1))
                 a, b = rest[0], rest[-1] + 1
                 ts(v("xl", a, b), v("xa", a, b), 0.5, MUL, 48.0, ADD)
                 act(v("xb", a, b), v("xa", a, b), F.Identity, bias=48.0, scale=0.5)
             if mine:
                 for c in mine:
-                    ts(v("sg", 96 * c, 96 * c + 96), v("Sx"), C("bj", c, c + 1), A.is_lt)
+                    ts(v("sq", 108 * c, 108 * c + 97 + c), v("Sx", 12, 109 + c), C("bj", c, c + 1), A.is_lt)
                 a, b = mine[0], mine[-1] + 1
-                scan(v("sv", 96 * a, 96 * b), v("rv", 0, 96 * (b - a)), v("sg", 96 * a, 96 * b), MUL, ADD)
-                cp(v("xl", a, b), v("sv", 96 * a + 95, 96 * b, 96))
-                act(v("xb", a, b), v("sv", 96 * a + 95, 96 * b, 96))
+                scan(v("sv", 108 * a, 108 * b), v("rv", 0, 108 * (b - a)), v("sq", 108 * a, 108 * b), MUL, ADD)
+                cp(v("xl", a, b), v("sv", 108 * a + 107, 108 * b, 108))
+                act(v("xb", a, b), v("sv", 108 * a + 107, 108 * b, 108))
             pn = v(CFG["nb"][n % 3], c0, c1)
             tt(v("cm", 16 * c0, 16 * c1), ind(v("P2"), v("xl", c0, c1)), v("jr", 16 * c0, 16 * c1), A.is_le)
-            mms(pn, [(mb("I16"), v("xb", c0, c1))] + [(slide("B1", m), v("cm", 16 * c0 + m, 16 * c1, 16)) for m in range(16)])
+            mms(pn, [(mb("I16"), v("xb", c0, c1))], True, False)
+            mms(pn, [(slide("B1", m), v("cm", 16 * c0 + m, 16 * c1, 16)) for m in range(16)], False, True)
             ts(v("no16", c0, c1), pn, 1024.0, ADD)
             cp(v("s4", 16 * c0, 16 * c1), ind(sut, v("no16", c0, c1)))
-            tt(v("vl", c0, c1), pn, v("iv", c0, c1), MAX)
-        cp(v("vl16"), v("vl"))
         if not last:
-            ts(v("g2"), v("P2", 0, 96), 192.0, A.is_gt)
-            tt(v("old"), v("pC", 0, 96), v("g2"), MUL)
+            mms(v("pC", 0, 96), [(mb("I"), Sx)], False, True)
+            act(v("old"), v("pC", 0, 96), F.Relu, bias=-448.5)
+        else:
+            ts(v("vl16"), v("no16"), -1024.0, ADD)
         for c0, c1, e in CFG["rc"]:
             o, a = v("R", 256 * c0, 256 * c1), ind(XH, v("s4", 16 * c0, 16 * c1))
             if e == "S":
@@ -725,7 +793,7 @@ def rank_program(g, core, T, topo):
         for c0, c1 in CFG["sc"]:
             a, b = v("mx", 256 * c0 + 15, 256 * c1, 16), v("mn", 256 * c0 + 15, 256 * c1, 16)
             if not last:
-                scatter(v("X", PAD + 1024, XW), v("vl16", c0, c1), a, b)
+                scatter(v("X", PAD, XW), v("no16", c0, c1), a, b)
             else:
                 tt(v("vb", 16 * c0, 16 * c1), a, b, ADD)
                 scatter(v("X0", PAD + 1024, XW), v("vl16", c0, c1), v("vb", 16 * c0, 16 * c1), v("m128", 16 * c0, 16 * c1))

@@ -1,3 +1,4 @@
+import math
 from concourse.mybir import dt, AluOpType as A, AxisListType, ActivationFunctionType as F
 
 PAD = 16
@@ -15,7 +16,7 @@ CFG = {
     "rc": ((0, 3, "V"), (3, 8, "S"), (8, 12, "S")),
     "vi": "S",
     "sc": ((0, 12),),
-    "look": 0.0, "wake": 0.2, "idle": 1.0, "fit": 0.0, "passes": 6, "inorder": "", "tries": 0, "frac": 30, "amp": 1.0,
+    "look": 0.0, "wake": 0.2, "idle": 1.0, "fit": 0.0, "passes": 6, "inorder": "", "xs": 0, "polish": 12000, "ld": (2.0, 0.0012, 1.5), "ahead": {}, "tries": 0, "frac": 30, "amp": 1.0,
 }
 CFG.update({'passes': 3, 'look': 0.1, 'f2': 'ASAAAaSS', 'z2': 'PPvVPVRP', 'z1': 'PPVVVVvV', 'f1': 'aASSSSSS', "lift": "S", 'sc': ((0, 8), (8, 12)),
             'rc': ((0, 2, 'S'), (2, 4, 'V'), (4, 8, 'S'), (8, 11, 'S'), (11, 12, 'S')), 'pre': ((0, 4), (4, 8), (8, 12)), 'sv': (0, 1, 2, 3), 'hc': 'S', 'fq': 'S',
@@ -23,38 +24,43 @@ CFG.update({'passes': 3, 'look': 0.1, 'f2': 'ASAAAaSS', 'z2': 'PPvVPVRP', 'z1': 
 CFG.update({'hs': 6, 'hc': 'VVVVVVV', 'kh': 2, 'es': 'V', 'g2': 'V', 'fq': 'S', 'lift': 'V', 'sv': (10, 11), 'pre': ((0, 4), (4, 8), (8, 12)), 'rc': ((0, 2, 'S'), (2, 4, 'S'), (4, 6, 'V'), (6, 8, 'S'), (8, 10, 'S'), (10, 11, 'S'), (11, 12, 'S')), 'sc': ((0, 6), (6, 12)), 'look': 0.1, 'z1': 'vPVVVVvV', 'z2': 'PPvVPVRP', 'f1': 'aSSSSSSS', 'f2': 'ASAAAaSS'})
 CFG.update({'rem': 8.0, 'cof': 1, 'pk': 1, 'l1': ((0, 8),), 'l2': ((0, 8),), 'l3': ((0, 8),), 'passes': 3, 'hs': 6, 'hc': 'SSSSSSS', 'fq': 'V', 'lift': 'S', 'es': 'V', 'g2': 'S', 'idle': 3, 'fit': 0.05, 'sv': (2, 3), 'pre': ((0, 4), (4, 8), (8, 12)), 'rc': ((0, 2, 'S'), (2, 4, 'V'), (4, 8, 'S'), (8, 11, 'S'), (11, 12, 'S')), 'sc': ((0, 6), (6, 12)), 'look': 0.15, 'p1': ((4, 8), (2, 4), (0, 2)), 'p2': ((4, 8), (2, 4), (0, 2)), 'p3': ((4, 8), (0, 4)), 'z1': 'RRpVvVVV', 'z2': 'vPVpppRV', 'f1': 'aSaaSSSa', 'f2': 'AaaSaAsA'})
 CFG.update({'hs': 6, 'hc': 'SSSSSSS', 'fq': 'V', 'lift': 'S', 'es': 'S', 'l1': ((0, 4), (4, 8)), 'l2': ((0, 8),), 'l3': ((0, 4), (4, 8)), 'cof': 1, 'pk': 1, 'idle': 6, 'fit': 0.05, 'sv': (2, 3), 'pre': ((0, 4), (4, 8), (8, 12)), 'rc': ((0, 2, 'S'), (2, 4, 'V'), (4, 6, 'S'), (6, 8, 'S'), (8, 10, 'S'), (10, 11, 'S'), (11, 12, 'V')), 'sc': ((0, 6), (6, 12)), 'look': 0.15, 'p1': ((0, 4), (4, 6), (6, 8)), 'p2': ((0, 4), (4, 8)), 'p3': ((0, 4), (4, 8)), 'z1': 'PPPvVpRR', 'z2': 'vRppPvpv', 'f1': 'aASVaaSa', 'f2': 'aASSasAa'})
+CFG.update({'hs': 6, 'hc': 'SSSSSSS', 'fq': 'V', 'lift': 'V', 'es': 'S', 'l1': ((0, 4), (4, 8)), 'l2': ((0, 8),), 'l3': ((0, 4), (4, 8)), 'idle': 6, 'fit': 0.05, 'sv': (), 'pre': ((0, 4), (4, 8), (8, 12)), 'rc': ((0, 2, 'S'), (2, 3, 'S'), (3, 4, 'V'), (4, 6, 'S'), (6, 8, 'S'), (8, 10, 'S'), (10, 11, 'S'), (11, 12, 'V')), 'sc': ((0, 6), (6, 12)), 'look': 0.2, 'p1': ((0, 4), (4, 6), (6, 8)), 'p2': ((0, 4), (4, 6), (6, 8)), 'p3': ((0, 4), (4, 8)), 'z1': 'VVVVVVVV', 'z2': 'RRpVvpvR', 'f1': 'SSSSSSSS', 'f2': 'SSAAsAsa'})
+CFG.update({'fit': 0, 'sv': (2, 3, 4, 5), 'pre': ((0, 2), (2, 4), (4, 8), (8, 12)), 'rc': ((0, 2, 'S'), (2, 4, 'S'), (4, 6, 'V'), (6, 8, 'S'), (8, 10, 'S'), (10, 11, 'S'), (11, 12, 'S')), 'sc': ((0, 6), (6, 12)), 'look': 0.1, 'p1': ((0, 4), (4, 6), (6, 8)), 'p2': ((0, 4), (4, 6), (6, 8)), 'p3': ((0, 2), (2, 4), (4, 8)), 'z1': 'VVVVVVVV', 'z2': 'RRpVVPvR', 'f1': 'SSSSSSSS', 'f2': 'SSAaSASa'})
+CFG.update({'hs': 6, 'hc': 'SSSSSSS', 'fq': 'S', 'lift': 'V', 'es': 'S', 'l1': ((0, 4), (4, 8)), 'l2': ((0, 8),), 'l3': ((0, 8),), 'idle': 6, 'fit': 0.03, 'sv': (10, 11), 'pre': ((0, 2), (2, 4), (4, 8), (8, 12)), 'rc': ((0, 2, 'S'), (2, 4, 'S'), (4, 6, 'V'), (6, 8, 'S'), (8, 10, 'S'), (10, 11, 'S'), (11, 12, 'S')), 'sc': ((0, 8), (8, 12)), 'look': 0.15, 'p1': ((0, 4), (4, 6), (6, 8)), 'p2': ((0, 4), (4, 6), (6, 8)), 'p3': ((0, 4), (4, 6), (6, 8)), 'z1': 'VVVVvVVV', 'z2': 'PRVvVRvP', 'f1': 'SSSSSSSS', 'f2': 'TaATaaTa', 'um': 'SSVV', 'nf1': 1, 'hc': 'SSSS'})
+CFG.update({'hs': 5, 'hc': 'VSSS', 'fq': 'S', 'lift': 'S', 'es': 'S', 'um': 'SVSV', 'nf1': 1, 'rem': 8.0, 'sv': (2, 3), 'z1': 'VVVVvVVV', 'z2': 'pRVvVRvp', 'f1': 'SSSSSSSS', 'f2': 'TaATaATa'})
+CFG.update({'hs': 6, 'hc': 'VSSS', 'fq': 'S', 'lift': 'V', 'l2': ((0, 4), (4, 8)), 'nf1': 0, 'z1': 'VVVVvVvV', 'z2': 'prVvVRVp', 'f1': 'SSSSSSSS', 'f2': 'tabtaATa'})
 
 _B, _F, _I, _U, _H = "bfloat16", "float32", "int32", "uint16", "float16"
 _S = {
     "X": (XW, _B), "X0": (XW, _B), "cot": (PAD + 2560, _I), "sut": (XW - PAD, _I), "dls": (512, _B), "dx0": (2048, _B), "dx1": (2048, _B),
     "ab16": (64, _U), "pt": (32, _I), "po": (32, _I), "abi": (16, _I), "lab": (16, _I), "wtc": (1, _B), "thi": (1, _I),
-    "dfk": (256, _U), "f2": (256, _F), "xf": (2048, _B), "xn": (2048, _B), "z": (2048, _B), "z2": (2048, _B), "e1": (2048, _B), "e": (2048, _B),
+    "dfk": (256, _U), "f2": (256, _H), "xf": (2048, _B), "xn": (2048, _B), "z": (2048, _B), "z2": (2048, _B), "e1": (2048, _B), "e": (2048, _B),
     "sc": (128, _F), "gp": (128, _F), "qq": (128, _F), "ds": (128, _F),
-    "key2": (128, _F), "sc2": (128, _F), "d16": (16, _U), "sj": (128, _U), "ui": (128, _I), "uv": (128, _I), "w2": (128, _F), "nn": (128, _I),
+    "key2": (128, _F), "sc2": (128, _F), "d16": (16, _U), "sj": (128, _U), "ui": (128, _I), "uv": (128, _I), "w2": (128, _F), "uy": (128, _B), "us": (128, _F), "nn": (128, _I),
     "ni": (128, _I), "n16": (128, _U), "pay": (128, _F),
     "k8": (8, _I), "n8": (8, _I), "j8": (8, _I), "nl": (8, _U), "jf": (8, _F), "jl": (8, _U),
-    "qb": (128, _F), "nb": (8, _F), "cg": (128, _F), "esel": (128, _B), "tabn": (1040, _F),
+    "qb": (128, _F), "nb": (8, _F), "cg": (128, _H), "mh": (1536, _H), "esel": (128, _B), "tabn": (1040, _F),
     "hs": (128, _B), "ohl": (4096, _B), "ohh": (6400, _B),
     "ab1": (1024, _F), "rl": (1024, _F), "los": (8, _F), "lt": (8, _F), "tg": (8, _F), "tg16": (8, _U),
     "Fq": (256, _H), "Eh": (96, _H), "Fl": (96, _B), "Sx": (120, _B), "P2": (112, _B), "sg": (1440, _B), "sq": (1296, _B), "sv": (1296, _B), "rv": (1296, _B),
     "xa": (12, _F), "xb": (12, _B), "xl": (12, _U),
     "cm": (192, _B), "no16": (12, _U), "s4": (192, _U),
     "R": (3072, _B), "mx": (3072, _B), "mn": (3072, _B), "vb": (192, _B), "m128": (192, _B),
-    "vl16": (12, _U), "old": (96, _B), "cof": (2560, _F),
+    "XS": (4096, _B), "spot": (256, _U), "su1": (256, _I), "su2": (256, _I), "vl16": (12, _U), "old": (96, _B),
     "dv": (8, _B), "u8": (8, _F), "abf": (16, _F), "a8": (8, _F), "az": (1, _F), "ay": (1, _B), "thb": (1, _F), "thv": (1, _F), "th8": (1, _F),
-    "pc": (32, _F), "ci": (160, _I), "cf": (1408, _F), "mf": (1024, _F), "mb": (3872, _B), "rr": (3072, _B), "tmp": (256, _F), "jr": (192, _B),
+    "pc": (40, _F), "ci": (160, _I), "cf": (1408, _F), "mf": (256, _F), "mb": (4512, _B), "rr": (3072, _B), "tmp": (256, _F), "jr": (192, _B),
     "ks": (128, _F), "k4": (192, _F),
 }
 SCRATCH = {k: ("sbuf", [128, n], d) for k, (n, d) in _S.items()}
 for _k in ("a3", "b3", "da", "db"):
     SCRATCH[_k] = ("sbuf", [128, 8, 256], _B)
-SCRATCH["t3"] = ("sbuf", [128, 8, 32], _F)
-SCRATCH["t4"] = ("sbuf", [128, 4, 32], _F)
-SCRATCH["k3"] = ("sbuf", [128, 16, 16], _B)
+SCRATCH["t3"] = ("sbuf", [128, 8, 32], _H)
+SCRATCH["t4"] = ("sbuf", [128, 4, 32], _H)
+SCRATCH["k3"] = ("sbuf", [128, 20, 16], _B)
 SCRATCH["hi4"] = ("sbuf", [128, 4, 128], _B)
 SCRATCH["lo4"] = ("sbuf", [128, 4, 128], _B)
 PSUM = ("pA", "pB", "pC", "pE", "pU", "pD0", "pD1", "pQ")
-SCRATCH["nf"] = ("sbuf", [128, 4, 32], _F)
+SCRATCH["nf"] = ("sbuf", [128, 4, 32], _H)
 for _k in PSUM[:7]:
     SCRATCH[_k] = ("psum", [128, 512], _F)
 for _k in PSUM[7:]:
@@ -65,6 +71,58 @@ STORES = ["stx0", "stx1", "sta", "stb"]
 SEMAPHORES = ["sV", "sS", "sP", "sG", "loc", "ab1a", "ab2a", "ab3a", "dl1a", "dl2a", "dl3a"] + LOADS + STORES
 CY, PCY, GAT, SCT = 0.00091, 0.00046, 1.56, 3.8
 ORDER = []
+
+
+def polish(ops, succ, before, order, tries):
+    eng, seed = [o[0] for o in ops], [1]
+
+    def chance():
+        seed[0] = (seed[0] * 1103515245 + 12345) % 2147483648
+        return seed[0] / 2147483648
+
+    def times(order):
+        end, why, free, last = [0.0] * len(ops), [None] * len(ops), {}, {}
+        for i in order:
+            t, w = free.get(eng[i], 0.0), (last.get(eng[i]), True)
+            for j, x in before[i]:
+                if end[j] + x > t + 1e-9:
+                    t, w = end[j] + x, (j, False)
+            end[i], why[i], free[eng[i]], last[eng[i]] = t + ops[i][3], w, t + (ops[i][3] if ops[i][4] is None else 0.1), i
+        return max(end), end, why
+
+    def moved(seg, nxt):
+        along, queues = {seg[-1]}, set()
+        for i in seg[-2::-1]:
+            if eng[i] in queues or any(j in along for j, w in nxt[i]):
+                if eng[i] == eng[seg[-1]]:
+                    return None
+                along.add(i)
+                queues.add(eng[i])
+        return [i for i in seg if i in along] + [i for i in seg if i not in along]
+
+    now = times(order)
+    best = (now[0], order)
+    while tries > 0:
+        chain = [now[1].index(now[0])]
+        while now[2][chain[-1]][0] is not None:
+            chain.append(now[2][chain[-1]][0])
+        queued = [now[2][i][1] and eng[i] != "Y" and j >= len(LOADS) for i, j in zip(chain, chain[1:])] + [False]
+        spots = [k for k, x in enumerate(queued) if x]
+        place = {i: x for x, i in enumerate(order)}
+        for _ in range(30):
+            k, d = spots[int(chance() * len(spots))], 1
+            while chance() < 0.5 and queued[k + d]:
+                d += 1
+            a, b = place[chain[k + d]], place[chain[k]] + 1
+            seg = moved(order[a:b], succ) if chance() < 0.5 else (moved(order[a:b][::-1], before) or [])[::-1]
+            tries -= 1
+            if seg:
+                new = times(order[:a] + seg + order[b:])
+                if new[0] < now[0] or chance() < 0.5 * math.exp((now[0] - new[0]) / 0.02):
+                    order, now = order[:a] + seg + order[b:], new
+                    best = min(best, (now[0], order), key=lambda x: x[0])
+                    break
+    return best
 
 
 def rank_program(g, core, T, topo):
@@ -214,12 +272,14 @@ def rank_program(g, core, T, topo):
             for i in range(n - 1, -1, -1):
                 prio[i] = ops[i][3] + max([prio[j] + w for j, w in succ[i]] + [0.0])
             best = None
+            ahead = [CFG["ahead"].get(([a[0] for a in op[2] if a[4]] + [""])[0], 0.0) for op in ops]
             for _ in range(CFG["passes"]):
-                order, end = plan(succ, before, prio)
+                order, end = plan(succ, before, [x + y for x, y in zip(prio, ahead)])
                 if best is None or max(end) < best[0]:
                     best = (max(end), order)
                     keep = prio
                 prio = plan(before, succ, end)[1]
+            best = polish(ops, succ, before, best[1], CFG["polish"]) if CFG["polish"] else best
             if "hook" in CFG:
                 best = CFG["hook"](ops, marks, plan, succ, before, keep, best)
             ORDER.extend(best[1])
@@ -300,7 +360,7 @@ def rank_program(g, core, T, topo):
         rec("G", [lambda: g.affine_select(o[0], a[0], [[0, a[2]]], A.is_ge, 0.0, 0, 0)], [a] + list(after), [o], 0.17 + 2 * CY * o[2])
 
     def load(eng, name, o, src, after=(), more=0.0):
-        rec(eng, [lambda: que[eng].dma_start(o[0], src[:])], list(after), [o], 3.0 + o[2] * 0.0015 + more, name)
+        rec(eng, [lambda: que[eng].dma_start(o[0], src[:])], list(after), [o], CFG["ld"][0] + o[2] * CFG["ld"][1] + more, name)
 
     def store(name, dst, a):
         rec("Y", [lambda: g.sync.dma_start(dst, a[0])], [a], [], 3.0, name)
@@ -331,7 +391,7 @@ def rank_program(g, core, T, topo):
     load("S", "lddl", v("dls", 0, 128), T.dl)
     load("S", "ldth", (T.thi[0:8, 0:1], [("thi", 0, 1, True)], 1), T.th)
     load("S", "ldwt", v("wtc"), T.wt)
-    load("S", "ldx", v("X0", PAD, PAD + 2560), T.x0, more=2.0)
+    load("S", "ldx", v("X0", PAD, PAD + 2560), T.x0, more=CFG["ld"][2])
     load("Y", "ldsu", v("sut", 0, 2560), T.su, [cot])
     landed = {}
     for s in range(1, RO):
@@ -385,24 +445,31 @@ def rank_program(g, core, T, topo):
     tt(P(9), P(0), P(2), SUB)
     ts(P(10), P(9), 15.0, ADD)
     MB, nb_ = {}, 0
-    for k, n in ([(k, 144) for k in ("B1", "K1", "nK1", "K2", "nK2", "W")] + [(k, 128) for k in ("I16", "I", "nI", "Z", "ON")] + [("U", 512), ("c240", 112)]
+    for k, n in ([(k, 144) for k in ("B1", "K1", "nK1", "K2", "nK2", "W")] + [(k, 128) for k in ("I16", "I32", "I", "nI", "Z", "ON")] + [("U", 512), ("SH", 512), ("c240", 112)]
                  + [(k + str(b), 128) for k in "TOC" for b in range(4)]):
         MB[k], nb_ = nb_, nb_ + n
     mb = lambda k, n=128: v("mb", MB[k], MB[k] + n)
     slide = lambda k, m: v("mb", MB[k] + 15 - m, MB[k] + 143 - m)
-    MF = {"I": 0, "SL": 128, "E8": 384, "SW00": 512, "SW01": 640, "SW10": 768, "SW11": 896}
+    MF = {"I": 0, "E8": 128}
+    sw = lambda cpx, gp, w: cv("mh", 2 * cpx + gp, 2 * cpx + gp + 1, 128, w)
+    cv = lambda name, a, b, w=256, o=0: v(name, o + w * a, o + w * b)
     mf = lambda k: v("mf", MF[k], MF[k] + 128)
     U1, U2 = 2.0 ** 28, 2.0 ** 15
     ts(mb("B1", 144), col(144), P(10), A.is_equal)
     act(mb("K1", 144), mb("B1", 144), scale=U1)
     act(v3("k3", 0, 8), C("kc"), scale=U1 / 16)
-    ms(v3("k3", 8, 16), -2.0 ** 24)
+    ts(v("ks"), C("kc"), -32.0, MUL, 480.0, ADD)
+    ts(P(22), P(4), -2.0 ** 18, MUL)
+    ts(v3("k3", 8, 16), v("ks"), P(5), MUL, P(22), ADD)
+    ts(P(28), P(4), 65520.0, MUL, 16.0, ADD)
+    ts(v3("k3", 16, 20), C("kc", 0, 64), 0.0, MUL, P(28), ADD)
     ts(cf("R1", 128), C("kc"), 0.0, A.is_equal, 2.0 ** 45, MUL)
     ts(mf("I"), col(128), P(0), A.is_equal)
     for cpx in range(2):
         for gp in range(2):
             ts(P(11 + 2 * cpx + gp), P(0), 16.0 * (gp - cpx), ADD)
-            ts(mf("SW%d%d" % (cpx, gp)), col(128), P(11 + 2 * cpx + gp), A.is_equal, P(4 + cpx), MUL)
+            ts(sw(cpx, gp, 0), col(128), P(11 + 2 * cpx + gp), A.is_equal, P(4 + cpx), MUL)
+    ts(v("mh", 512, 1024), v("mh", 0, 512), 4096.0, MUL)
     act(mb("I"), mf("I"))
     act(mb("nI"), mf("I"), scale=-1.0)
     act(mb("nK1", 144), mb("B1", 144), scale=-U1)
@@ -415,7 +482,6 @@ def rank_program(g, core, T, topo):
     ts(v("thv"), v("thb"), U1, MUL)
     ts(P(20), v("thb"), 10240.0, ADD, U1 / 8, MUL)
     ts(P(21), v("thb"), -1.0 / 64, MUL, -63.0 / 128, ADD)
-    ts(P(22), P(2), -2048.0, MUL, 15.0 * 2048 + PAD, ADD)
     ts(cf("R2", 128), C("kc"), 0.0, A.is_gt, 2.0 ** 26, MUL)
     ts(C("R2"), C("R2"), -2.0 ** 25, ADD)
     act(mb("K2", 144), mb("B1", 144), scale=U2)
@@ -426,7 +492,12 @@ def rank_program(g, core, T, topo):
         ts(P(24), P(2), 7.5, A.is_gt, 56.0, MUL)
         ts(P(25), P(1), 8.0, MUL, P(2), ADD)
         tt(P(24), P(24), P(25), ADD)
-        ts(mf("SL"), col(128), P(24), A.is_equal)
+    iota(v("ab1", 0, 512), [[32, 4], [0, 4], [1, 32]], 0, 0, **SM)
+    ts(v("mh", 1024, 1536), v("ab1", 0, 512), P(24), A.is_equal)
+    iota(v("rl", 0, 256), [[0, 2], [1, 4], [0, 32]], 0, 0, **SM)
+    act(mb("SH", 256), v("rl", 0, 256), scale=-32.0 / 128)
+    act(v("mb", MB["SH"] + 256, MB["SH"] + 512), v("rl", 0, 256), scale=-33.0 / 128)
+    act(mb("I32"), mf("I"), scale=-32.0)
     ts(cf("lf", 8), col(8), 16.0, MUL, P(2), ADD)
     ts(cf("cT", 8), C("lf"), PAD + 2560.0, ADD)
     ts(cf("c15", 8), C("lf"), 16.0, MUL, 15.0, ADD)
@@ -434,7 +505,9 @@ def rank_program(g, core, T, topo):
     ts(cf("c2", 8), C("lf"), -1.0 / 256, MUL, 1.0 / 256, ADD)
     act(cf("lfr", 128), col(128), scale=1.0 / 128)
     act(mb("I16"), mf("I"), scale=16.0)
-    ts(v("ks"), C("kc"), P(2), A.is_lt, -1.0, MUL)
+    ts(v("ks"), C("kc"), P(2), A.is_ge, 100.0, MUL)
+    tt(v("ks"), v("ks"), C("c4"), ADD)
+    ts(v("pc", 32, 34), v("pc", 4, 6), -1.0, MUL)
     ts(P(18), P(3), 16.0, MUL, P(2), ADD)
     ts(P(19), P(18), 64.0, ADD)
     ts(v("pc", 26, 28), v("pc", 4, 6), 256.0, MUL)
@@ -443,8 +516,7 @@ def rank_program(g, core, T, topo):
             i = str(2 * Q + b)
             ts(mb("O" + i), C("c4"), P(6 if Q else 3), A.is_equal, P(4 + b), MUL)
             ts(mb("C" + i), col(128), P(18 + Q), A.is_equal, P(26 + b), MUL)
-            tt(mb("T" + i), mb("O" + i), v("ks"), MUL)
-            tt(mb("C" + i), mb("C" + i), mb("T" + i), ADD)
+            ts(mb("T" + i), v("ks"), P(6 if Q else 3), A.is_equal, v("pc", 32 + b, 33 + b), MUL)
     ts(P(16), P(1), 32.0, MUL, P(2), ADD)
     ts(P(17), P(16), 16.0, ADD)
     for b in range(2):
@@ -464,6 +536,15 @@ def rank_program(g, core, T, topo):
     ms(v("m128"), -128.0)
     mms(v("pU", 0, 1), [(slide("W", j), v("m128", 0, 1)) for j in range(16)])
     cp(P(23), v("pU", 0, 1))
+    if CFG["xs"]:
+        ts(v("su1"), col(256), 16.0, MUL, P(2), ADD)
+        ts(v("ab1", 512, 768), v("su1"), 1184.0, ADD)
+        tt(v("su2"), v("ab1", 512, 768), v("su1"), MUL)
+        ts(v("su1"), v("su2"), 5, SHR, 1023, AND)
+        cp(v("spot"), v("su1"))
+    UB = 160.0 * 4096
+    ts(P(29), P(23), UB - 2048, ADD)
+    ts(P(30), P(23), UB + 592, ADD)
     ts(cf("jl", 12), col(12), 16.0, MUL, P(2), ADD)
     ts(cf("bj", 12), C("jl"), 0.5, ADD)
     ms(v("P2", 96, 112), 0.0)
@@ -478,8 +559,7 @@ def rank_program(g, core, T, topo):
         for n, m in ((128, 128), (256, 256), (512, 512), (1024, 512)):
             act(v("rr", x + n, x + n + m), v("rr", x, x + m))
 
-    cv = lambda name, a, b, w=256, o=0: v(name, o + w * a, o + w * b)
-    shifts = lambda dx, a, b: (cv(dx, a, b)[0], [(dx, 0, 16, False)], 256 * (b - a))
+    shifts = lambda dx, a, b: (cv(dx, a, b, 128)[0], [(dx, 0, 16, False)], 128 * (b - a))
     bank = lambda a, b: v(BANK[a // 2], 256 * (a % 2), 256 * (a % 2 + b - a))
 
     def runs(part, how, kinds):
@@ -489,10 +569,10 @@ def rank_program(g, core, T, topo):
             out += [x + (how[x[0]].upper(),) for x in two if how[x[0]].upper() in kinds]
         return out
 
-    def swap(out, nblk, srcs, start=True, stop=True):
+    def swap(out, nblk, srcs, start=True, stop=True, more=()):
         for cpx in range(2):
             mms(out(cpx),
-                [(mf("SW%d%d" % (cpx, gp)), v3(t, a0, a0 + nblk, 16 * gp, 16 * gp + 16)) for t, a0 in srcs for gp in range(2)], start, stop, True)
+                list(more) + [(sw(cpx, gp, w), v3(t, a0, a0 + nblk, 16 * gp, 16 * gp + 16)) for t, a0, w in srcs for gp in range(2)], start, stop)
 
     def distance(pd, part, w, ab, db, how):
         p0, p1 = part
@@ -508,29 +588,31 @@ def rank_program(g, core, T, topo):
         mms(o, [then], False, True)
 
     def shifted(o, z, lists, dx, part, how):
-        for a, b, h in runs(part, how, "PRV"):
-            if h == "V":
-                tt(cv(z, a, b), ind(X, cv(lists, a, b, 16)), shifts(dx, a, b), ADD)
+        for a, b, h in runs(part, how, "PRVW"):
+            if h in "VW":
+                for x, y in ([(2 * a, 2 * b)] if h == "V" else [(x, x + 1) for x in range(2 * a, 2 * b)]):
+                    tt(cv(z, x, y, 128), ind(X, cv(lists, x, y, 8)), shifts(dx, x, y), ADD)
                 ts(cv(o, a, b), cv(z, a, b), off, MAX, off + 63.0, MIN)
                 continue
             act(cv(z, a, b), ind(X, cv(lists, a, b, 16)))
-            two(bank(a, b), (mb("I"), shifts(dx, a, b)), (mb("I"), cv(z, a, b)))
+            two(bank(a, b), (mb("I"), shifts(dx, 2 * a, 2 * b)), (mb("I"), cv(z, a, b)))
             if h == "P":
                 ts(cv(o, a, b), bank(a, b), off, MAX, off + 63.0, MIN)
             else:
                 act(cv(z, a, b), bank(a, b), F.Relu, bias=-off)
                 ts(cv(o, a, b), cv(z, a, b), 63.0, MIN, off, ADD)
 
-    def apart(xb, db, eb, ab, lists, l0, part, how, early):
-        for a, b, h in runs(part, how, "SAV"):
+    def apart(xb, db, eb, ab, lists, l0, part, how, X):
+        for a, b, h in runs(part, how, "STABV"):
             lst = cv(lists, a, b, 16, l0)
-            if h == "S":
+            if h in "ST":
                 act(cv(xb, a, b), ind(X, lst))
                 pair = [(mb("I"), cv(xb, a, b)), (mb("nI"), cv(eb, a, b))]
-                two(bank(a, b), pair[1 - early], pair[early])
+                two(bank(a, b), pair[h == "T"], pair[h == "S"])
                 act(v3(ab, a, b), bank(a, b), F.Abs)
-            elif h == "A":
-                tt(cv(xb, a, b), ind(X, lst), cv(eb, a, b), SUB)
+            elif h in "AB":
+                for x, y in ([(2 * a, 2 * b)] if h == "A" else [(x, x + 1) for x in range(2 * a, 2 * b)]):
+                    tt(cv(xb, x, y, 128), ind(X, cv(lists, x, y, 8, l0)), cv(eb, x, y, 128), SUB)
                 act(v3(ab, a, b), cv(xb, a, b), F.Abs)
             else:
                 for c in range(b - 1, a - 1, -1):
@@ -553,16 +635,20 @@ def rank_program(g, core, T, topo):
         ts(r8("n8"), r8("k8"), 2047, AND)
         cp(r8("nl"), r8("n8"))
         cg, tb = v("cg", l0, l0 + nl), BANK[2 * hf] if final else "pU"
-        cp(cg, ind(v("cot"), r8("nl")))
-        for kh in range(KH):
-            mms(v(tb, 0, nl, 1, (nl * kh, nl * kh + nl)), [(cg, v("mf", MF["SL"] + nl * kh, MF["SL"] + nl * kh + nl) if KH > 1 else mf("I"))], f32=True)
-        sec = lambda k, s: v3(k, s0, s0 + NS, WQ * s, WQ * s + WQ)
-        ts(sec("hi4", 0), v(tb, 0, nl), 1.0 / 32, MUL, HB - 31.0 / 64, ADD)
-        shift(CFG["hc"][0], v("hs", l0, l0 + nl), sec("hi4", 0), 32.0 * HB, -32.0)
-        tt(sec("lo4", 0), v(tb, 0, nl), v("hs", l0, l0 + nl), ADD)
-        for s in range(1, NQ):
-            shift(CFG["hc"][s], sec("hi4", s), sec("hi4", 0), -float(s))
-            shift(CFG["hc"][3 + s], sec("lo4", s), sec("lo4", 0), -float(s))
+        ts(cg, ind(v("cot"), r8("nl")), -1024.0, ADD)
+        half = lambda b, p=(0, 128): v(b, 0, 256, 1, p) if b != "pQ" else (T.pQ[p[0]:p[1], 16:32, :], [("pQ", 256, 512, False)], 256)
+        t2 = BANK[2 * hf + 1] if final else "pQ"
+        for b, x in ((tb, 0), (t2, 256)):
+            mms(half(b), [(mb("ON"), v("mb", MB["SH"] + x, MB["SH"] + x + 256))], True, False)
+            for kh in range(KH):
+                mms(half(b, (nl * kh, nl * kh + nl)), [(cg, cv("mh", kh, kh + 1, 256, 1024))], False, False)
+            if not x:
+                mms(half(b), [(mb("Z"), v("mb", MB["SH"], MB["SH"] + 256))], False, True)
+        hc = CFG["hc"][2 * final:]
+        for s in range(s0, s0 + NS):
+            shift(hc[0], v3("hi4", s, s + 1), v(tb, 128 * (s - s0), 128 * (s - s0) + 128), HB + 32 - 31.0 / 64, 1.0 / 32)
+        mms(half(t2), [(mb("I32"), v3("hi4", s0, s0 + NS))], False, True)
+        shift(hc[1], v3("lo4", s0, s0 + NS), half(t2), 32.0 * (HB + 32))
         FB = BANK[2 * (hf != final):][:2] if KH > 1 else CFG["fb"]
         if not final:
             for b in FB:
@@ -614,36 +700,22 @@ def rank_program(g, core, T, topo):
         last = t == RO - 1
         marks.append(len(ops))
         off = 128.0 if t else 0.0
+        byu = t and CFG["xs"]
         X = XH if t else v("X0", PAD, PAD + 2560)
         ab, pt = v("ab16", 16 * t, 16 * t + 16), v("pt", 8 * t, 8 * t + 8)
         if t:
             unpack(ab, pt, [trip("ab%da" % t)])
-        if t and CFG["cof"]:
-            act(v("f2", 0, 128), ind(v("cof"), v("ab16", 16 * t, 16 * t + 8)), scale=4096.0)
-            act(v("f2", 128, 256), ind(v("cof"), v("ab16", 16 * t + 8, 16 * t + 16)))
-            ts(v("dfk", 0, 128), v("f2", 0, 128), 1.0 / 4096, MUL)
-            cp(v("dfk", 128, 256), v("f2", 128, 256))
-        else:
-            cp(v("dfk"), ind(cot, ab))
-            ts(v("f2", 0, 128), v("dfk", 0, 128), 4096.0, MUL)
-            cp(v("f2", 128, 256), v("dfk", 128, 256))
-        if t == 0 and CFG["cof"]:
-            for lo in range(0, 2560, 320):
-                cp(v("cof", lo, lo + 320), v("cot", PAD + lo, PAD + lo + 320))
-        if CFG["pk"]:
-            mms(v3("pQ", 24, 32), [(mf("I"), v("f2", 0, 128)), (mf("I"), v("f2", 128, 256))], f32=True)
-            turn(v3("t3", 0, 4), v3("pQ", 24, 32))
-            swap(lambda cpx: v3("pQ", cpx, 8, step=2), 4, (("t3", 0),))
-        else:
-            turn(v3("t3", 0, 8), v("f2"))
-            swap(lambda cpx: v3("pQ", cpx, 8, step=2), 4, (("t3", 0), ("t3", 4)))
+        cp(v("dfk"), ind(cot, ab))
+        ts(v("f2"), v("dfk"), -1024.0, ADD)
+        turn(v3("t3", 0, 8), v("f2"))
+        swap(lambda cpx: v3("pQ", cpx, 8, step=2), 4, (("t3", 0, 512), ("t3", 4, 0)), more=[(mb("ON"), v3("k3", 16, 20))])
         for n, part in enumerate(CFG["p1"]):
             lo, hi = 16 * part[0], 16 * part[1]
             r = lambda k: v(k, lo, hi)
             pd = "pD%d" % (n % 2)
             key = v(pd, 0, hi - lo)
             shifted("e1", "z", "dfk", dx, part, CFG["z1"])
-            apart("xf", "da", "e1", "a3", "dfk", 128, part, CFG["f1"], 1)
+            apart("xf", "da", "e1", "a3", "dfk", 128, part, CFG["f1"], X)
             mms(key, [(mb("I"), v3("k3", 0, part[1] - part[0]))], True, False)
             distance(pd, part, "K1", "a3", "da", CFG["f1"])
             scan(r("sc"), C("R1", lo, hi), key, MAX, MIN)
@@ -658,35 +730,48 @@ def rank_program(g, core, T, topo):
             pu = v3("pQ", 8, 8 + part[1] - part[0]) if n % 2 else v("pU", 0, hi - lo)
             shifted("e", "z2", "sj", dx, part, CFG["z2"])
             mms(pu, [(slide("W", j), v("e", 16 * lo + j, 16 * hi, 16)) for j in range(16)])
-            if t:
-                ts(r("ui"), pu, P(23), ADD)
+            if CFG["um"][n] == "S" and not byu:
+                act(r("uy"), pu, F.Identity, bias=P(29) if t else UB - 2048)
+                tt(r("w2"), pu, r("uy"), SUB)
+                act(r("us"), r("w2"), F.Square, bias=P(30) if t else UB + 592)
+                ts(r("nn"), r("us"), 1.0 / 32, MUL, 312 - 13.0 / 32, ADD)
+                ts(r("ni"), r("nn"), 1023, AND)
             else:
-                cp(r("ui"), pu)
-            ts(r("uv"), r("ui"), 4095, AND)
-            ts(r("w2"), r("uv"), 1184.0, ADD)
-            tt(r("nn"), r("w2"), r("uv"), MUL)
-            ts(r("ni"), r("nn"), 5, SHR, 1023, AND)
-            cp(r("n16"), r("ni"))
+                if t:
+                    ts(r("ui"), pu, P(23), ADD)
+                else:
+                    cp(r("ui"), pu)
+                ts(r("uv"), r("ui"), 4095, AND)
+                ts(r("w2"), r("uv"), 1184.0, ADD)
+                tt(r("nn"), r("w2"), r("uv"), MUL)
+                ts(r("ni"), r("nn"), 5, SHR, 1023, AND)
+            cp(r("n16"), r("uv" if byu else "ni"))
         ts(v("dv"), v("sc", 15, 128, 16), v("thv"), A.is_ge)
         for n, part in enumerate(CFG["p3"]):
             lo, hi = 16 * part[0], 16 * part[1]
             r = lambda k: v(k, lo, hi)
             pd, a0, nh = "pD%d" % (n % 2), part[0] // 2, (part[1] - part[0]) // 2
             key = v(pd, 0, hi - lo)
-            if nh == 1:
-                ts(v3("nf", a0, a0 + 1), r("ni"), P(22), ADD)
+            if nh == 1 or CFG["nf1"]:
+                ts(v3("nf", a0, a0 + nh), r("ni"), float(PAD), ADD)
             else:
                 for cpx in range(2):
-                    ts(v3("nf", a0, a0 + nh, 16 * cpx, 16 * cpx + 16), cv("ni", cpx, cpx + 1, 16 * nh, lo), P(22), ADD)
+                    ts(v3("nf", a0, a0 + nh, 16 * cpx, 16 * cpx + 16), cv("ni", cpx, cpx + 1, 16 * nh, lo), float(PAD), ADD)
             turn(v3("t4", a0, a0 + nh), v3("nf", a0, a0 + nh))
             direct = not runs(part, CFG["f2"], "V")
-            mms(key, [(mb("I"), v3("k3", 8, 8 + 2 * nh))], True, False)
-            if direct:
-                swap(lambda cpx: cv(pd, cpx, cpx + 1, 16 * nh), nh, (("t4", a0),), False, False)
-            else:
-                swap(lambda cpx: v3("pQ", 16 + nh * cpx, 16 + nh * cpx + nh), nh, (("t4", a0),))
+            mms(key, [(mb("ON"), v3("k3", 8, 8 + 2 * nh))], True, False)
+            if direct and CFG["nf1"]:
+                for a in range(nh):
+                    swap(lambda cpx: cv(pd, 2 * a + cpx, 2 * a + cpx + 1, 16), 1, (("t4", a0 + a, 0),), False, False)
+            elif direct:
+                swap(lambda cpx: cv(pd, cpx, cpx + 1, 16 * nh), nh, (("t4", a0, 0),), False, False)
+            elif CFG["nf1"]:
+                swap(lambda cpx: v3("pQ", 16 + cpx, 16 + 2 * nh, step=2), nh, (("t4", a0, 0),))
                 act(r("pay"), v3("pQ", 16, 16 + 2 * nh))
-            apart("xn", "db", "e", "b3", "n16", 0, part, CFG["f2"], 0)
+            else:
+                swap(lambda cpx: v3("pQ", 16 + nh * cpx, 16 + nh * cpx + nh), nh, (("t4", a0, 0),))
+                act(r("pay"), v3("pQ", 16, 16 + 2 * nh))
+            apart("xn", "db", "e", "b3", "n16", 0, part, CFG["f2"], v("XS") if byu else X)
             distance(pd, part, "K2", "b3", "db", CFG["f2"])
             if direct:
                 scan(r("sc2"), C("R2", lo, hi), key, MIN, MAX)
@@ -728,6 +813,10 @@ def rank_program(g, core, T, topo):
             tt(r("tg"), r("lt"), r("n8"), MAX)
             cp(r("tg16"), r("tg"))
             scatter(v("X", 0, PAD + 2560 + 128), r("tg16"), cv("esel", a, b, 16))
+        if CFG["xs"] and not last:
+            w = CFG["xs"]
+            for lo in range(0, 256, w):
+                act(cv("XS", lo, lo + w, 16), ind(v("X", PAD, PAD + 1024), v("spot", lo, lo + w)))
         if last:
             for lo in (PAD, PAD + 512):
                 lift(v("X0", lo, lo + 512), v("X", lo, lo + 512), -128.0)
@@ -748,7 +837,7 @@ def rank_program(g, core, T, topo):
             if mi == "C":
                 mms(v(pb, 0, 96), [(mb("Z"), mb("I", 96))], True, False)
             for b in range(2):
-                mms(v(pb, b, 96, 2), [(mb(mi + str(2 * Q + b)), v("Fl", 48 * Q, 48 * Q + 48)) for Q in range(2)], mi != "C", mi != "C")
+                mms(v(pb, b, 96, 2), [(mb(k + str(2 * Q + b)), v("Fl", 48 * Q, 48 * Q + 48)) for Q in range(2) for k in {"C": "CT"}.get(mi, mi)], mi != "C", mi != "C")
         Sx = v("Sx", 12, 108)
         scan(v("Sx", 12, 120), v("pA", 0, 108), mb("c240", 108), ADD, MIN)
         tt(v("P2", 0, 96), Sx, v("pB", 0, 96), ADD)
@@ -778,7 +867,7 @@ def rank_program(g, core, T, topo):
         if not last:
             mms(v("pC", 0, 96), [(mb("I"), Sx)], False, True)
             act(v("old"), v("pC", 0, 96), F.Relu, bias=-448.5)
-        else:
+        if last or CFG["xs"]:
             ts(v("vl16"), v("no16"), -1024.0, ADD)
         for c0, c1, e in CFG["rc"]:
             o, a = v("R", 256 * c0, 256 * c1), ind(XH, v("s4", 16 * c0, 16 * c1))
@@ -793,7 +882,7 @@ def rank_program(g, core, T, topo):
         for c0, c1 in CFG["sc"]:
             a, b = v("mx", 256 * c0 + 15, 256 * c1, 16), v("mn", 256 * c0 + 15, 256 * c1, 16)
             if not last:
-                scatter(v("X", PAD, XW), v("no16", c0, c1), a, b)
+                scatter(v("X", PAD + 1024, XW), v("vl16", c0, c1), a, b) if CFG["xs"] else scatter(v("X", PAD, XW), v("no16", c0, c1), a, b)
             else:
                 tt(v("vb", 16 * c0, 16 * c1), a, b, ADD)
                 scatter(v("X0", PAD + 1024, XW), v("vl16", c0, c1), v("vb", 16 * c0, 16 * c1), v("m128", 16 * c0, 16 * c1))

import math
from concourse.mybir import dt, AluOpType as A, AxisListType, ActivationFunctionType as F

PAD = 16
XW = PAD + 2560 + 208
NA = 64
RO = 4
CFG = {
    "z1": "VVVV", "z2": "VVVV", "f1": "SSSS", "f2": "SSSS",
    "nq": 4,
    "hs": 6,
    "hc": "S",
    "fq": "V",
    "sv": (8, 9, 10, 11),
    "pre": ((0, 12),),
    "rc": ((0, 3, "V"), (3, 8, "S"), (8, 12, "S")),
    "vi": "S",
    "sc": ((0, 12),),
    "look": 0.0, "wake": 0.2, "idle": 1.0, "fit": 0.0, "passes": 6, "inorder": "", "xs": 0, "polish": 12000, "ld": (2.0, 0.0012, 1.5), "ahead": {}, "tries": 0, "frac": 30, "amp": 1.0,
}
CFG.update({'passes': 3, 'look': 0.1, 'f2': 'ASAAAaSS', 'z2': 'PPvVPVRP', 'z1': 'PPVVVVvV', 'f1': 'aASSSSSS', "lift": "S", 'sc': ((0, 8), (8, 12)),
            'rc': ((0, 2, 'S'), (2, 4, 'V'), (4, 8, 'S'), (8, 11, 'S'), (11, 12, 'S')), 'pre': ((0, 4), (4, 8), (8, 12)), 'sv': (0, 1, 2, 3), 'hc': 'S', 'fq': 'S',
            "p1": ((4, 8), (0, 4)), "p2": ((4, 8), (0, 4)), "p3": ((4, 8), (0, 4)), "fb": ("pB", "pC", "pE", "pD1"), "nb": ("pE", "pU", "pD0")})
CFG.update({'hs': 6, 'hc': 'VVVVVVV', 'kh': 2, 'es': 'V', 'g2': 'V', 'fq': 'S', 'lift': 'V', 'sv': (10, 11), 'pre': ((0, 4), (4, 8), (8, 12)), 'rc': ((0, 2, 'S'), (2, 4, 'S'), (4, 6, 'V'), (6, 8, 'S'), (8, 10, 'S'), (10, 11, 'S'), (11, 12, 'S')), 'sc': ((0, 6), (6, 12)), 'look': 0.1, 'z1': 'vPVVVVvV', 'z2': 'PPvVPVRP', 'f1': 'aSSSSSSS', 'f2': 'ASAAAaSS'})
CFG.update({'rem': 8.0, 'cof': 1, 'pk': 1, 'l1': ((0, 8),), 'l2': ((0, 8),), 'l3': ((0, 8),), 'passes': 3, 'hs': 6, 'hc': 'SSSSSSS', 'fq': 'V', 'lift': 'S', 'es': 'V', 'g2': 'S', 'idle': 3, 'fit': 0.05, 'sv': (2, 3), 'pre': ((0, 4), (4, 8), (8, 12)), 'rc': ((0, 2, 'S'), (2, 4, 'V'), (4, 8, 'S'), (8, 11, 'S'), (11, 12, 'S')), 'sc': ((0, 6), (6, 12)), 'look': 0.15, 'p1': ((4, 8), (2, 4), (0, 2)), 'p2': ((4, 8), (2, 4), (0, 2)), 'p3': ((4, 8), (0, 4)), 'z1': 'RRpVvVVV', 'z2': 'vPVpppRV', 'f1': 'aSaaSSSa', 'f2': 'AaaSaAsA'})
CFG.update({'hs': 6, 'hc': 'SSSSSSS', 'fq': 'V', 'lift': 'S', 'es': 'S', 'l1': ((0, 4), (4, 8)), 'l2': ((0, 8),), 'l3': ((0, 4), (4, 8)), 'cof': 1, 'pk': 1, 'idle': 6, 'fit': 0.05, 'sv': (2, 3), 'pre': ((0, 4), (4, 8), (8, 12)), 'rc': ((0, 2, 'S'), (2, 4, 'V'), (4, 6, 'S'), (6, 8, 'S'), (8, 10, 'S'), (10, 11, 'S'), (11, 12, 'V')), 'sc': ((0, 6), (6, 12)), 'look': 0.15, 'p1': ((0, 4), (4, 6), (6, 8)), 'p2': ((0, 4), (4, 8)), 'p3': ((0, 4), (4, 8)), 'z1': 'PPPvVpRR', 'z2': 'vRppPvpv', 'f1': 'aASVaaSa', 'f2': 'aASSasAa'})
CFG.update({'hs': 6, 'hc': 'SSSSSSS', 'fq': 'V', 'lift': 'V', 'es': 'S', 'l1': ((0, 4), (4, 8)), 'l2': ((0, 8),), 'l3': ((0, 4), (4, 8)), 'idle': 6, 'fit': 0.05, 'sv': (), 'pre': ((0, 4), (4, 8), (8, 12)), 'rc': ((0, 2, 'S'), (2, 3, 'S'), (3, 4, 'V'), (4, 6, 'S'), (6, 8, 'S'), (8, 10, 'S'), (10, 11, 'S'), (11, 12, 'V')), 'sc': ((0, 6), (6, 12)), 'look': 0.2, 'p1': ((0, 4), (4, 6), (6, 8)), 'p2': ((0, 4), (4, 6), (6, 8)), 'p3': ((0, 4), (4, 8)), 'z1': 'VVVVVVVV', 'z2': 'RRpVvpvR', 'f1': 'SSSSSSSS', 'f2': 'SSAAsAsa'})
CFG.update({'fit': 0, 'sv': (2, 3, 4, 5), 'pre': ((0, 2), (2, 4), (4, 8), (8, 12)), 'rc': ((0, 2, 'S'), (2, 4, 'S'), (4, 6, 'V'), (6, 8, 'S'), (8, 10, 'S'), (10, 11, 'S'), (11, 12, 'S')), 'sc': ((0, 6), (6, 12)), 'look': 0.1, 'p1': ((0, 4), (4, 6), (6, 8)), 'p2': ((0, 4), (4, 6), (6, 8)), 'p3': ((0, 2), (2, 4), (4, 8)), 'z1': 'VVVVVVVV', 'z2': 'RRpVVPvR', 'f1': 'SSSSSSSS', 'f2': 'SSAaSASa'})
CFG.update({'hs': 6, 'hc': 'SSSSSSS', 'fq': 'S', 'lift': 'V', 'es': 'S', 'l1': ((0, 4), (4, 8)), 'l2': ((0, 8),), 'l3': ((0, 8),), 'idle': 6, 'fit': 0.03, 'sv': (10, 11), 'pre': ((0, 2), (2, 4), (4, 8), (8, 12)), 'rc': ((0, 2, 'S'), (2, 4, 'S'), (4, 6, 'V'), (6, 8, 'S'), (8, 10, 'S'), (10, 11, 'S'), (11, 12, 'S')), 'sc': ((0, 8), (8, 12)), 'look': 0.15, 'p1': ((0, 4), (4, 6), (6, 8)), 'p2': ((0, 4), (4, 6), (6, 8)), 'p3': ((0, 4), (4, 6), (6, 8)), 'z1': 'VVVVvVVV', 'z2': 'PRVvVRvP', 'f1': 'SSSSSSSS', 'f2': 'TaATaaTa', 'um': 'SSVV', 'nf1': 1, 'hc': 'SSSS'})
CFG.update({'hs': 5, 'hc': 'VSSS', 'fq': 'S', 'lift': 'S', 'es': 'S', 'um': 'SVSV', 'nf1': 1, 'rem': 8.0, 'sv': (2, 3), 'z1': 'VVVVvVVV', 'z2': 'pRVvVRvp', 'f1': 'SSSSSSSS', 'f2': 'TaATaATa'})
CFG.update({'hs': 6, 'hc': 'VSSS', 'fq': 'S', 'lift': 'V', 'l2': ((0, 4), (4, 8)), 'nf1': 0, 'z1': 'VVVVvVvV', 'z2': 'prVvVRVp', 'f1': 'SSSSSSSS', 'f2': 'tabtaATa'})

_B, _F, _I, _U, _H = "bfloat16", "float32", "int32", "uint16", "float16"
_S = {
    "X": (XW, _B), "X0": (XW, _B), "cot": (PAD + 2560, _I), "sut": (XW - PAD, _I), "dls": (512, _B), "dx0": (2048, _B), "dx1": (2048, _B),
    "ab16": (64, _U), "pt": (32, _I), "po": (32, _I), "abi": (16, _I), "lab": (16, _I), "wtc": (1, _B), "thi": (1, _I),
    "dfk": (256, _U), "f2": (256, _H), "xf": (2048, _B), "xn": (2048, _B), "z": (2048, _B), "z2": (2048, _B), "e1": (2048, _B), "e": (2048, _B),
    "sc": (128, _F), "gp": (128, _F), "qq": (128, _F), "ds": (128, _F),
    "key2": (128, _F), "sc2": (128, _F), "d16": (16, _U), "sj": (128, _U), "ui": (128, _I), "uv": (128, _I), "w2": (128, _F), "uy": (128, _B), "us": (128, _F), "nn": (128, _I),
    "ni": (128, _I), "n16": (128, _U), "pay": (128, _F),
    "k8": (8, _I), "n8": (8, _I), "j8": (8, _I), "nl": (8, _U), "jf": (8, _F), "jl": (8, _U),
    "qb": (128, _F), "nb": (8, _F), "cg": (128, _H), "mh": (1536, _H), "esel": (128, _B), "tabn": (1040, _F),
    "hs": (128, _B), "ohl": (4096, _B), "ohh": (6400, _B),
    "ab1": (1024, _F), "rl": (1024, _F), "los": (8, _F), "lt": (8, _F), "tg": (8, _F), "tg16": (8, _U),
    "Fq": (256, _H), "Eh": (96, _H), "Fl": (96, _B), "Sx": (120, _B), "P2": (112, _B), "sg": (1440, _B), "sq": (1296, _B), "sv": (1296, _B), "rv": (1296, _B),
    "xa": (12, _F), "xb": (12, _B), "xl": (12, _U),
    "cm": (192, _B), "no16": (12, _U), "s4": (192, _U),
    "R": (3072, _B), "mx": (3072, _B), "mn": (3072, _B), "vb": (192, _B), "m128": (192, _B),
    "XS": (4096, _B), "spot": (256, _U), "su1": (256, _I), "su2": (256, _I), "vl16": (12, _U), "old": (96, _B),
    "dv": (8, _B), "u8": (8, _F), "abf": (16, _F), "a8": (8, _F), "az": (1, _F), "ay": (1, _B), "thb": (1, _F), "thv": (1, _F), "th8": (1, _F),
    "pc": (40, _F), "ci": (160, _I), "cf": (1408, _F), "mf": (256, _F), "mb": (4512, _B), "rr": (3072, _B), "tmp": (256, _F), "jr": (192, _B),
    "ks": (128, _F), "k4": (192, _F),
}
SCRATCH = {k: ("sbuf", [128, n], d) for k, (n, d) in _S.items()}
for _k in ("a3", "b3", "da", "db"):
    SCRATCH[_k] = ("sbuf", [128, 8, 256], _B)
SCRATCH["t3"] = ("sbuf", [128, 8, 32], _H)
SCRATCH["t4"] = ("sbuf", [128, 4, 32], _H)
SCRATCH["k3"] = ("sbuf", [128, 20, 16], _B)
SCRATCH["hi4"] = ("sbuf", [128, 4, 128], _B)
SCRATCH["lo4"] = ("sbuf", [128, 4, 128], _B)
PSUM = ("pA", "pB", "pC", "pE", "pU", "pD0", "pD1", "pQ")
SCRATCH["nf"] = ("sbuf", [128, 4, 32], _H)
for _k in PSUM[:7]:
    SCRATCH[_k] = ("psum", [128, 512], _F)
for _k in PSUM[7:]:
    SCRATCH[_k] = ("psum", [128, 32, 16], _F)
BANK = ("pA", "pB", "pC", "pE")
LOADS = ["ldla", "ldlb", "ldco", "ldsu", "lddl", "ldx", "ldwt", "ldth"]
STORES = ["stx0", "stx1", "sta", "stb"]
SEMAPHORES = ["sV", "sS", "sP", "sG", "loc", "ab1a", "ab2a", "ab3a", "dl1a", "dl2a", "dl3a"] + LOADS + STORES
CY, PCY, GAT, SCT = 0.00091, 0.00046, 1.56, 3.8
ORDER = []


def polish(ops, succ, before, order, tries):
    eng, seed = [o[0] for o in ops], [1]

    def chance():
        seed[0] = (seed[0] * 1103515245 + 12345) % 2147483648
        return seed[0] / 2147483648

    def times(order):
        end, why, free, last = [0.0] * len(ops), [None] * len(ops), {}, {}
        for i in order:
            t, w = free.get(eng[i], 0.0), (last.get(eng[i]), True)
            for j, x in before[i]:
                if end[j] + x > t + 1e-9:
                    t, w = end[j] + x, (j, False)
            end[i], why[i], free[eng[i]], last[eng[i]] = t + ops[i][3], w, t + (ops[i][3] if ops[i][4] is None else 0.1), i
        return max(end), end, why

    def moved(seg, nxt):
        along, queues = {seg[-1]}, set()
        for i in seg[-2::-1]:
            if eng[i] in queues or any(j in along for j, w in nxt[i]):
                if eng[i] == eng[seg[-1]]:
                    return None
                along.add(i)
                queues.add(eng[i])
        return [i for i in seg if i in along] + [i for i in seg if i not in along]

    now = times(order)
    best = (now[0], order)
    while tries > 0:
        chain = [now[1].index(now[0])]
        while now[2][chain[-1]][0] is not None:
            chain.append(now[2][chain[-1]][0])
        queued = [now[2][i][1] and eng[i] != "Y" and j >= len(LOADS) for i, j in zip(chain, chain[1:])] + [False]
        spots = [k for k, x in enumerate(queued) if x]
        place = {i: x for x, i in enumerate(order)}
        for _ in range(30):
            k, d = spots[int(chance() * len(spots))], 1
            while chance() < 0.5 and queued[k + d]:
                d += 1
            a, b = place[chain[k + d]], place[chain[k]] + 1
            seg = moved(order[a:b], succ) if chance() < 0.5 else (moved(order[a:b][::-1], before) or [])[::-1]
            tries -= 1
            if seg:
                new = times(order[:a] + seg + order[b:])
                if new[0] < now[0] or chance() < 0.5 * math.exp((now[0] - new[0]) / 0.02):
                    order, now = order[:a] + seg + order[b:], new
                    best = min(best, (now[0], order), key=lambda x: x[0])
                    break
    return best


def rank_program(g, core, T, topo):
    rank = T.rank_of(core)
    if rank is None:
        return
    N = len(T.cores)
    WAKE, LOOK, IDLE, FIT = CFG["wake"], CFG["look"], CFG["idle"], CFG["fit"]
    que = {"V": g.vector, "S": g.scalar, "P": g.tensor, "G": g, "Y": g.sync}
    cnt = {"V": 0, "S": 0, "P": 0, "G": 0}
    known = {k: {} for k in que}
    snap, hist, ops, marks = {}, {}, [], []

    def v(name, lo=0, hi=None, step=1, p=None):
        hi = (_S[name][0] if name in _S else 512) if hi is None else hi
        ps = slice(0, 128) if p is None else slice(p[0], p[1])
        ap = T[name][ps, lo:hi] if step == 1 else T[name][ps, lo:hi:step]
        return (ap, [(name, lo, hi, step == 1 and p is None)], -(-(hi - lo) // step))

    def v3(name, c0, c1, k0=0, k1=None, step=1):
        w = SCRATCH[name][1][2]
        k1 = w if k1 is None else k1
        ap = T[name][:, c0:c1, k0:k1] if step == 1 else T[name][:, c0:c1:step, k0:k1]
        if k0 == 0 and k1 == w and step == 1:
            return (ap, [(name, w * c0, w * c1, True)], (c1 - c0) * w)
        return (ap, [(name, w * c + k0, w * c + k1, True) for c in range(c0, c1, step)], -(-(c1 - c0) // step) * (k1 - k0))

    def ind(win, off):
        return (win[0].indirect(off[0]), win[1] + off[1], 16 * off[2], True)

    def clash(eng, b, lo, hi, isw, e2, w2, l2, h2):
        if b in PSUM and e2 != eng:
            return 2
        if b in PSUM and e2 == "P":
            return 1
        if not ((isw or w2) and lo < h2 and l2 < hi):
            return 0
        return 1 if isw and e2 == eng and eng in CFG["inorder"] else 2

    def need_of(eng, acc):
        need = {}
        for (b, lo, hi, _c, isw) in acc:
            for (e2, c2, w2, l2, h2) in hist.get(b, ()):
                if need.get(e2, 0) < c2 and clash(eng, b, lo, hi, isw, e2, w2, l2, h2) == 2:
                    need[e2] = c2
        return need

    def sem_of(e):
        return T.sem["s" + e] if e in ("V", "S", "P", "G") else T.sem[e]

    def wait(eng, need):
        for e2 in sorted(need, key=lambda e: (e != eng, e)):
            c2 = need[e2]
            if known[eng].get(e2, 0) < c2:
                que[eng].wait_ge(sem_of(e2), c2)
                for k, n in snap.get((e2, c2), {}).items():
                    if known[eng].get(k, 0) < n:
                        known[eng][k] = n
                known[eng][e2] = c2

    def note(e, c, acc):
        for (b, lo, hi, full, isw) in acc:
            h = hist.setdefault(b, [])
            h[:] = [x for x in h if not (((isw and full) or (x[0] == e and x[2] == isw)) and lo <= x[3] and x[4] <= hi)]
            h.append((e, c, isw, lo, hi))

    def accs(rd, wr):
        return [a + (False,) for x in rd for a in x[1]] + [a + (True,) for x in wr for a in x[1]]

    def rec(eng, fns, rd, wr, cost, sem=None):
        ops.append((eng, fns, accs(rd, wr), cost, sem))

    def issue(op):
        eng, fns, acc, cost, sem = op
        wait(eng, need_of(eng, acc))
        if sem is None:
            for fn in fns:
                cnt[eng] += 1
                fn().then_inc(sem_of(eng), 1)
            s = dict(known[eng])
            s[eng] = cnt[eng] - 1
            snap[(eng, cnt[eng])] = s
            note(eng, cnt[eng], acc)
        elif sem == "remote":
            fns[0]()
        else:
            fns[0]().then_inc(T.sem[sem], 16)
            snap[(sem, 16)] = dict(known[eng])
            note(sem, 16, acc)

    def flush():
        n = len(ops)
        succ, npred, h2 = [[] for _ in range(n)], [0] * n, {}
        for i, (eng, _f, acc, cost, _s) in enumerate(ops):
            pred = {}
            for (b, lo, hi, _c, isw) in acc:
                for (j, e2, w2, l2, hh) in h2.get(b, ()):
                    c = clash(eng, b, lo, hi, isw, e2, w2, l2, hh)
                    if c and pred.get(j, 0) < c:
                        pred[j] = c
            for (b, lo, hi, full, isw) in acc:
                h = h2.setdefault(b, [])
                if isw and full and b not in PSUM:
                    h[:] = [x for x in h if not (lo <= x[3] and x[4] <= hi)]
                elif b in PSUM and eng == "P":
                    del h[:]
                h.append((i, eng, isw, lo, hi))
            for j, c in pred.items():
                if j != i:
                    succ[j].append((i, WAKE if c == 2 else 0.0))
                    npred[i] += 1
        before = [[] for _ in range(n)]
        for i in range(n):
            for j, w in succ[i]:
                before[j].append((i, w))

        def plan(nxt, prv, prio):
            left, ready, free, end, order = [len(x) for x in prv], [0.0] * n, {k: 0.0 for k in que}, [0.0] * n, []
            avail = {k: [i for i in range(n) if not left[i] and ops[i][0] == k] for k in que}
            prio = [x + 1000.0 * max(0, len(LOADS) - i) for i, x in enumerate(prio)]
            pick = {}
            while len(order) < n:
                for e in que:
                    if avail[e] and e not in pick:
                        t0 = max(free[e], min([ready[i] for i in avail[e]]))
                        worth = lambda i: (prio[i] - IDLE * (ready[i] - t0) if ready[i] > t0 else prio[i], -i)
                        i = max([i for i in avail[e] if ready[i] <= t0 + LOOK], key=worth)
                        if ready[i] > t0:
                            i = max([j for j in avail[e] if max(t0, ready[j]) + ops[j][3] <= ready[i] + FIT], key=worth, default=i)
                        pick[e] = (max(t0, ready[i]), e, i)
                t0, e, i = min(pick.values())
                del pick[e]
                avail[e].remove(i)
                free[e] = t0 + (ops[i][3] if ops[i][4] is None else 0.1)
                end[i] = t0 + ops[i][3]
                order.append(i)
                for j, w in nxt[i]:
                    ready[j] = max(ready[j], end[i] + w)
                    left[j] -= 1
                    if not left[j]:
                        avail[ops[j][0]].append(j)
                        pick.pop(ops[j][0], None)
            return order, end

        if not ORDER:
            prio = [0.0] * n
            for i in range(n - 1, -1, -1):
                prio[i] = ops[i][3] + max([prio[j] + w for j, w in succ[i]] + [0.0])
            best = None
            ahead = [CFG["ahead"].get(([a[0] for a in op[2] if a[4]] + [""])[0], 0.0) for op in ops]
            for _ in range(CFG["passes"]):
                order, end = plan(succ, before, [x + y for x, y in zip(prio, ahead)])
                if best is None or max(end) < best[0]:
                    best = (max(end), order)
                    keep = prio
                prio = plan(before, succ, end)[1]
            best = polish(ops, succ, before, best[1], CFG["polish"]) if CFG["polish"] else best
            if "hook" in CFG:
                best = CFG["hook"](ops, marks, plan, succ, before, keep, best)
            ORDER.extend(best[1])
        for i in ORDER:
            issue(ops[i])
        del ops[:]

    isv = lambda x: isinstance(x, tuple)
    raw = lambda x: x[0] if isv(x) else x
    vec, sca, ten = g.vector, g.scalar, g.tensor
    small = lambda *xs: all(SCRATCH[x[1][0][0]][2] in (_B, _U, _H) for x in xs)
    isind = lambda x: len(x) > 3
    inps = lambda x: x[1][0][0] in PSUM

    def vcost(o, a, k=1.0):
        if isind(a):
            return 0.05 + GAT * CY * o[2]
        return max(64, k * o[2]) * CY

    def tt(o, a, b, op):
        k = 1 if inps(a) or inps(b) else 2
        rec("V", [lambda: vec.tensor_tensor(o[0], a[0], b[0], op)], [a, b], [o], vcost(o, a, k))

    def ts(o, a, s1, op0, s2=None, op1=None, after=()):
        rd = [a] + [x for x in (s1, s2) if isv(x)] + list(after)
        c = vcost(o, a, 0.5 if small(o, a) else 1)
        if op1 is None:
            rec("V", [lambda: vec.tensor_scalar(o[0], a[0], raw(s1), None, op0)], rd, [o], c)
        else:
            rec("V", [lambda: vec.tensor_scalar(o[0], a[0], raw(s1), raw(s2), op0, op1)], rd, [o], c)

    def cp(o, a, after=()):
        rec("V", [lambda: vec.tensor_copy(o[0], a[0])], [a] + list(after), [o], vcost(o, a, 0.5 if small(o, a) else 1))

    def scatter(win, off, a, b=None):
        if b is None:
            rec("V", [lambda: vec.tensor_copy(win[0].indirect(off[0]), a[0])], [a, off], [win], 0.05 + SCT * CY * a[2])
        else:
            rec("V", [lambda: vec.tensor_tensor(win[0].indirect(off[0]), a[0], b[0], A.add)], [a, b, off], [win], 0.05 + SCT * CY * a[2])

    def ms(o, c):
        rec("V", [lambda: vec.memset(o[0], c)], [], [o], max(64, o[2]) * CY)

    def scan(o, a, b, op0, op1, first=0.0):
        rec("V", [lambda: vec.tensor_tensor_scan(o[0], a[0], b[0], first, op0, op1)], [a, b], [o], vcost(o, b, 0.5 if small(o, a, b) else 1))

    def turn(o, i):
        rec("V", [lambda: vec.transpose(o[0], i[0])], [i], [o], max(64, i[2]) * CY)

    def act(o, a, f=F.Copy, bias=None, scale=None, acc=None):
        rd = [a] + [x for x in (bias, scale) if isv(x)]
        kw = {}
        if bias is not None:
            kw["bias"] = raw(bias)
        if scale is not None:
            kw["scale"] = raw(scale)
        if acc is not None:
            kw["accum_out"] = acc[0]
        rec("S", [lambda: sca.activation(o[0], a[0], f, **kw)], rd, [o] + ([acc] if acc is not None else []),
            vcost(o, a) + (0.0 if acc is None else 0.02))

    def mms(o, pairs, start=True, stop=True, f32=False):
        n = len(pairs)
        fns = [(lambda l=l, r=r, i=i: ten.matmul(o[0], l[0], r[0], start and i == 0, stop and i == n - 1)) for i, (l, r) in enumerate(pairs)]
        rd = {}
        for side in range(2):
            for x in pairs:
                for (b, lo, hi, c) in x[side][1]:
                    q = rd.get((b, side), (lo, hi))
                    rd[(b, side)] = (min(lo, q[0]), max(hi, q[1]))
        cost = sum(max(min(64, l[2]), r[2]) for l, r in pairs) * PCY * (4 if f32 else 1)
        rec("P", fns, [(None, [(b, lo, hi, False)], 0) for (b, _s), (lo, hi) in rd.items()], [o], cost)

    def iota(o, pat, base, cm, **kw):
        rec("G", [lambda: g.iota(o[0], pat, base, cm, **kw)], [], [o], 0.13 + 2 * CY * o[2])

    def gcopy(o, a, after=()):
        rec("G", [lambda: g.affine_select(o[0], a[0], [[0, a[2]]], A.is_ge, 0.0, 0, 0)], [a] + list(after), [o], 0.17 + 2 * CY * o[2])

    def load(eng, name, o, src, after=(), more=0.0):
        rec(eng, [lambda: que[eng].dma_start(o[0], src[:])], list(after), [o], CFG["ld"][0] + o[2] * CFG["ld"][1] + more, name)

    def store(name, dst, a):
        rec("Y", [lambda: g.sync.dma_start(dst, a[0])], [a], [], 3.0, name)

    locs = [0]
    trip = lambda s: (None, [("~" + s, 0, 1, True)], 0)

    def remote(dst, name, lo, hi, a, rsem):
        rid, pid = topo.addr(dst)[:2]
        en = topo.engines(core, dst)[:4]
        locs[0] += len(en)
        rec("G", [lambda: g.remote_dma(T[name][:, lo:hi], a[0], T.sem[rsem], T.sem.loc, pid, rid, sum(1 << x for x in en))], [a], [trip(rsem)], CFG["rem"], "remote")
        return len(en)

    ADD, SUB, MUL, MAX, MIN = A.add, A.subtract, A.mult, A.max, A.min
    SHR, AND = A.arith_shift_right, A.bitwise_and
    XH, cot, sut = v("X", PAD, PAD + 2560), v("cot", PAD), v("sut")
    NQ, KH = CFG["nq"], CFG["kh"]
    WQ, HR, LR = 128 // NQ, 48 // NQ, 32 // NQ
    HV = HR - CFG["hs"]
    HB = 128 + NQ - 1
    HW = 128 * HR + WQ

    lab = v("lab")
    load("Y", "ldla", v("lab", 0, 8), T.la)
    load("Y", "ldlb", v("lab", 8, 16), T.lb)
    load("Y", "ldco", cot, T.co)
    load("S", "lddl", v("dls", 0, 128), T.dl)
    load("S", "ldth", (T.thi[0:8, 0:1], [("thi", 0, 1, True)], 1), T.th)
    load("S", "ldwt", v("wtc"), T.wt)
    load("S", "ldx", v("X0", PAD, PAD + 2560), T.x0, more=CFG["ld"][2])
    load("Y", "ldsu", v("sut", 0, 2560), T.su, [cot])
    landed = {}
    for s in range(1, RO):
        dst = T.cores[(rank + s) % N]
        k = remote(dst, "dls", 128 * s, 128 * s + 128, v("dls", 0, 128), "dl%da" % s)
        landed["dl%da" % s], landed["ab%da" % s] = k, k
        note("dl%da" % s, k, [("dls", 128 * s, 128 * s + 128, True, True)])
        note("ab%da" % s, k, [("pt", 8 * s, 8 * s + 8, True, True)])

    def spread(t):
        for k in range(16):
            o, a = v("dx%d" % (t % 2), k, 2048, 16), v("dls", 128 * t, 128 * t + 128)
            o = (o[0], [(o[1][0][0], k, k + 1, True)], 128)
            if t:
                gcopy(o, a, [trip("dl%da" % t)])
            else:
                act(o, a)

    spread(0)

    CF, at = {}, [0]

    def cf(k, n):
        CF[k] = (at[0], n)
        at[0] += n
        return v("cf", CF[k][0], CF[k][0] + n)

    C = lambda k, lo=0, hi=None: v("cf", CF[k][0] + lo, CF[k][0] + (CF[k][1] if hi is None else hi))
    SM = {"allow_small_or_imprecise_dtypes": True}
    iota(v("tmp"), [[1, 256]], 0, 0, **SM)
    iota(v("ci", 128, 129), [[0, 1]], 0, 1)
    iota(cf("kc", 128), [[0, 8], [1, 16]], 0, 0, **SM)
    iota(cf("c4", 128), [[1, 8], [0, 16]], 0, 0, **SM)
    iota(v("jr"), [[1, 192]], 0, 0, **SM)
    iota(v("tabn"), [[1, 1040]], 0, 0, **SM)
    col = lambda n: v("tmp", 0, n)
    cp(v("ab16", 0, 16), lab)
    ts(v("u8"), v("lab", 0, 8), 4096.0, MUL)
    tt(v("pt", 0, 8), v("u8"), v("lab", 8, 16), ADD)
    ms(v("cot", 0, PAD), 0)
    ms(v("sut", 2560), 0)
    P = lambda i: v("pc", i, i + 1)
    cp(P(0), v("ci", 128, 129))
    for d, s1, op in ((129, 4, SHR), (130, 15, AND), (131, 5, SHR), (132, 16, AND)):
        ts(v("ci", d, d + 1), v("ci", 128, 129), s1, op)
    for d, s in ((1, 129), (2, 130), (3, 131)):
        cp(P(d), v("ci", s, s + 1))
    ts(P(5), v("ci", 132, 133), 1.0 / 16, MUL)
    ts(P(4), P(5), -1.0, MUL, 1.0, ADD)
    ts(P(6), P(3), 4.0, ADD)
    tt(P(9), P(0), P(2), SUB)
    ts(P(10), P(9), 15.0, ADD)
    MB, nb_ = {}, 0
    for k, n in ([(k, 144) for k in ("B1", "K1", "nK1", "K2", "nK2", "W")] + [(k, 128) for k in ("I16", "I32", "I", "nI", "Z", "ON")] + [("U", 512), ("SH", 512), ("c240", 112)]
                 + [(k + str(b), 128) for k in "TOC" for b in range(4)]):
        MB[k], nb_ = nb_, nb_ + n
    mb = lambda k, n=128: v("mb", MB[k], MB[k] + n)
    slide = lambda k, m: v("mb", MB[k] + 15 - m, MB[k] + 143 - m)
    MF = {"I": 0, "E8": 128}
    sw = lambda cpx, gp, w: cv("mh", 2 * cpx + gp, 2 * cpx + gp + 1, 128, w)
    cv = lambda name, a, b, w=256, o=0: v(name, o + w * a, o + w * b)
    mf = lambda k: v("mf", MF[k], MF[k] + 128)
    U1, U2 = 2.0 ** 28, 2.0 ** 15
    ts(mb("B1", 144), col(144), P(10), A.is_equal)
    act(mb("K1", 144), mb("B1", 144), scale=U1)
    act(v3("k3", 0, 8), C("kc"), scale=U1 / 16)
    ts(v("ks"), C("kc"), -32.0, MUL, 480.0, ADD)
    ts(P(22), P(4), -2.0 ** 18, MUL)
    ts(v3("k3", 8, 16), v("ks"), P(5), MUL, P(22), ADD)
    ts(P(28), P(4), 65520.0, MUL, 16.0, ADD)
    ts(v3("k3", 16, 20), C("kc", 0, 64), 0.0, MUL, P(28), ADD)
    ts(cf("R1", 128), C("kc"), 0.0, A.is_equal, 2.0 ** 45, MUL)
    ts(mf("I"), col(128), P(0), A.is_equal)
    for cpx in range(2):
        for gp in range(2):
            ts(P(11 + 2 * cpx + gp), P(0), 16.0 * (gp - cpx), ADD)
            ts(sw(cpx, gp, 0), col(128), P(11 + 2 * cpx + gp), A.is_equal, P(4 + cpx), MUL)
    ts(v("mh", 512, 1024), v("mh", 0, 512), 4096.0, MUL)
    act(mb("I"), mf("I"))
    act(mb("nI"), mf("I"), scale=-1.0)
    act(mb("nK1", 144), mb("B1", 144), scale=-U1)
    ts(mb("W", 144), mb("B1", 144), v("wtc"), MUL)
    ts(mf("E8"), C("c4"), P(0), A.is_equal)
    th8 = v("th8", 0, 1, 1, (0, 8))
    cp(th8, v("thi", 0, 1, 1, (0, 8)))
    mms(v("pU", 0, 1), [(v("mf", MF["E8"], MF["E8"] + 128, 1, (0, 8)), th8)], f32=True)
    cp(v("thb"), v("pU", 0, 1))
    ts(v("thv"), v("thb"), U1, MUL)
    ts(P(20), v("thb"), 10240.0, ADD, U1 / 8, MUL)
    ts(P(21), v("thb"), -1.0 / 64, MUL, -63.0 / 128, ADD)
    ts(cf("R2", 128), C("kc"), 0.0, A.is_gt, 2.0 ** 26, MUL)
    ts(C("R2"), C("R2"), -2.0 ** 25, ADD)
    act(mb("K2", 144), mb("B1", 144), scale=U2)
    act(mb("nK2", 144), mb("B1", 144), scale=-U2)
    ms(mb("ON"), 1.0)
    ms(mb("Z"), 0.0)
    if KH > 1:
        ts(P(24), P(2), 7.5, A.is_gt, 56.0, MUL)
        ts(P(25), P(1), 8.0, MUL, P(2), ADD)
        tt(P(24), P(24), P(25), ADD)
    iota(v("ab1", 0, 512), [[32, 4], [0, 4], [1, 32]], 0, 0, **SM)
    ts(v("mh", 1024, 1536), v("ab1", 0, 512), P(24), A.is_equal)
    iota(v("rl", 0, 256), [[0, 2], [1, 4], [0, 32]], 0, 0, **SM)
    act(mb("SH", 256), v("rl", 0, 256), scale=-32.0 / 128)
    act(v("mb", MB["SH"] + 256, MB["SH"] + 512), v("rl", 0, 256), scale=-33.0 / 128)
    act(mb("I32"), mf("I"), scale=-32.0)
    ts(cf("lf", 8), col(8), 16.0, MUL, P(2), ADD)
    ts(cf("cT", 8), C("lf"), PAD + 2560.0, ADD)
    ts(cf("c15", 8), C("lf"), 16.0, MUL, 15.0, ADD)
    ts(cf("hl", 8), C("lf"), 8192.0, MUL)
    ts(cf("c2", 8), C("lf"), -1.0 / 256, MUL, 1.0 / 256, ADD)
    act(cf("lfr", 128), col(128), scale=1.0 / 128)
    act(mb("I16"), mf("I"), scale=16.0)
    ts(v("ks"), C("kc"), P(2), A.is_ge, 100.0, MUL)
    tt(v("ks"), v("ks"), C("c4"), ADD)
    ts(v("pc", 32, 34), v("pc", 4, 6), -1.0, MUL)
    ts(P(18), P(3), 16.0, MUL, P(2), ADD)
    ts(P(19), P(18), 64.0, ADD)
    ts(v("pc", 26, 28), v("pc", 4, 6), 256.0, MUL)
    for Q in range(2):
        for b in range(2):
            i = str(2 * Q + b)
            ts(mb("O" + i), C("c4"), P(6 if Q else 3), A.is_equal, P(4 + b), MUL)
            ts(mb("C" + i), col(128), P(18 + Q), A.is_equal, P(26 + b), MUL)
            ts(mb("T" + i), v("ks"), P(6 if Q else 3), A.is_equal, v("pc", 32 + b, 33 + b), MUL)
    ts(P(16), P(1), 32.0, MUL, P(2), ADD)
    ts(P(17), P(16), 16.0, ADD)
    for b in range(2):
        ts(v("mb", MB["U"] + 256 * b, MB["U"] + 256 * b + 256), col(256), P(16 + b), A.is_equal)
    for Q in range(2):
        a, b = v("k4", 48 * Q, 48 * Q + 48), v("k4", 96 + 48 * Q, 144 + 48 * Q)
        ts(a, col(48), 2.0, MUL, float(Q), ADD)
        ts(b, col(48), NQ * HV - 0.5, A.is_lt, 512.0, MUL)
        tt(b, b, a, ADD)
        ts(b, b, 2.0, ADD, P(0), A.is_equal)
        ts(a, a, P(0), A.is_equal)
    tt(v("Eh"), v("k4", 0, 96), v("k4", 96, 192), SUB)
    for s in range(NQ):
        ms(v("ohh", HW * s + 128 * HR, HW * s + HW), -1.0)
    ms(mb("c240", 108), 240.0)
    ms(v("Sx", 0, 12), -1.0)
    ms(v("m128"), -128.0)
    mms(v("pU", 0, 1), [(slide("W", j), v("m128", 0, 1)) for j in range(16)])
    cp(P(23), v("pU", 0, 1))
    if CFG["xs"]:
        ts(v("su1"), col(256), 16.0, MUL, P(2), ADD)
        ts(v("ab1", 512, 768), v("su1"), 1184.0, ADD)
        tt(v("su2"), v("ab1", 512, 768), v("su1"), MUL)
        ts(v("su1"), v("su2"), 5, SHR, 1023, AND)
        cp(v("spot"), v("su1"))
    UB = 160.0 * 4096
    ts(P(29), P(23), UB - 2048, ADD)
    ts(P(30), P(23), UB + 592, ADD)
    ts(cf("jl", 12), col(12), 16.0, MUL, P(2), ADD)
    ts(cf("bj", 12), C("jl"), 0.5, ADD)
    ms(v("P2", 96, 112), 0.0)
    ts(v("P2", 97, 109), C("jl"), 1.0, ADD)
    SV = CFG["sv"]
    if SV:
        ms(v("rv", 0, 108 * len(SV)), 1.0)
        ms(v("rv", 0, 108 * len(SV), 108), 0.0)
        ms(v("sq", 108 * SV[0], 108 * SV[-1] + 108), 0.0)
    for x, y in ((0, -32.25), (1536, 32.0)):
        ts(v("rr", x, x + 128), C("kc"), 15.0, A.is_equal, y, MUL)
        for n, m in ((128, 128), (256, 256), (512, 512), (1024, 512)):
            act(v("rr", x + n, x + n + m), v("rr", x, x + m))

    shifts = lambda dx, a, b: (cv(dx, a, b, 128)[0], [(dx, 0, 16, False)], 128 * (b - a))
    bank = lambda a, b: v(BANK[a // 2], 256 * (a % 2), 256 * (a % 2 + b - a))

    def runs(part, how, kinds):
        out = []
        for a in range(part[1] - 2, part[0] - 2, -2):
            two = [(a, a + 2)] if how[a] == how[a + 1] and how[a].isupper() else [(a + 1, a + 2), (a, a + 1)]
            out += [x + (how[x[0]].upper(),) for x in two if how[x[0]].upper() in kinds]
        return out

    def swap(out, nblk, srcs, start=True, stop=True, more=()):
        for cpx in range(2):
            mms(out(cpx),
                list(more) + [(sw(cpx, gp, w), v3(t, a0, a0 + nblk, 16 * gp, 16 * gp + 16)) for t, a0, w in srcs for gp in range(2)], start, stop)

    def distance(pd, part, w, ab, db, how):
        p0, p1 = part
        vs = [c for c in range(p0, p1) if how[c].upper() == "V"]
        if vs:
            c0, c1 = vs[0], vs[-1] + 1
            assert c1 - c0 == len(vs)
            mms(cv(pd, c0 - p0, c1 - p0, 16), [(slide("n" + w, m), v3(db, c0, c1, 16 * m, 16 * m + 16)) for m in range(16)], False, False)
        mms(cv(pd, 0, p1 - p0, 16), [(slide(w, m), v3(ab, p0, p1, 16 * m, 16 * m + 16)) for m in range(16)], False, True)

    def two(o, first, then):
        mms(o, [first], True, False)
        mms(o, [then], False, True)

    def shifted(o, z, lists, dx, part, how):
        for a, b, h in runs(part, how, "PRVW"):
            if h in "VW":
                for x, y in ([(2 * a, 2 * b)] if h == "V" else [(x, x + 1) for x in range(2 * a, 2 * b)]):
                    tt(cv(z, x, y, 128), ind(X, cv(lists, x, y, 8)), shifts(dx, x, y), ADD)
                ts(cv(o, a, b), cv(z, a, b), off, MAX, off + 63.0, MIN)
                continue
            act(cv(z, a, b), ind(X, cv(lists, a, b, 16)))
            two(bank(a, b), (mb("I"), shifts(dx, 2 * a, 2 * b)), (mb("I"), cv(z, a, b)))
            if h == "P":
                ts(cv(o, a, b), bank(a, b), off, MAX, off + 63.0, MIN)
            else:
                act(cv(z, a, b), bank(a, b), F.Relu, bias=-off)
                ts(cv(o, a, b), cv(z, a, b), 63.0, MIN, off, ADD)

    def apart(xb, db, eb, ab, lists, l0, part, how, X):
        for a, b, h in runs(part, how, "STABV"):
            lst = cv(lists, a, b, 16, l0)
            if h in "ST":
                act(cv(xb, a, b), ind(X, lst))
                pair = [(mb("I"), cv(xb, a, b)), (mb("nI"), cv(eb, a, b))]
                two(bank(a, b), pair[h == "T"], pair[h == "S"])
                act(v3(ab, a, b), bank(a, b), F.Abs)
            elif h in "AB":
                for x, y in ([(2 * a, 2 * b)] if h == "A" else [(x, x + 1) for x in range(2 * a, 2 * b)]):
                    tt(cv(xb, x, y, 128), ind(X, cv(lists, x, y, 8, l0)), cv(eb, x, y, 128), SUB)
                act(v3(ab, a, b), cv(xb, a, b), F.Abs)
            else:
                for c in range(b - 1, a - 1, -1):
                    tt((T[db][:, c, :],) + v3(db, c, c + 1)[1:], ind(X, cv(lists, c, c + 1, 16, l0)), cv(eb, c, c + 1), SUB)
                ts(v3(ab, a, b), v3(db, a, b), 0.0, MAX, 2.0, MUL)

    def shift(e, o, a, x, scale=None):
        if e == "S":
            act(o, a, F.Identity, bias=x, scale=scale)
        elif scale is None:
            ts(o, a, x, ADD)
        else:
            ts(o, a, scale, MUL, x, ADD)

    def flags(hf, final, t):
        nc, KK, NS = 8 // KH, 16 // KH, NQ // KH
        c0, l0, nl, s0, PP = nc * hf, 16 * nc * hf, 16 * nc, NS * hf, 4 // NS
        r8 = lambda k: v(k, c0, c0 + nc)
        tt(r8("k8"), v("sc2", l0 + 15, l0 + nl, 16), r8("dv"), MUL)
        ts(r8("n8"), r8("k8"), 2047, AND)
        cp(r8("nl"), r8("n8"))
        cg, tb = v("cg", l0, l0 + nl), BANK[2 * hf] if final else "pU"
        ts(cg, ind(v("cot"), r8("nl")), -1024.0, ADD)
        half = lambda b, p=(0, 128): v(b, 0, 256, 1, p) if b != "pQ" else (T.pQ[p[0]:p[1], 16:32, :], [("pQ", 256, 512, False)], 256)
        t2 = BANK[2 * hf + 1] if final else "pQ"
        for b, x in ((tb, 0), (t2, 256)):
            mms(half(b), [(mb("ON"), v("mb", MB["SH"] + x, MB["SH"] + x + 256))], True, False)
            for kh in range(KH):
                mms(half(b, (nl * kh, nl * kh + nl)), [(cg, cv("mh", kh, kh + 1, 256, 1024))], False, False)
            if not x:
                mms(half(b), [(mb("Z"), v("mb", MB["SH"], MB["SH"] + 256))], False, True)
        hc = CFG["hc"][2 * final:]
        for s in range(s0, s0 + NS):
            shift(hc[0], v3("hi4", s, s + 1), v(tb, 128 * (s - s0), 128 * (s - s0) + 128), HB + 32 - 31.0 / 64, 1.0 / 32)
        mms(half(t2), [(mb("I32"), v3("hi4", s0, s0 + NS))], False, True)
        shift(hc[1], v3("lo4", s0, s0 + NS), half(t2), 32.0 * (HB + 32))
        FB = BANK[2 * (hf != final):][:2] if KH > 1 else CFG["fb"]
        if not final:
            for b in FB:
                mms(v(b, 0, 128, 1, (0, 98)), [(mb("Z", 98), mb("I"))], True, False)
        else:
            mms(v("pU", 0, 96), [(mb("Z"), mb("I", 96))], True, False)
            for Q in range(2 if t else 0):
                mms(v("pU", 48 * Q, 48 * Q + 48), [(v("mb", MB["U"] + 256 * b + 128 * Q, MB["U"] + 256 * b + 128 * Q + 128), v("old", b, 96, 2)) for b in range(2)], False, False)
        for s in range(s0, s0 + NS):
            for h in range(HR):
                o, x = v("ohh", HW * s + 128 * h, HW * s + 128 * h + 128), HB + 32.0 + NQ * h
                if h < HV:
                    ts(o, v3("hi4", s, s + 1), x, A.is_equal)
                else:
                    act(o, v3("hi4", s, s + 1), F.Sign, bias=0.5 - x)
            for h in range(LR):
                ts(v("ohl", 128 * (LR * s + h), 128 * (LR * s + h) + 128), v3("lo4", s, s + 1), float(NQ * h), A.is_equal)
            for pp in range(PP):
                pr = (s - s0) * PP + pp
                o = v(FB[pr // KH], 64 * (pr % KH), 64 * (pr % KH) + 64, 1, (0, 98))
                mms(o, [(v("ohh", HW * s + KK * pp + k, HW * s + HW, WQ // 2), v("ohl", 128 * LR * s + KK * pp + k, 128 * LR * (s + 1), WQ // 2)) for k in range(KK)],
                    KH == 1, KH == 1)
                if final and (pr + 1) % KH == 0:
                    if KH > 1:
                        mms(v(FB[pr // KH], 0, 128, 1, (0, 98)), [(mb("Z", 98), mb("I"))], False, True)
                    cp(v("Fq", 64 * (pr + 1 - KH), 64 * pr + 64, 1, (0, 98)), v(FB[pr // KH], 0, 64 * KH, 1, (0, 98)))
                    for p2 in range(pr + 1 - KH, pr + 1):
                        for Q in range(2):
                            gi = 2 * PP * (p2 // PP) + p2 % PP + Q * PP
                            mms(v("pU", 48 * (gi // 4), 48 * (gi // 4) + 48, 1, (32 * (gi % 4), 32 * (gi % 4) + 32)),
                                [(v("Fq", 64 * p2 + Q, 64 * p2 + 64, 2, (0, 98)), v("Eh", 48 * Q, 48 * Q + 48, 1, (0, 98)))], False, False)
        if final:
            mms(v("pU", 0, 96), [(mb("Z"), mb("I", 96))], False, True)

    def lift(o, a, x):
        a = (a[0], a[1] + v("sc")[1], a[2])
        if CFG["lift"] == "S":
            act(o, a, F.Identity, bias=x)
        else:
            ts(o, a, x, ADD)

    def unpack(o, p, after=()):
        ts(v("abi", 0, 8), p, 12, SHR, after=after)
        ts(v("abi", 8, 16), p, 4095, AND, after=after)
        cp(o, v("abi"))

    for t in range(RO):
        dx = "dx%d" % (t % 2)
        last = t == RO - 1
        marks.append(len(ops))
        off = 128.0 if t else 0.0
        byu = t and CFG["xs"]
        X = XH if t else v("X0", PAD, PAD + 2560)
        ab, pt = v("ab16", 16 * t, 16 * t + 16), v("pt", 8 * t, 8 * t + 8)
        if t:
            unpack(ab, pt, [trip("ab%da" % t)])
        cp(v("dfk"), ind(cot, ab))
        ts(v("f2"), v("dfk"), -1024.0, ADD)
        turn(v3("t3", 0, 8), v("f2"))
        swap(lambda cpx: v3("pQ", cpx, 8, step=2), 4, (("t3", 0, 512), ("t3", 4, 0)), more=[(mb("ON"), v3("k3", 16, 20))])
        for n, part in enumerate(CFG["p1"]):
            lo, hi = 16 * part[0], 16 * part[1]
            r = lambda k: v(k, lo, hi)
            pd = "pD%d" % (n % 2)
            key = v(pd, 0, hi - lo)
            shifted("e1", "z", "dfk", dx, part, CFG["z1"])
            apart("xf", "da", "e1", "a3", "dfk", 128, part, CFG["f1"], X)
            mms(key, [(mb("I"), v3("k3", 0, part[1] - part[0]))], True, False)
            distance(pd, part, "K1", "a3", "da", CFG["f1"])
            scan(r("sc"), C("R1", lo, hi), key, MAX, MIN)
            tt(r("gp"), key, r("sc"), SUB)
            tt(r("qq"), v3("pQ", part[0], part[1]), r("gp"), SUB)
            scan(r("ds"), r("gp"), r("qq"), MIN, MAX)
            ts(v("d16", part[0], part[1]), v("ds", lo + 15, hi, 16), 1.0 / 4096, MUL, -0.3125, ADD)
            cp(r("sj"), ind(sut, v("d16", part[0], part[1])))
        for n, part in enumerate(CFG["p2"]):
            lo, hi = 16 * part[0], 16 * part[1]
            r = lambda k: v(k, lo, hi)
            pu = v3("pQ", 8, 8 + part[1] - part[0]) if n % 2 else v("pU", 0, hi - lo)
            shifted("e", "z2", "sj", dx, part, CFG["z2"])
            mms(pu, [(slide("W", j), v("e", 16 * lo + j, 16 * hi, 16)) for j in range(16)])
            if CFG["um"][n] == "S" and not byu:
                act(r("uy"), pu, F.Identity, bias=P(29) if t else UB - 2048)
                tt(r("w2"), pu, r("uy"), SUB)
                act(r("us"), r("w2"), F.Square, bias=P(30) if t else UB + 592)
                ts(r("nn"), r("us"), 1.0 / 32, MUL, 312 - 13.0 / 32, ADD)
                ts(r("ni"), r("nn"), 1023, AND)
            else:
                if t:
                    ts(r("ui"), pu, P(23), ADD)
                else:
                    cp(r("ui"), pu)
                ts(r("uv"), r("ui"), 4095, AND)
                ts(r("w2"), r("uv"), 1184.0, ADD)
                tt(r("nn"), r("w2"), r("uv"), MUL)
                ts(r("ni"), r("nn"), 5, SHR, 1023, AND)
            cp(r("n16"), r("uv" if byu else "ni"))
        ts(v("dv"), v("sc", 15, 128, 16), v("thv"), A.is_ge)
        for n, part in enumerate(CFG["p3"]):
            lo, hi = 16 * part[0], 16 * part[1]
            r = lambda k: v(k, lo, hi)
            pd, a0, nh = "pD%d" % (n % 2), part[0] // 2, (part[1] - part[0]) // 2
            key = v(pd, 0, hi - lo)
            if nh == 1 or CFG["nf1"]:
                ts(v3("nf", a0, a0 + nh), r("ni"), float(PAD), ADD)
            else:
                for cpx in range(2):
                    ts(v3("nf", a0, a0 + nh, 16 * cpx, 16 * cpx + 16), cv("ni", cpx, cpx + 1, 16 * nh, lo), float(PAD), ADD)
            turn(v3("t4", a0, a0 + nh), v3("nf", a0, a0 + nh))
            direct = not runs(part, CFG["f2"], "V")
            mms(key, [(mb("ON"), v3("k3", 8, 8 + 2 * nh))], True, False)
            if direct and CFG["nf1"]:
                for a in range(nh):
                    swap(lambda cpx: cv(pd, 2 * a + cpx, 2 * a + cpx + 1, 16), 1, (("t4", a0 + a, 0),), False, False)
            elif direct:
                swap(lambda cpx: cv(pd, cpx, cpx + 1, 16 * nh), nh, (("t4", a0, 0),), False, False)
            elif CFG["nf1"]:
                swap(lambda cpx: v3("pQ", 16 + cpx, 16 + 2 * nh, step=2), nh, (("t4", a0, 0),))
                act(r("pay"), v3("pQ", 16, 16 + 2 * nh))
            else:
                swap(lambda cpx: v3("pQ", 16 + nh * cpx, 16 + nh * cpx + nh), nh, (("t4", a0, 0),))
                act(r("pay"), v3("pQ", 16, 16 + 2 * nh))
            apart("xn", "db", "e", "b3", "n16", 0, part, CFG["f2"], v("XS") if byu else X)
            distance(pd, part, "K2", "b3", "db", CFG["f2"])
            if direct:
                scan(r("sc2"), C("R2", lo, hi), key, MIN, MAX)
            else:
                tt(r("key2"), key, r("pay"), ADD)
                scan(r("sc2"), C("R2", lo, hi), r("key2"), MIN, MAX)
            done = sum(b - a for a, b in CFG["p3"][:n + 1])
            if done % (8 // KH) == 0:
                flags(part[0] // (8 // KH), done == 8, t)
        dsl, po = v("ds", 15, 128, 16), v("po", 8 * t, 8 * t + 8)
        tt(v("u8"), pt, dsl, SUB)
        tt(v("u8"), v("u8"), v("dv"), MUL)
        tt(po, v("u8"), dsl, ADD)
        if not last:
            remote(T.cores[(rank + 1) % N], "pt", 8 * t + 8, 8 * t + 16, po, "ab%da" % (t + 1))
        else:
            unpack(v("abf"), po)
            store("sta", T.ya[:], v("abf", 0, 8))
            store("stb", T.yb[:], v("abf", 8, 16))
        for a, b in CFG["l1"]:
            tt(cv("qb", a, b, 16), ind(v("tabn"), v("nl", a, b)), C("lfr", 16 * a, 16 * b), ADD)
            tt(v("nb", a, b), C("c2", a, b), v("n8", a, b), SUB)
        for c in range(8):
            act(v("ab1", 128 * c, 128 * c + 16 * c + 16), v("qb", 0, 16 * c + 16), F.Abs, bias=v("nb", c, c + 1))
        for c in range(8):
            act(v("rl", 128 * c, 128 * c + 16 * c + 16), v("ab1", 128 * c, 128 * c + 16 * c + 16), F.Relu, bias=C("hl", c, c + 1), scale=-2.0 ** 21, acc=v("los", c, c + 1))
        if t in (0, RO - 1):
            for lo in range(PAD + (1024 if last else 0), PAD + 2560, 512):
                lift(v("X0" if last else "X", lo, lo + 512), v("X" if last else "X0", lo, lo + 512), -128.0 if last else 128.0)
        for a, b in CFG["l2"]:
            r = lambda k: v(k, a, b)
            ts(r("j8"), r("k8"), 11, SHR, 15, AND)
            tt(r("jf"), C("c15", a, b), r("j8"), SUB)
            cp(r("jl"), r("jf"))
            shift(CFG["es"], cv("esel", a, b, 16), ind(v("e"), r("jl")), 128.0 - off)
        for a, b in CFG["l3"]:
            r = lambda k: v(k, a, b)
            tt(r("lt"), r("los"), C("cT", a, b), MIN)
            tt(r("tg"), r("lt"), r("n8"), MAX)
            cp(r("tg16"), r("tg"))
            scatter(v("X", 0, PAD + 2560 + 128), r("tg16"), cv("esel", a, b, 16))
        if CFG["xs"] and not last:
            w = CFG["xs"]
            for lo in range(0, 256, w):
                act(cv("XS", lo, lo + w, 16), ind(v("X", PAD, PAD + 1024), v("spot", lo, lo + w)))
        if last:
            for lo in (PAD, PAD + 512):
                lift(v("X0", lo, lo + 512), v("X", lo, lo + 512), -128.0)
            store("stx0", T.yx[:, 0:1024], v("X0", PAD, PAD + 1024))
        if not last:
            spread(t + 1)
            cn = v("pD0", 0, 8)
            mms(cn, [(mb("ON"), v("dv"))])
            act(v("a8"), cn, F.Identity, bias=P(20), scale=U1, acc=v("az"))
            act(v("ay"), v("az"), F.Identity, bias=P(21), scale=1.0 / (64 * U1))
            act(v("thv"), v("ay"), F.Identity, bias=v("az"), scale=-64 * U1)
        if CFG["fq"] == "S":
            act(v("Fl"), v("pU", 0, 96), F.Sign)
        else:
            ts(v("Fl"), v("pU", 0, 96), 0.0, A.is_gt)
        mms(v("pA", 96, 108), [(mb("Z"), mb("I", 12))])
        for mi, pb in (("O", "pA"), ("T", "pB")) + ((("C", "pC"),) if not last else ()):
            if mi == "C":
                mms(v(pb, 0, 96), [(mb("Z"), mb("I", 96))], True, False)
            for b in range(2):
                mms(v(pb, b, 96, 2), [(mb(k + str(2 * Q + b)), v("Fl", 48 * Q, 48 * Q + 48)) for Q in range(2) for k in {"C": "CT"}.get(mi, mi)], mi != "C", mi != "C")
        Sx = v("Sx", 12, 108)
        scan(v("Sx", 12, 120), v("pA", 0, 108), mb("c240", 108), ADD, MIN)
        tt(v("P2", 0, 96), Sx, v("pB", 0, 96), ADD)
        for n, (c0, c1) in enumerate(CFG["pre"]):
            mine = [c for c in range(c0, c1) if c in SV]
            rest = [c for c in range(c0, c1) if c not in SV]
            assert all(x[-1] - x[0] < len(x) for x in (mine, rest) if x)
            if rest:
                for c in rest:
                    act(v("sg", 120 * c, 120 * c + 98 + 2 * c), v("Sx", 11 - c, 109 + c), F.Sign, bias=C("bj", c, c + 1), scale=-1.0, acc=v("xa", c, c + 1))
                a, b = rest[0], rest[-1] + 1
                ts(v("xl", a, b), v("xa", a, b), 0.5, MUL, 48.0, ADD)
                act(v("xb", a, b), v("xa", a, b), F.Identity, bias=48.0, scale=0.5)
            if mine:
                for c in mine:
                    ts(v("sq", 108 * c, 108 * c + 97 + c), v("Sx", 12, 109 + c), C("bj", c, c + 1), A.is_lt)
                a, b = mine[0], mine[-1] + 1
                scan(v("sv", 108 * a, 108 * b), v("rv", 0, 108 * (b - a)), v("sq", 108 * a, 108 * b), MUL, ADD)
                cp(v("xl", a, b), v("sv", 108 * a + 107, 108 * b, 108))
                act(v("xb", a, b), v("sv", 108 * a + 107, 108 * b, 108))
            pn = v(CFG["nb"][n % 3], c0, c1)
            tt(v("cm", 16 * c0, 16 * c1), ind(v("P2"), v("xl", c0, c1)), v("jr", 16 * c0, 16 * c1), A.is_le)
            mms(pn, [(mb("I16"), v("xb", c0, c1))], True, False)
            mms(pn, [(slide("B1", m), v("cm", 16 * c0 + m, 16 * c1, 16)) for m in range(16)], False, True)
            ts(v("no16", c0, c1), pn, 1024.0, ADD)
            cp(v("s4", 16 * c0, 16 * c1), ind(sut, v("no16", c0, c1)))
        if not last:
            mms(v("pC", 0, 96), [(mb("I"), Sx)], False, True)
            act(v("old"), v("pC", 0, 96), F.Relu, bias=-448.5)
        if last or CFG["xs"]:
            ts(v("vl16"), v("no16"), -1024.0, ADD)
        for c0, c1, e in CFG["rc"]:
            o, a = v("R", 256 * c0, 256 * c1), ind(XH, v("s4", 16 * c0, 16 * c1))
            if e == "S":
                act(o, a, scale=0.5)
            else:
                ts(o, a, 0.5, MUL)
        for n, (c0, c1, e) in enumerate(CFG["rc"]):
            lo, hi = 256 * c0, 256 * c1
            scan(v("mx", lo, hi), v("R", lo, hi), v("rr", 0, hi - lo), MAX, ADD)
            scan(v("mn", lo, hi), v("R", lo, hi), v("rr", 1536, 1536 + hi - lo), MIN, ADD, 128.0)
        for c0, c1 in CFG["sc"]:
            a, b = v("mx", 256 * c0 + 15, 256 * c1, 16), v("mn", 256 * c0 + 15, 256 * c1, 16)
            if not last:
                scatter(v("X", PAD + 1024, XW), v("vl16", c0, c1), a, b) if CFG["xs"] else scatter(v("X", PAD, XW), v("no16", c0, c1), a, b)
            else:
                tt(v("vb", 16 * c0, 16 * c1), a, b, ADD)
                scatter(v("X0", PAD + 1024, XW), v("vl16", c0, c1), v("vb", 16 * c0, 16 * c1), v("m128", 16 * c0, 16 * c1))
    store("stx1", T.yx[:, 1024:2560], v("X0", PAD + 1024, PAD + 2560))
    flush()

    for e in ("V", "S", "P", "G"):
        wait("G", {e: cnt[e]})
    for k in LOADS:
        wait("G", {k: 16})
    for k in STORES:
        g.sync.wait_ge(T.sem[k], 16)
    g.wait_ge(T.sem.loc, locs[0])
    wait("G", landed)
